import numpy as np, ml_dtypes
CORES = [35,38,43,46]
N = 4
import mx_ref
BF = ml_dtypes.bfloat16
def entries(a):
    return np.ascontiguousarray(a.T).reshape(-1)
def table(e):
    return np.ascontiguousarray(np.reshape(e, (-1, 16)).T).astype(np.int32)
def pick(q, e):
    c = np.concatenate([q[0].reshape(128, -1, 4), np.zeros((128, 1, 4), np.uint8)], axis=1); s = np.concatenate([q[1], np.ones((16, 1), np.uint8)], axis=1)
    return (np.ascontiguousarray(c[:, e].reshape(128, -1)), np.ascontiguousarray(s[:, e]))
def join(*qs):
    return (np.concatenate([q[0] for q in qs], axis=1), np.concatenate([q[1] for q in qs], axis=1))
def put(q, e, v):
    c, s = q[0].reshape(128, -1, 4).copy(), q[1].copy(); c[:, e] = v[0].reshape(128, -1, 4); s[:, e] = v[1]
    return (c.reshape(128, -1), s)
def pk(c, s):
    return (np.ascontiguousarray(c), mx_ref.live(s))
def emit(q):
    return q[0], q[1]
def packed(v, rng):
    q = [mx_ref.quantize(np.ascontiguousarray(v[r])) for r in range(N)]
    return np.stack([a for a, b in q]), np.stack([mx_ref.plane(b, rng) for a, b in q])
def f(rng, *shape):
    return mx_ref.flush((rng.standard_normal(shape, dtype=np.float32) * np.exp2(rng.integers(-2, 3, shape[:-1] + (1,)))).astype(BF))
def wide(rng, *shape, cols=0):
    v = rng.standard_normal(shape, dtype=np.float32) * np.exp2(rng.integers(-12, 13, shape)).astype(np.float32)
    if cols: v *= np.repeat(np.exp2(rng.integers(-cols, cols + 1, shape[:-2] + (1, shape[-1] // 4))) * (rng.random(shape[:-2] + (1, shape[-1] // 4)) > 0.0625), 4, axis=-1).astype(np.float32)
    return mx_ref.flush(v.astype(BF))
C, CB, CAPP, S = 512, 288, 176, 640
def counts(rng, total, cap, least):
    n = np.array(least)
    while n.sum() < total: n[rng.choice(np.flatnonzero(n < cap))] += 1
    return n
def runs(rng, least, cap):
    n = np.zeros((N, N), int)
    for s in range(N)[::-1]: n[s] = counts(rng, C, np.minimum(cap[s], CAPP + n[N - 1]), least[s])
    return n
def keeps(rng, n, fall=0, least=np.zeros((N, N), int)):
    k = np.zeros((N, N), int)
    for s in range(N)[::-1]:
        above = k.sum(axis=0)
        k[s] = np.clip(np.minimum(rng.integers(0, 2 * n[s] // 3 + 1), n[s] - fall), np.maximum(n[s] - above, least[s]), np.minimum(np.minimum(n[s], CAPP), S - above))
    return k
def lists(rng, n, k, ends=False, narrow=False):
    p = np.sort(rng.choice(65536 - 2 * N * S, N - 1, replace=False)) + 2 * S * np.arange(1, N)
    if ends: p[0] = int(k[:, 0].sum()) + 2 + int(rng.integers(0, 4))
    if narrow: p[-1] = 65535
    lo, hi = np.append(0, p), np.append(p, 65536)
    keys = [[] for s in range(N)]
    for d in range(N):
        e, i, j = int(ends), -1, -1
        u = lo[d] + e + rng.choice(int(hi[d] - lo[d]) - 2 * e, int(k[:, d].sum()), replace=False)
        at = np.append(np.cumsum(k[::-1, d])[::-1], 0)[1:]
        if ends:
            low, c = np.flatnonzero(n[:, d] - k[:, d] > 1), np.flatnonzero(k[:, d] > 1)
            c = c[c > low[0]]
            if d in (0, N - 1): c = c[c < N - 1]
            i = rng.choice(c); j = rng.choice(low[low < i])
            u[at[i]] = lo[d]; u[at[i] + 1] = hi[d] - 1
        for s in range(N):
            m = at[i] + np.arange(2) if s == j else np.zeros(0, int)
            old = np.concatenate([m, rng.permutation(np.setdiff1d(np.arange(at[s]), m))])[:n[s, d] - k[s, d]]
            keys[s].append(u[np.concatenate([old, at[s] + np.arange(k[s, d])])])
    return {"ky": np.stack([table(np.sort(np.concatenate(v))) for v in keys]), "sp": np.stack([table(np.append(p, np.full(17 - N, 65535)))] * N)}
def setup_inputs(rng):
    kc, ks = packed(f(rng, N, 128, 4 * C), rng)
    n = runs(rng, rng.integers(1, CAPP // 2 + 1, (N, N)), np.full((N, N), CB))
    return {"kc": kc, "ks": ks, "w": f(rng, N, 128, 512), **lists(rng, n, keeps(rng, n))}
def setup_inputs_single(rng):
    least, cap = rng.integers(1, CAPP // 2 + 1, (N, N)), np.full((N, N), CB)
    least[:, N - 1] = rng.integers(0, 2, N); least[rng.permutation(N - 1)[:2], N - 1] = 1; cap[:, N - 1] = least[:, N - 1]
    n = runs(rng, least, cap)
    return {**setup_inputs(rng), **lists(rng, n, keeps(rng, n), narrow=True)}
def setup_inputs_narrow(rng):
    least, cap = rng.integers(1, CAPP // 2 + 1, (N, N)), np.full((N, N), CB)
    least[:, N - 1] = 0; cap[:, N - 1] = 0
    n = runs(rng, least, cap)
    return {**setup_inputs(rng), **lists(rng, n, keeps(rng, n), narrow=True)}
def setup_inputs_full(rng):
    h = int(rng.integers(0, N)); least = np.ones((N, N), int)
    a = np.append(h, rng.permutation(np.delete(np.arange(N), h)))[:(C - N) // CAPP]
    least[N - 1, a] = CAPP
    for s in range(N - 1): least[s, np.append(h, rng.permutation(a[1:]))[:(C - N) // CB]] = CB
    n = runs(rng, least, np.full((N, N), CB)); k = keeps(rng, n)
    v = np.zeros(N, int); v[N - 2:] = CAPP; v[rng.permutation(N - 2)[:S // CAPP - 2]] = CAPP
    k[:, h] = counts(rng, S, CAPP, v)
    return {**setup_inputs(rng), **lists(rng, n, k)}
def setup_inputs_edges(rng):
    q = int(rng.integers(1, N)); h = int(rng.choice(np.delete(np.arange(N - 1), min(q, N - 2))))
    least, cap = rng.integers(2, CAPP // 2 + 1, (N, N)), np.full((N, N), CB)
    least[h, q] = 0; cap[h, q] = 0
    few = rng.integers(2, 5, N)
    few[rng.permutation(np.setdiff1d(np.arange(N), [int(rng.integers(0, N - 2)), N - 2]))[:int(rng.integers(2, N - 1))]] = 0
    least[:, 0] = few; cap[:, 0] = few
    n = runs(rng, least, cap)
    two = np.zeros((N, N), int); two[N - 2, [0, N - 1]] = 2
    return {**setup_inputs(rng), **lists(rng, n, keeps(rng, n, 2, two), ends=True)}
def setup_inputs_spread(rng):
    d = setup_inputs(rng); d["kc"], d["ks"] = packed(wide(rng, N, 128, 4 * C, cols=8), rng); return d
def check_inputs(d):
    b = []
    p = entries(d["sp"][0]).astype(np.int64); g = p[:N - 1]
    if (d["sp"] != d["sp"][:1]).any() or (p[N - 1:] != 65535).any() or g.min() < 1 or g.max() > 65535 or (np.diff(g) <= 0).any(): b.append("sp")
    lo, hi = np.append(0, g), np.append(g, 65536)
    k = [entries(d["ky"][s]).astype(np.int64) for s in range(N)]
    bad = any(v.min() < 0 or v.max() > 65535 or (np.diff(v) <= 0).any() for v in k)
    x, s = np.concatenate(k), np.repeat(np.arange(N), C)
    o = np.argsort(x, kind="stable"); o = o[np.append(x[o][1:] != x[o][:-1], True)]
    x, s = x[o], s[o]
    for q in range(N):
        m = (x >= lo[q]) & (x < hi[q])
        if max(((v >= lo[q]) & (v < hi[q])).sum() for v in k) > CB or m.sum() > S or np.bincount(s[m], minlength=N).max() > CAPP: bad = True
    if bad: b.append("ky")
    return b
def reference(kc, ks, w, ky, sp):
    every = join(*[pk(kc[s], ks[s]) for s in range(N)])
    keys = np.concatenate([entries(ky[s]) for s in range(N)])
    oc, osc = np.zeros((N, 128, 4 * S), np.uint8), np.zeros((N, 16, S), np.uint8)
    ok, y = np.zeros((N, 2, S), np.float32), np.zeros((N, 128, S), np.float32)
    for d in range(N):
        p = entries(sp[d])[:N - 1]
        lo, hi = np.append(0, p)[d], np.append(p, 65536)[d]
        e = np.flatnonzero((keys >= lo) & (keys < hi))
        e = e[np.argsort(keys[e], kind="stable")]
        e = e[np.append(keys[e][1:] != keys[e][:-1], True)[:e.size]]
        a = np.full(S, -1); a[:e.size] = e
        kept = pick(every, a)
        oc[d], osc[d] = emit(kept)
        ok[d, 0] = np.where(a >= 0, keys[a], -1); ok[d, 1] = np.where(a >= 0, a // C, -1)
        y[d] = mx_ref.matmul(mx_ref.quantize(np.ascontiguousarray(w[d])), kept)
    return {"oc": oc, "osc": osc, "ok": ok, "y": y}

@@ -1,0 +1,315 @@
+from concourse.bass import DstId, RemoteDMATransfer
+from concourse.mybir import dt, AluOpType as OP, ActivationFunctionType as AF
+
+N, C, S, CAPP = 4, 512, 640, 176
+SL = 192
+NB = SL // 32
+NS = N * SL
+Z0 = 32
+BIG = 70000.0
+CH = 320
+YV = 384
+A3 = 11
+M3 = 24 - A3
+R0 = -float(M3 * SL // 2)
+
+
+def _s(n, d="float32"):
+    return ("sbuf", [128, n], d)
+
+
+X4, U8, U16, BF, I32 = "float8_e4m3fn_x4", "uint8", "uint16", "bfloat16", "int32"
+SCRATCH = {
+    "kl": _s(4, I32), "lki": _s(32, I32), "spi": _s(1, I32), "wt": _s(512, BF), "kcs": _s(C, X4), "kss": _s(C, U8),
+    "pidx": _s(1, I32), "pm": _s(6, I32), "pf": _s(6), "six": _s(1), "v32": _s(1), "vhf": _s(1), "vsum": _s(1), "ones": _s(32),
+    "i_exp": _s(32, I32), "expk": _s(32, U16), "i_sel": _s(16), "sel": _s(16, U16), "i_e3": _s(12), "exp3": _s(12, U16),
+    "i_dup": _s(4), "dup": _s(4, U16), "i_il": _s(3), "il": _s(3, U16), "i_d3": _s(24), "d3": _s(24),
+    "i_vj": _s(256), "cj": _s(256), "i_v3": _s(384), "v3": _s(384), "zt": _s(512, BF), "zc": _s(128, X4), "zs": _s(128, U8),
+    "lkf": _s(32), "at": _s(32), "spf": _s(1), "spx": _s(32), "spb": _s(32), "r1": _s(16), "r2": _s(16), "r3": _s(16), "r12": _s(16), "r123": _s(16), "rr": _s(16),
+    "xa": _s(512), "fa": _s(512), "fs": _s(256), "vk": _s(256),
+    "kb": _s(12, I32), "x1": _s(384), "b1": _s(384), "b1u": _s(256, U16), "cmp": _s(16 * 256, BF), "sc": _s(16 * 128 + 1, BF), "js": _s(16 * 128, BF),
+    "rc": _s(33), "qu": _s(33), "qo": _s(33, I32), "par": _s(16, I32), "fv": _s(16), "fl": _s(16),
+    "q0": _s(16), "tot": _s(1), "ct": _s(64), "ctt": _s(64), "st": _s(64), "bt": _s(32), "qq": _s(16), "e1": _s(16), "e2": _s(16), "o2": _s(16), "off": _s(16, U16),
+    "wk": _s(NS + 256), "tk": _s(NS), "zi": _s(24, I32), "ki": _s(24, I32), "ji": _s(24, I32), "bz": _s(24), "ho": _s(24), "kz": _s(24), "zj": _s(32),
+    "sw1": _s(32), "sw2": _s(64), "sw3": _s(64), "lj": _s(48, U16),
+    "pc0": _s(CAPP, X4), "pc1": _s(CAPP, X4), "pc2": _s(CAPP, X4), "pc3": _s(CAPP, X4),
+    "ps0": _s(CAPP, U8), "ps1": _s(CAPP, U8), "ps2": _s(CAPP, U8), "ps3": _s(CAPP, U8),
+    "ap": _s(24), "x3": _s(SL), "b3": _s(SL), "b3u": _s(SL, U16), "cmp3": _s(M3 * SL, "float16"), "sc3": _s(M3 * SL // 2 + 1, "float16"), "j3": _s(A3 * SL, BF), "rs3": _s(24),
+    "rc3": _s(24), "qu3": _s(24), "qo3": _s(24), "vs": _s(24), "vd": _s(24), "p2": _s(24), "off3": _s(24, U16),
+    "wo": _s(NS + 384), "to": _s(S), "zo": _s(32), "so1": _s(32), "so2": _s(64), "so3": _s(64), "lf": _s(48, U16),
+    "fw": _s(Z0 + NS, X4), "fsc": _s(Z0 + NS, U8), "oq": _s(S, X4), "os_": _s(S, U8), "wq": _s(128, X4), "wsc": _s(128, U8),
+    "kf": _s(Z0 + NS), "okf": _s(S), "yw": _s(Z0 + NS), "ys": _s(S), "pz": ("psum", [128, 512 * N], "float32"),
+}
+SEMAPHORES = ["v", "s", "t", "gi", "dkl", "dlk", "dsp", "dw", "dk", "dz", "kin", "slk", "colc", "cols", "lsent", "own", "st1", "st2"]
+
+
+def rank_program(g, core, T, topo):
+    r = T.rank_of(core)
+    if r is None:
+        return
+    Q = {"v": g.vector, "s": g.scalar, "t": g.tensor, "g": g, "y": g.sync}
+    seen, total = {}, {}
+
+    def need(q, toks):
+        for tok in toks:
+            if tok is not None and seen.get((q, tok[0]), 0) < tok[1]:
+                Q[q].wait_ge(T.sem[tok[0]], tok[1])
+                seen[(q, tok[0])] = tok[1]
+
+    def done(inst, sem, n=1):
+        inst.then_inc(T.sem[sem], n)
+        total[sem] = total.get(sem, 0) + n
+        return (sem, total[sem])
+
+    vec, act = g.vector, g.scalar
+
+    def vop(deps, name, *a):
+        need("v", deps)
+        f = {"copy": vec.tensor_copy, "tt": vec.tensor_tensor, "ts": vec.tensor_scalar, "tr": vec.transpose, "scan": vec.tensor_tensor_scan,
+             "set": vec.memset, "q": vec.quantize_mx}[name]
+        return done(f(*a), "v")
+
+    def sop(deps, *a, **k):
+        need("s", deps)
+        return done(act.activation(*a, **k), "s")
+
+    def dma(q, deps, out, in_, sem):
+        need(q, deps)
+        return done(Q[q].dma_start(out, in_), sem, 16)
+
+    others = [d for d in range(N) if d != r]
+    far = [d for d in others if topo.chip(T.cores[d]) != topo.chip(core)]
+    near = [d for d in others if d not in far]
+    fe = topo.engines(core, T.cores[far[0]])
+    KE = len(fe) // len(far)
+    eng = {d: fe[i * KE:(i + 1) * KE] for i, d in enumerate(far)}
+    for d in near:
+        eng[d] = [e for e in topo.engines(core, T.cores[d]) if e not in fe]
+
+    def send(dests, sem, src, dst, few):
+        tr = []
+        for d in dests:
+            rid, pid, _ = topo.addr(T.cores[d])
+            m = sum(1 << e for e in (eng[d][:KE] if few else eng[d]))
+            tr.append(RemoteDMATransfer(dst_ids=[DstId(rid=rid, pnc=pid)], dma_engine_mask=m, remote_sem=T.sem[sem], src=src(d), dst=dst(d)))
+            total["lsent"] = total.get("lsent", 0) + (KE if few else len(eng[d]))
+        g.remote_dma_fused(tr, local_sem=T.sem.lsent)
+
+    t_kl = dma("y", [], T.kl[:], T.ky[:], "dkl")
+    for a in range(8):
+        t_lk = dma("ys"[a % 2], [], T.lki[16 * a:16 * a + 16, :], T.ky[:], "dlk")
+    for a in range(8):
+        t_sp = dma("ys"[a % 2], [], T.spi[16 * a:16 * a + 16, :], T.sp[:], "dsp")
+    dma("y", [], T.kcs[:].bitcast(dt.uint8), T.kc[:], "dk")
+    t_k = dma("y", [], T.kss[:], T.ks[:], "dk")
+    t_w = dma("y", [], T.wt[:], T.w[:], "dw")
+
+    def iota(out, pat, base, cm=0, i32=False):
+        if i32:
+            return done(g.iota(out, pat, base, cm), "gi")
+        return done(g.iota(out, pat, base, cm, allow_small_or_imprecise_dtypes=True), "gi")
+    t_pi = iota(T.pidx[:], [[0, 1]], 0, 1, True)
+    t_ie = iota(T.i_exp[:], [[1, 16], [0, 2]], 0, 0, True)
+    iota(T.i_sel[:], [[32, 16]], 0)
+    iota(T.i_e3[:], [[1, NB], [0, 2]], 0)
+    iota(T.i_dup[:], [[16, 2], [0, 2]], 0)
+    iota(T.i_il[:], [[8, 3]], 0)
+    t_ic = iota(T.i_d3[:], [[16, 24]], NS)
+    low = [d for d in others if d < r]
+    if low:
+        need("g", [t_kl])
+        send(low, "kin", lambda d: T.kl[:], lambda d: T.kb[:, 4 * (r - d - 1):4 * (r - d)], True)
+    t_ivj = iota(T.i_vj[:], [[1, 16], [16, 16]], 0)
+    t_wk = iota(T.wk[:, 0:NS], [[0, NS]], -1)
+    t_iv3 = iota(T.i_v3[:], [[32, 24], [1, 16]], Z0)
+    iota(T.kf[:, 0:Z0], [[0, Z0]], -1)
+    t_kf = iota(T.kf[:, Z0:Z0 + NS], [[1, N], [0, SL]], 0)
+    t_yw = iota(T.yw[:], [[0, Z0 + NS]], 0)
+    t_wo = iota(T.wo[:, 0:S], [[0, S]], 0)
+
+    vop([], "set", T.ones[:], 1.0)
+    vop([], "set", T.zj[:], 0.0)
+    vop([], "set", T.zo[:], 0.0)
+    vop([], "set", T.st[:], -1.0)
+    vop([], "set", T.sc[:, 0:1], 0.0)
+    t_zt = vop([], "set", T.zt[:], 0.0)
+    need("v", [t_pi])
+    for i, b in enumerate((15, 31, 16, 1, 14)):
+        vop([], "ts", T.pm[:, i:i + 1], T.pidx[:], b, None, OP.bitwise_and)
+    t = vop([], "ts", T.pm[:, 5:6], T.pidx[:], 5, None, OP.arith_shift_right)
+    t_pf = vop([t], "copy", T.pf[:], T.pm[:])
+    t_ek = vop([t_ie], "copy", T.expk[:], T.i_exp[:])
+    need("v", [t_pf, t_ic])
+    vop([], "ts", T.six[:], T.pf[:, 5:6], float(NB), None, OP.mult)
+    vop([], "ts", T.v32[:], T.pf[:, 3:4], 32.0, None, OP.mult)
+    t = vop([], "ts", T.vhf[:], T.pf[:, 4:5], 0.5, None, OP.mult)
+    t_sel = vop([], "ts", T.sel[:], T.i_sel[:], T.pf[:, 1:2], None, OP.add)
+    vop([], "ts", T.dup[:], T.i_dup[:], T.pf[:, 0:1], None, OP.add)
+    vop([], "ts", T.d3[:], T.i_d3[:], T.pf[:, 0:1], None, OP.add)
+    vop([], "ts", T.sc3[:, 0:1], T.pf[:, 0:1], 0.0, R0, OP.mult, OP.add)
+    t = vop([t], "ts", T.vsum[:], T.v32[:], T.vhf[:], None, OP.add)
+    vop([], "ts", T.exp3[:], T.i_e3[:], T.six[:], None, OP.add)
+    t_c = vop([t], "ts", T.il[:], T.i_il[:], T.vsum[:], None, OP.add)
+    t_lkf = vop([t_lk], "copy", T.lkf[:], T.lki[:])
+    t_at = vop([t_lkf], "tr", T.at[:], T.lkf[:])
+    t_xa = sop([t_at, t_ek], T.xa[:], T.at[:, 0:16].indirect(T.expk[:]), AF.Copy)
+    t_spf = vop([t_sp], "copy", T.spf[:], T.spi[:])
+    t_spx = vop([t_spf], "ts", T.spx[:], T.ones[:], T.spf[:], None, OP.mult)
+    t_spb = vop([t_spx], "tr", T.spb[:], T.spx[:])
+    vop([t_spb], "ts", T.r1[:], T.at[:, 0:16], T.spb[:, 0:1], float(SL), OP.is_ge, OP.mult)
+    t_r = vop([], "ts", T.r2[:], T.at[:, 0:16], T.spb[:, 1:2], float(SL), OP.is_ge, OP.mult)
+    t_r3 = vop([], "ts", T.r3[:], T.at[:, 0:16], T.spb[:, 2:3], float(SL), OP.is_ge, OP.mult)
+    t_r = vop([t_r], "tt", T.r12[:], T.r1[:], T.r2[:], OP.add)
+    t_r = vop([t_r, t_r3], "tt", T.r123[:], T.r12[:], T.r3[:], OP.add)
+    t_rr = vop([t_r], "ts", T.rr[:], T.r123[:], -1.0, None, OP.add)
+    t_fa = vop([t_xa], "tr", T.fa[:], T.xa[:])
+    t_fs = sop([t_fa, t_sel], T.fs[:], T.fa[:].indirect(T.sel[:]), AF.Copy)
+    t_cj = vop([t_ivj], "ts", T.cj[:], T.i_vj[:], 65536.0, 1.0, OP.mult, OP.add)
+    t_vk = vop([t_cj, t_fs], "tt", T.vk[:], T.fs[:], T.cj[:], OP.add)
+
+    nl = N - 1 - r
+
+    def quads(tok, src, qu, qo, n):
+        t = vop([tok], "tt", qu[0:64, 0:n], src[0:64, 0:n], src[64:128, 0:n], OP.add)
+        need("v", [t])
+        for b in range(4):
+            t = vop([], "tt", qo[32 * b:32 * b + 32, 0:n], qu[0:32, 0:n], qu[32:64, 0:n], OP.add)
+        return t
+
+    if nl == 0:
+        t_f = vop([], "set", T.fl[:], 1.0)
+    else:
+        W = 128 * nl
+        WV, H = W - 128, W // 2
+        total["kin"] = KE * nl
+        t_kin = ("kin", KE * nl)
+        t2 = sop([t_kin, t_ek], T.x1[:, H:W], T.kb[:, 0:4 * nl].indirect(T.expk[:, 4 * nl:8 * nl]), AF.Copy)
+        t = vop([t_kin], "copy", T.x1[:, 0:H], T.kb[:, 0:4 * nl].indirect(T.expk[:, 0:4 * nl]))
+        t_b = vop([t, t2], "tr", T.b1[:, 0:W], T.x1[:, 0:W])
+        for c in range(16):
+            t_s = sop([t_b, t_at], T.js[:, 128 * c:128 * c + 128], T.b1[:, WV:W], AF.Sign, bias=T.at[:, c:c + 1], scale=-1.0, accum_out=T.rc[:, c:c + 1])
+        if nl > 1:
+            H = WV // 2
+            t = vop([t_b], "copy", T.b1u[:, 0:WV], T.b1[:, 0:WV])
+            for c in range(16):
+                t = vop([t] if c == 0 else [], "ts", T.cmp[:, WV * c:WV * (c + 1)], T.b1u[:, 0:WV], T.at[:, c:c + 1], None, OP.is_equal)
+            t = vop([t], "scan", T.sc[:, 1:16 * H + 1], T.cmp[:, 0:16 * WV:2], T.cmp[:, 1:16 * WV:2], 0.0, OP.add, OP.add)
+            t = vop([t], "copy", T.rc[:, 16:33], T.sc[:, 0:16 * H + 1:H])
+        need("v", [t_s])
+        t = quads(t, T.rc, T.qu, T.qo, 33 if nl > 1 else 16)
+        t_p = vop([t], "ts", T.par[:], T.qo[:, 0:16], 1, None, OP.bitwise_and)
+        if nl > 1:
+            t = vop([], "tt", T.fv[:], T.qo[:, 17:33], T.qo[:, 16:32], OP.is_equal)
+            t_f = vop([t, t_p], "tt", T.fl[:], T.fv[:], T.par[:], OP.is_gt)
+        else:
+            t_f = vop([t_p], "ts", T.fl[:], T.par[:], 0.0, None, OP.is_equal)
+
+    t_tot = sop([t_f], T.js[:, 0:16], T.fl[:], AF.Copy, accum_out=T.tot[:])
+    t_q = vop([t_f, t_rr], "scan", T.q0[:], T.rr[:], T.fl[:], -1.0, OP.max, OP.add)
+    t_e = vop([t_c], "ts", T.e1[:], T.fl[:], 0.0, None, OP.is_equal)
+    vop([t_q], "ts", T.ct[:, 0:32], T.ones[:], T.q0[:, 15:16], None, OP.mult)
+    t = vop([t_tot], "ts", T.ct[:, 32:64], T.ones[:], T.tot[:], None, OP.mult)
+    t2 = vop([t_e], "tt", T.e2[:], T.d3[:, 0:16], T.e1[:], OP.mult)
+    t = vop([t], "tr", T.ctt[:], T.ct[:])
+    t = vop([t], "scan", T.st[:, 1:33], T.ctt[:, 32:64], T.ctt[:, 0:32], -1.0, OP.add, OP.max)
+    t = vop([t], "tr", T.bt[:], T.st[:, 0:32])
+    t = vop([t], "scan", T.qq[:], T.rr[:], T.fl[:], T.bt[:, 0:1], OP.max, OP.add)
+    t = vop([t, t2], "tt", T.o2[:], T.qq[:], T.e2[:], OP.max)
+    t_off = vop([t], "copy", T.off[:], T.o2[:])
+
+    t = vop([t_off, t_vk, t_wk], "copy", T.wk[:].indirect(T.off[:]), T.vk[:])
+    t = vop([t], "tr", T.tk[:], T.wk[:, 0:NS])
+    te, to = T.tk[:, 0:NS:32], T.tk[:, 16:NS:32]
+    t_zi = vop([t], "tt", T.zi[:], te, to, OP.add)
+    vop([t_zi], "ts", T.ki[:], T.zi[:], 65535, None, OP.bitwise_and)
+    t = vop([], "ts", T.bz[:], T.zi[:], 0.0, BIG, OP.is_lt, OP.mult)
+    t_kz = vop([t], "tt", T.kz[:], T.ki[:], T.bz[:], OP.add)
+    need("g", [t_kz])
+    send(others, "slk", lambda d: T.kz[:, NB * d:NB * (d + 1)], lambda d: T.ap[:, NB * r:NB * (r + 1)], True)
+    t_own = dma("y", [t_kz], T.ap[:, NB * r:NB * (r + 1)], T.kz[:, NB * r:NB * (r + 1)], "own")
+
+    def lists(tok, z, s1, s2, s3, out):
+        t = vop([tok], "tr", s1[:], z[:])
+        t = vop([t], "copy", s2[:], s1[:].indirect(T.dup[:]))
+        t = vop([t], "tr", s3[:], s2[:])
+        return vop([t], "copy", out[:], s3[:].indirect(T.il[:]))
+
+    vop([], "ts", T.ji[:], T.zi[:], 16, None, OP.arith_shift_right)
+    t = vop([], "ts", T.ho[:], to, 0.0, 256.0, OP.is_ge, OP.mult)
+    t = vop([t], "tt", T.zj[:, 0:24], T.ji[:], T.ho[:], OP.add)
+    t_lj = lists(t, T.zj, T.sw1, T.sw2, T.sw3, T.lj)
+
+    def pick(d, oc, osc):
+        L = T.lj[:, 12 * d:12 * d + CAPP // 16]
+        return (vop([t_lj, t_k], "copy", oc.bitcast(dt.uint32), T.kcs[:].bitcast(dt.uint32).indirect(L)),
+                sop([t_lj, t_k], osc, T.kss[:].indirect(L), AF.Copy))
+    for d in far + near:
+        t_pv, t_ps = pick(d, T["pc%d" % d][:], T["ps%d" % d][:])
+    w0 = Z0 + SL * r
+    need("g", [t_pv])
+    send(far + near, "colc", lambda d: T["pc%d" % d][:].bitcast(dt.uint8), lambda d: T.fw[:, w0:w0 + CAPP].bitcast(dt.uint8), False)
+    need("g", [t_ps])
+    send(far + near, "cols", lambda d: T["ps%d" % d][:], lambda d: T.fsc[:, w0:w0 + CAPP], False)
+
+    tk = {}
+
+    def own():
+        tk["v"], tk["s"] = pick(r, T.fw[:, w0:w0 + CAPP], T.fsc[:, w0:w0 + CAPP])
+        t = vop([t_zt], "q", T.zc[:], T.zs[:], T.zt[:])
+        dma("y", [t], T.fw[:, 0:Z0].bitcast(dt.uint8), T.zc[:, 0:Z0].bitcast(dt.uint8), "dz")
+        tk["z"] = dma("y", [t], T.fsc[:, 0:Z0], T.zs[:, 0:Z0], "dz")
+        tk["w"] = vop([t_w], "q", T.wq[:], T.wsc[:], T.wt[:])
+    if r:
+        own()
+
+    total["slk"] = KE * (N - 1)
+    total["colc"] = total["cols"] = sum(len(eng[d]) for d in others)
+    t_in = [("slk", total["slk"]), t_own]
+    H = SL // 2
+    t2 = sop(t_in + [t_c], T.x3[:, H:SL], T.ap[:].indirect(T.exp3[:, NB:2 * NB]), AF.Copy)
+    t = vop(t_in, "copy", T.x3[:, 0:H], T.ap[:].indirect(T.exp3[:, 0:NB]))
+    t_b3 = vop([t, t2], "tr", T.b3[:], T.x3[:])
+    for x in range(A3):
+        t_s = sop(t_in + [t_b3], T.j3[:, SL * x:SL * (x + 1)], T.b3[:], AF.Sign, bias=T.ap[:, x:x + 1], scale=-1.0, accum_out=T.rs3[:, x:x + 1])
+    t = vop([t_b3], "copy", T.b3u[:], T.b3[:])
+    need("v", [t])
+    for x in range(M3):
+        t = vop([], "ts", T.cmp3[:, SL * x:SL * (x + 1)], T.b3u[:], T.ap[:, A3 + x:A3 + x + 1], None, OP.is_lt)
+    t_vs = vop([], "ts", T.vs[:], T.ap[:], 65536.0, None, OP.is_ge)
+    t = vop([t], "scan", T.sc3[:, 1:M3 * H + 1], T.cmp3[:, 0:M3 * SL:2], T.cmp3[:, 1:M3 * SL:2], R0, OP.add, OP.add)
+    t_vd = vop([t_vs], "tt", T.vd[:], T.d3[:], T.vs[:], OP.mult)
+    t = vop([t], "tt", T.rc3[:, A3:24], T.sc3[:, H:M3 * H + 1:H], T.sc3[:, 0:(M3 - 1) * H + 1:H], OP.subtract)
+    if r == 0:
+        own()
+    t = vop([t, t_s], "ts", T.rc3[:, 0:A3], T.rs3[:, 0:A3], 0.5, SL / 2 - 0.125, OP.mult, OP.add)
+    t_v3 = sop([t_iv3, t_pf], T.v3[:], T.i_v3[:], AF.Identity, bias=T.pf[:, 2:3])
+    for s in range(N):
+        t_kc = sop([t_kf], T.kf[0:32, Z0 + SL * s:Z0 + SL * (s + 1)], T.b3[32 * s:32 * s + 32, :], AF.Copy)
+    for s in [r] + others:
+        a = Z0 + SL * s
+        need("t", [tk["w"]] + ([tk["v"], tk["s"]] if s == r else [("colc", total["colc"]), ("cols", total["cols"])]))
+        t_t = done(g.tensor.matmul_mx(T.pz[:, 512 * s:512 * s + CAPP], T.wq[:], T.wsc[:], T.fw[:, a:a + CAPP], T.fsc[:, a:a + CAPP], True, True), "t")
+        t_y = sop([t_t, t_yw], T.yw[:, a:a + CAPP], T.pz[:, 512 * s:512 * s + CAPP], AF.Copy)
+    t = quads(t, T.rc3, T.qu3, T.qo3, 24)
+    t = vop([t, t_vd], "tt", T.p2[:], T.qo3[:], T.vd[:], OP.max)
+    t = vop([t], "copy", T.off3[:], T.p2[:])
+    t = vop([t, t_v3, t_wo], "copy", T.wo[:].indirect(T.off3[:]), T.v3[:])
+    t = vop([t], "tr", T.to[:], T.wo[:, 0:S])
+    t = vop([t], "tt", T.zo[:, 0:20], T.to[:, 0:S:32], T.to[:, 16:S:32], OP.add)
+    t_lf = lists(t, T.zo, T.so1, T.so2, T.so3, T.lf)
+
+    t_sc = sop([t_lf, ("cols", total["cols"]), tk["s"], tk["z"]], T.os_[:], T.fsc[:].indirect(T.lf[:, 0:S // 16]), AF.Copy)
+    for c in range(S // CH):
+        lo, hi = c * CH, (c + 1) * CH
+        t = vop([t_lf, ("colc", total["colc"]), tk["v"], tk["z"]], "copy", T.oq[:, lo:hi].bitcast(dt.uint32), T.fw[:].bitcast(dt.uint32).indirect(T.lf[:, lo // 16:hi // 16]))
+        dma("y", [t], T.oc[:, 4 * lo:4 * hi], T.oq[:, lo:hi].bitcast(dt.uint8), "st1")
+    for i in range(4):
+        dma("y", [t_sc], T.osc[4 * i:4 * i + 4, :], T.os_[32 * i:32 * i + 4, :], "st1")
+    t = vop([t_y], "copy", T.ys[:, 0:YV], T.yw[:].indirect(T.lf[:, 0:YV // 16]))
+    dma("y", [t], T.y[:, 0:YV], T.ys[:, 0:YV], "st1")
+    t = sop([t_y, t_lf], T.ys[:, YV:S], T.yw[:].indirect(T.lf[:, YV // 16:S // 16]), AF.Copy)
+    t2 = sop([t_kc], T.okf[:], T.kf[:].indirect(T.lf[:, 0:S // 16]), AF.Copy)
+    dma("y", [t], T.y[:, YV:S], T.ys[:, YV:S], "st1")
+    dma("s", [t2], T.ok[0:1, :], T.okf[0:1, :], "st2")
+    dma("s", [], T.ok[1:2, :], T.okf[32:33, :], "st2")
+    need("g", list(total.items()))

@@ -2,45 +2,50 @@ from concourse.bass import DstId, RemoteDMATransfer
 from concourse.mybir import dt, AluOpType as OP, ActivationFunctionType as AF
 
 N, C, S, CAPP = 4, 512, 640, 176
+KEYS = 65536
 SL = 192
 NB = SL // 32
 NS = N * SL
-Z0 = 32
-BIG = 70000.0
-CH = 320
-YV = 384
-A3 = 11
-M3 = 24 - A3
-R0 = -float(M3 * SL // 2)
+LW = 256
+EMPTY = 2 * KEYS
+GAP = 576
+OFF = 2.0 ** 19
+GV = 256
+A3 = 7
+M3 = 3 * NB - A3
+R0 = -float(M3 * CAPP)
+CHC = (192, 448)
+CHY = (192, 448)
 
 
 def _s(n, d="float32"):
     return ("sbuf", [128, n], d)
 
 
-X4, U8, U16, BF, I32 = "float8_e4m3fn_x4", "uint8", "uint16", "bfloat16", "int32"
+X4, U8, U16, BF, I32, F16 = "float8_e4m3fn_x4", "uint8", "uint16", "bfloat16", "int32", "float16"
 SCRATCH = {
-    "kl": _s(4, I32), "lki": _s(32, I32), "spi": _s(1, I32), "wt": _s(512, BF), "kcs": _s(C, X4), "kss": _s(C, U8),
-    "pidx": _s(1, I32), "pm": _s(6, I32), "pf": _s(6), "six": _s(1), "v32": _s(1), "vhf": _s(1), "vsum": _s(1), "ones": _s(32),
-    "i_exp": _s(32, I32), "expk": _s(32, U16), "i_sel": _s(16), "sel": _s(16, U16), "i_e3": _s(12), "exp3": _s(12, U16),
-    "i_dup": _s(4), "dup": _s(4, U16), "i_il": _s(3), "il": _s(3, U16), "i_d3": _s(24), "d3": _s(24),
-    "i_vj": _s(256), "cj": _s(256), "i_v3": _s(384), "v3": _s(384), "zt": _s(512, BF), "zc": _s(128, X4), "zs": _s(128, U8),
-    "lkf": _s(32), "at": _s(32), "spf": _s(1), "spx": _s(32), "spb": _s(32), "r1": _s(16), "r2": _s(16), "r3": _s(16), "r12": _s(16), "r123": _s(16), "rr": _s(16),
-    "xa": _s(512), "fa": _s(512), "fs": _s(256), "vk": _s(256),
-    "kb": _s(12, I32), "x1": _s(384), "b1": _s(384), "b1u": _s(256, U16), "cmp": _s(16 * 256, BF), "sc": _s(16 * 128 + 1, BF), "js": _s(16 * 128, BF),
-    "rc": _s(33), "qu": _s(33), "qo": _s(33, I32), "par": _s(16, I32), "fv": _s(16), "fl": _s(16),
-    "q0": _s(16), "tot": _s(1), "ct": _s(64), "ctt": _s(64), "st": _s(64), "bt": _s(32), "qq": _s(16), "e1": _s(16), "e2": _s(16), "o2": _s(16), "off": _s(16, U16),
-    "wk": _s(NS + 256), "tk": _s(NS), "zi": _s(24, I32), "ki": _s(24, I32), "ji": _s(24, I32), "bz": _s(24), "ho": _s(24), "kz": _s(24), "zj": _s(32),
+    "kl": _s(4, I32), "klu": _s(4, U16), "lki": _s(40, I32), "wt": _s(512, BF), "kcs": _s(C, X4), "kss": _s(C, U8),
+    "pidx": _s(1, I32), "pm": _s(5, I32), "pf": _s(5), "m0": _s(1), "sa": _s(1), "sb": _s(1),
+    "i_dup": _s(4), "dup": _s(4, U16), "i_sel": _s(NB), "sel": _s(NB, U16), "i_exp": _s(2 * NB), "xe": _s(8, U16), "exp3": _s(2 * NB, U16),
+    "i_16": _s(16), "rot1": _s(2, I32), "rot2": _s(2, I32), "rot": _s(2, U16), "dmp": _s(16),
+    "i_cj": _s(64), "cj": _s(64), "i_v3": _s(96), "v3c": _s(96), "i_oc": _s(NB), "oc6": _s(NB),
+    "ones": _s(C, BF), "zt": _s(C, BF),
+    "xd": _s(64), "yd": _s(64), "ol": _s(32, U16), "spf": _s(1), "lkf": _s(32), "at": _s(32), "r4": _s(64), "rr": _s(32),
+    "xa": _s(128), "fa": _s(128), "vk": _s(64),
+    "kb": _s(12, U16), "tab": _s(KEYS, BF), "hit": _s(C, BF), "hitt": _s(C, BF), "h2": _s(16), "h4": _s(16), "fl": _s(16),
+    "zq": _s(64), "zqt": _s(64), "st": _s(64), "bt": _s(32), "qq": _s(16), "e1": _s(16), "e2": _s(16), "o2": _s(16), "off": _s(4, U16),
+    "wk": _s(NS + 264), "tk": _s(NS), "z2": _s(48), "z4": _s(48), "zz": _s(56),
     "sw1": _s(32), "sw2": _s(64), "sw3": _s(64), "lj": _s(48, U16),
     "pc0": _s(CAPP, X4), "pc1": _s(CAPP, X4), "pc2": _s(CAPP, X4), "pc3": _s(CAPP, X4),
     "ps0": _s(CAPP, U8), "ps1": _s(CAPP, U8), "ps2": _s(CAPP, U8), "ps3": _s(CAPP, U8),
-    "ap": _s(24), "x3": _s(SL), "b3": _s(SL), "b3u": _s(SL, U16), "cmp3": _s(M3 * SL, "float16"), "sc3": _s(M3 * SL // 2 + 1, "float16"), "j3": _s(A3 * SL, BF), "rs3": _s(24),
-    "rc3": _s(24), "qu3": _s(24), "qo3": _s(24), "vs": _s(24), "vd": _s(24), "p2": _s(24), "off3": _s(24, U16),
-    "wo": _s(NS + 384), "to": _s(S), "zo": _s(32), "so1": _s(32), "so2": _s(64), "so3": _s(64), "lf": _s(48, U16),
-    "fw": _s(Z0 + NS, X4), "fsc": _s(Z0 + NS, U8), "oq": _s(S, X4), "os_": _s(S, U8), "wq": _s(128, X4), "wsc": _s(128, U8),
-    "kf": _s(Z0 + NS), "okf": _s(S), "yw": _s(Z0 + NS), "ys": _s(S), "pz": ("psum", [128, 512 * N], "float32"),
+    "ap": _s(32), "apx": _s(32), "x3": _s(SL), "b3": _s(SL), "b3u": _s(CAPP, U16), "cmp3": _s(M3 * CAPP, F16), "sc3": _s(M3 * CAPP // 2 + 1, F16),
+    "j3": _s(A3 * CAPP, BF), "em": _s(NB), "rc": _s(4 * NB), "u3": _s(4 * NB), "p3": _s(NB), "off3": _s(NB, U16), "v3": _s(96),
+    "wo": _s(S + NB * (GAP + 64)), "to": _s(S), "y2": _s(40), "y4": _s(40), "zo": _s(64), "so1": _s(64), "so2": _s(64), "so3": _s(64), "lf": _s(S // 16, U16),
+    "rki": _s(32, I32), "rkf": _s(32),
+    "fw": _s(LW * (N + 1), X4), "fsc": _s(LW * (N + 1), U8), "oq": _s(S, X4), "os_": _s(S, U8), "wq": _s(128, X4), "wsc": _s(128, U8),
+    "yw": _s(LW * (N + 1)), "ys": _s(S), "pz": ("psum", [128, 512 * N], "float32"),
 }
-SEMAPHORES = ["v", "s", "t", "gi", "dkl", "dlk", "dsp", "dw", "dk", "dz", "kin", "slk", "colc", "cols", "lsent", "own", "st1", "st2"]
+SEMAPHORES = ["v", "s", "t", "gi", "dkl", "dlk", "dsp", "dw", "dk", "kin", "slk", "colc", "cols", "ksent", "lsent", "st1"]
 
 
 def rank_program(g, core, T, topo):
@@ -77,6 +82,9 @@ def rank_program(g, core, T, topo):
         need(q, deps)
         return done(Q[q].dma_start(out, in_), sem, 16)
 
+    def quad(b):
+        return slice(32 * b, 32 * b + 32)
+
     others = [d for d in range(N) if d != r]
     far = [d for d in others if topo.chip(T.cores[d]) != topo.chip(core)]
     near = [d for d in others if d not in far]
@@ -86,230 +94,250 @@ def rank_program(g, core, T, topo):
     for d in near:
         eng[d] = [e for e in topo.engines(core, T.cores[d]) if e not in fe]
 
-    def send(dests, sem, src, dst, few):
+    def send(dests, sem, src, dst, few, local="lsent"):
         tr = []
         for d in dests:
             rid, pid, _ = topo.addr(T.cores[d])
             m = sum(1 << e for e in (eng[d][:KE] if few else eng[d]))
             tr.append(RemoteDMATransfer(dst_ids=[DstId(rid=rid, pnc=pid)], dma_engine_mask=m, remote_sem=T.sem[sem], src=src(d), dst=dst(d)))
-            total["lsent"] = total.get("lsent", 0) + (KE if few else len(eng[d]))
-        g.remote_dma_fused(tr, local_sem=T.sem.lsent)
+            total[local] = total.get(local, 0) + (KE if few else len(eng[d]))
+        g.remote_dma_fused(tr, local_sem=T.sem[local])
+        return (local, total[local])
 
-    t_kl = dma("y", [], T.kl[:], T.ky[:], "dkl")
-    for a in range(8):
-        t_lk = dma("ys"[a % 2], [], T.lki[16 * a:16 * a + 16, :], T.ky[:], "dlk")
-    for a in range(8):
-        t_sp = dma("ys"[a % 2], [], T.spi[16 * a:16 * a + 16, :], T.sp[:], "dsp")
-    dma("y", [], T.kcs[:].bitcast(dt.uint8), T.kc[:], "dk")
-    t_k = dma("y", [], T.kss[:], T.ks[:], "dk")
-    t_w = dma("y", [], T.wt[:], T.w[:], "dw")
+    low = [d for d in others if d < r]
+    nl = N - 1 - r
+
+    t_0 = vop([], "set", T.lki[:], 0)
+    if low:
+        t_kl = dma("y", [], T.kl[:], T.ky[:], "dkl")
+    for a in range(4):
+        t_lk = dma("sy"[a % 2], [t_0], T.lki[32 * a:32 * a + 16, 0:32], T.ky[:], "dlk")
+    for a in range(4):
+        t_sp = dma("sy"[a % 2], [], T.lki[32 * a + 16:32 * a + 32, 32:33], T.sp[:], "dsp")
 
     def iota(out, pat, base, cm=0, i32=False):
         if i32:
             return done(g.iota(out, pat, base, cm), "gi")
         return done(g.iota(out, pat, base, cm, allow_small_or_imprecise_dtypes=True), "gi")
     t_pi = iota(T.pidx[:], [[0, 1]], 0, 1, True)
-    t_ie = iota(T.i_exp[:], [[1, 16], [0, 2]], 0, 0, True)
-    iota(T.i_sel[:], [[32, 16]], 0)
-    iota(T.i_e3[:], [[1, NB], [0, 2]], 0)
-    iota(T.i_dup[:], [[16, 2], [0, 2]], 0)
-    iota(T.i_il[:], [[8, 3]], 0)
-    t_ic = iota(T.i_d3[:], [[16, 24]], NS)
-    low = [d for d in others if d < r]
-    if low:
-        need("g", [t_kl])
-        send(low, "kin", lambda d: T.kl[:], lambda d: T.kb[:, 4 * (r - d - 1):4 * (r - d)], True)
-    t_ivj = iota(T.i_vj[:], [[1, 16], [16, 16]], 0)
-    t_wk = iota(T.wk[:, 0:NS], [[0, NS]], -1)
-    t_iv3 = iota(T.i_v3[:], [[32, 24], [1, 16]], Z0)
-    iota(T.kf[:, 0:Z0], [[0, Z0]], -1)
-    t_kf = iota(T.kf[:, Z0:Z0 + NS], [[1, N], [0, SL]], 0)
-    t_yw = iota(T.yw[:], [[0, Z0 + NS]], 0)
-    t_wo = iota(T.wo[:, 0:S], [[0, S]], 0)
+    t_id = iota(T.i_dup[:], [[16, 2], [0, 2]], 0)
+    iota(T.i_exp[:], [[1, NB], [0, 2]], 0)
+    iota(T.i_sel[:], [[32, NB]], 0)
+    iota(T.i_16[:], [[16, 16]], 0)
+    t_ic = iota(T.i_cj[:], [[1, 4], [16, 16]], -2 * C)
+    iota(T.i_oc[:], [[64, NB]], CAPP)
+    if A3 > NB:
+        need("g", [("gi", total["gi"])])
+        iota(T.i_oc[:, 0:A3 - NB], [[64, A3 - NB]], 2 * CAPP)
+    t_iv = iota(T.i_v3[:], [[32, NB], [1, 16]], KEYS + LW)
 
-    vop([], "set", T.ones[:], 1.0)
-    vop([], "set", T.zj[:], 0.0)
-    vop([], "set", T.zo[:], 0.0)
-    vop([], "set", T.st[:], -1.0)
-    vop([], "set", T.sc[:, 0:1], 0.0)
+    t_one = vop([], "set", T.ones[:], 1.0)
     t_zt = vop([], "set", T.zt[:], 0.0)
+    vop([], "set", T.r4[:], 0.0)
+    vop([], "set", T.zq[:], 0.0)
+    vop([], "set", T.st[:], 0.0)
+    vop([], "set", T.zz[:], 0.0)
     need("v", [t_pi])
-    for i, b in enumerate((15, 31, 16, 1, 14)):
+    for i, b in enumerate((15, 31, 16)):
         vop([], "ts", T.pm[:, i:i + 1], T.pidx[:], b, None, OP.bitwise_and)
-    t = vop([], "ts", T.pm[:, 5:6], T.pidx[:], 5, None, OP.arith_shift_right)
+    vop([], "ts", T.pm[:, 3:4], T.pidx[:], 3, 12, OP.arith_shift_right, OP.bitwise_and)
+    t = vop([], "ts", T.pm[:, 4:5], T.pidx[:], 2, 24, OP.arith_shift_right, OP.bitwise_and)
     t_pf = vop([t], "copy", T.pf[:], T.pm[:])
-    t_ek = vop([t_ie], "copy", T.expk[:], T.i_exp[:])
-    need("v", [t_pf, t_ic])
-    vop([], "ts", T.six[:], T.pf[:, 5:6], float(NB), None, OP.mult)
-    vop([], "ts", T.v32[:], T.pf[:, 3:4], 32.0, None, OP.mult)
-    t = vop([], "ts", T.vhf[:], T.pf[:, 4:5], 0.5, None, OP.mult)
-    t_sel = vop([], "ts", T.sel[:], T.i_sel[:], T.pf[:, 1:2], None, OP.add)
-    vop([], "ts", T.dup[:], T.i_dup[:], T.pf[:, 0:1], None, OP.add)
-    vop([], "ts", T.d3[:], T.i_d3[:], T.pf[:, 0:1], None, OP.add)
-    vop([], "ts", T.sc3[:, 0:1], T.pf[:, 0:1], 0.0, R0, OP.mult, OP.add)
-    t = vop([t], "ts", T.vsum[:], T.v32[:], T.vhf[:], None, OP.add)
-    vop([], "ts", T.exp3[:], T.i_e3[:], T.six[:], None, OP.add)
-    t_c = vop([t], "ts", T.il[:], T.i_il[:], T.vsum[:], None, OP.add)
-    t_lkf = vop([t_lk], "copy", T.lkf[:], T.lki[:])
-    t_at = vop([t_lkf], "tr", T.at[:], T.lkf[:])
-    t_xa = sop([t_at, t_ek], T.xa[:], T.at[:, 0:16].indirect(T.expk[:]), AF.Copy)
-    t_spf = vop([t_sp], "copy", T.spf[:], T.spi[:])
-    t_spx = vop([t_spf], "ts", T.spx[:], T.ones[:], T.spf[:], None, OP.mult)
-    t_spb = vop([t_spx], "tr", T.spb[:], T.spx[:])
-    vop([t_spb], "ts", T.r1[:], T.at[:, 0:16], T.spb[:, 0:1], float(SL), OP.is_ge, OP.mult)
-    t_r = vop([], "ts", T.r2[:], T.at[:, 0:16], T.spb[:, 1:2], float(SL), OP.is_ge, OP.mult)
-    t_r3 = vop([], "ts", T.r3[:], T.at[:, 0:16], T.spb[:, 2:3], float(SL), OP.is_ge, OP.mult)
-    t_r = vop([t_r], "tt", T.r12[:], T.r1[:], T.r2[:], OP.add)
-    t_r = vop([t_r, t_r3], "tt", T.r123[:], T.r12[:], T.r3[:], OP.add)
-    t_rr = vop([t_r], "ts", T.rr[:], T.r123[:], -1.0, None, OP.add)
+    p15, p31, p16, q4, q8 = [T.pf[:, i:i + 1] for i in range(5)]
+    if low:
+        t_klu = vop([t_kl], "copy", T.klu[:], T.kl[:])
+    t_zq = vop([t_zt], "q", T.fw[:, 0:128], T.fsc[:, 0:128], T.zt[:])
+    t_dup = vop([t_pf, t_id], "ts", T.dup[:], T.i_dup[:], p15, None, OP.add)
+    need("v", [t_ic])
+    t_xe = vop([], "ts", T.xe[:], T.i_exp[:, 0:8], q4, None, OP.add)
+    vop([], "ts", T.sel[:], T.i_sel[:], p31, None, OP.add)
+    vop([], "ts", T.dmp[:], T.i_16[:], p15, float(NS + 1), OP.add, OP.add)
+    vop([], "ts", T.m0[:], p15, 0.0, OFF, OP.is_equal, OP.mult)
+    t = vop([], "ts", T.sa[:], p16, 16.0, q4, OP.mult, OP.add)
+    t_cj = vop([t], "ts", T.cj[:], T.i_cj[:], T.sa[:], T.m0[:], OP.add, OP.add)
+
+    def late_constants():
+        t1 = vop([t_iv], "ts", T.rot1[:], T.i_16[:, 0:2], p15, q8, OP.add, OP.add)
+        t2 = vop([], "ts", T.sb[:], q8, 32.0, p16, OP.mult, OP.add)
+        vop([], "ts", T.exp3[:], T.i_exp[:], q8, None, OP.add)
+        vop([], "ts", T.oc6[:], T.i_oc[:], p31, p31, OP.add, OP.add)
+        t1 = vop([t1], "ts", T.rot2[:], T.rot1[:], 31, None, OP.bitwise_and)
+        vop([t2], "ts", T.v3c[:], T.i_v3[:], T.sb[:], T.m0[:], OP.add, OP.subtract)
+        vop([], "ts", T.sc3[:, 0:1], p15, 0.0, R0, OP.mult, OP.add)
+        vop([], "set", T.zo[:], 0.0)
+        vop([], "set", T.yw[:, 0:8], 0.0)
+        return vop([t1], "copy", T.rot[:], T.rot2[:])
+
+    t_ks = None
+    if low:
+        need("g", [t_klu])
+        t_ks = send(low, "kin", lambda d: T.klu[:], lambda d: T.kb[:, 4 * (r - d - 1):4 * (r - d)], True, "ksent")
+    t_wk = iota(T.wk[:, 1:NS + 1], [[0, N], [2 * GAP, NB], [0, 32]], EMPTY)
+    t_wo = iota(T.wo[:, 0:S], [[0, S]], -1)
+    dma("y", [t_ks, t_lk], T.kcs[:].bitcast(dt.uint8), T.kc[:], "dk")
+    t_k = dma("y", [], T.kss[:], T.ks[:], "dk")
+    t_w = dma("y", [], T.wt[:], T.w[:], "dw")
+
+    if nl:
+        t = sop([t_lk, t_dup], T.xd[:], T.lki[:, 0:32].indirect(T.dup[:]), AF.Copy)
+        t = vop([t], "tr", T.yd[:], T.xd[:])
+        vop([t], "copy", T.ol[:, 0:32:2], T.yd[:, 0:16])
+        t_ol = vop([], "copy", T.ol[:, 1:32:2], T.yd[:, 32:48])
+    t = sop([t_sp], T.spf[:], T.lki[:, 32:33], AF.Copy)
+    t = sop([t, t_lk], T.lkf[:], T.lki[:, 0:32], AF.Identity, bias=T.spf[:])
+    t_at = vop([t], "tr", T.at[:], T.lkf[:])
+    t_xa = sop([t_at, t_xe], T.xa[:], T.at[:].indirect(T.xe[:]), AF.Copy)
+    if nl:
+        t_tab = vop([t_ol, t_one], "copy", T.tab[:].indirect(T.ol[:]), T.ones[:])
+    need("v", [t_at])
+    for j in range(N - 1):
+        t = vop([], "ts", T.r4[0:32, j:64:4], T.at[0:32, 0:16], T.at[0:32, 16 + j:17 + j], float(SL * (j + 1)), OP.is_ge, OP.mult)
     t_fa = vop([t_xa], "tr", T.fa[:], T.xa[:])
-    t_fs = sop([t_fa, t_sel], T.fs[:], T.fa[:].indirect(T.sel[:]), AF.Copy)
-    t_cj = vop([t_ivj], "ts", T.cj[:], T.i_vj[:], 65536.0, 1.0, OP.mult, OP.add)
-    t_vk = vop([t_cj, t_fs], "tt", T.vk[:], T.fs[:], T.cj[:], OP.add)
+    t_rr = vop([t], "scan", T.rr[0:32, :], T.r4[0:32, 0:64:2], T.r4[0:32, 1:64:2], 0.0, OP.max, OP.max)
+    rr = T.rr[0:32, 1:32:2]
+    t_vk = vop([t_fa, t_cj], "tt", T.vk[:], T.fa[:].indirect(T.sel[:, 0:4]), T.cj[:], OP.min)
+    if r:
+        t_c = late_constants()
 
-    nl = N - 1 - r
+    fl = T.fl[0:32, :]
+    if nl == 0:
+        t_f = vop([], "set", fl, 1.0)
+    else:
+        total["kin"] = KE * nl
+        t = t_tab
+        for a in range(nl):
+            t = vop([t, ("kin", KE * nl)], "copy", T.tab[:].indirect(T.kb[:, 4 * a:4 * a + 4]), T.zt[:, 0:64])
+        t2 = sop([t], T.hit[:, GV:C], T.tab[:].indirect(T.ol[:, GV // 16:C // 16]), AF.Copy)
+        t = vop([t], "copy", T.hit[:, 0:GV], T.tab[:].indirect(T.ol[:, 0:GV // 16]))
+        t = vop([t, t2], "tr", T.hitt[:], T.hit[:])
+        t = vop([t], "tt", T.h2[:], T.hitt[:, 0:C:32], T.hitt[:, 16:C:32], OP.min)
+        t = vop([t], "tt", T.h4[0:64, :], T.h2[0:64, :], T.h2[64:128, :], OP.min)
+        t_f = vop([t], "tt", fl, T.h4[0:32, :], T.h4[32:64, :], OP.min)
 
-    def quads(tok, src, qu, qo, n):
-        t = vop([tok], "tt", qu[0:64, 0:n], src[0:64, 0:n], src[64:128, 0:n], OP.add)
+    t_e = sop([t_f], T.e1[0:32, :], fl, AF.Copy, scale=float(2 * NS))
+    vop([t_f, t_rr], "scan", T.zq[0:32, 0:16], rr, fl, 0.0, OP.max, OP.add)
+    t = vop([], "scan", T.zq[0:32, 32:48], T.zq[0:32, 16:32], fl, 0.0, OP.add, OP.add)
+    t = vop([t], "tr", T.zqt[0:32, :], T.zq[0:32, :])
+    t = vop([t], "scan", T.st[0:32, 1:33], T.zqt[0:32, 32:64], T.zqt[0:32, 0:32], 0.0, OP.add, OP.max)
+    t2 = vop([t_e], "tt", T.e2[0:32, :], T.dmp[0:32, :], T.e1[0:32, :], OP.subtract)
+    t = vop([t], "tr", T.bt[0:32, :], T.st[0:32, 0:32])
+    t = vop([t], "scan", T.qq[0:32, :], rr, fl, T.bt[0:32, 15:16], OP.max, OP.add)
+    t = vop([t, t2], "tt", T.o2[0:32, :], T.qq[0:32, :], T.e2[0:32, :], OP.max)
+    need("v", [t])
+    for b in range(4):
+        t = vop([], "copy", T.off[quad(b), :], T.o2[0:32, 4 * b:4 * b + 4])
+
+    def groups(tok, turned, n, two, four, out, op):
+        vop([tok], "tt", two[:, 0:n], turned[:, 1:32 * n:32], turned[:, 17:32 * n:32], op)
+        t = vop([], "tt", two[:, n:2 * n], turned[:, 0:32 * n:32], turned[:, 16:32 * n:32], op)
+        t = vop([t], "tt", four[0:64, :], two[0:64, :], two[64:128, :], op)
         need("v", [t])
         for b in range(4):
-            t = vop([], "tt", qo[32 * b:32 * b + 32, 0:n], qu[0:32, 0:n], qu[32:64, 0:n], OP.add)
+            t = vop([], "tt", out[quad(b), 0:2 * n], four[0:32, :], four[32:64, :], op)
         return t
 
-    if nl == 0:
-        t_f = vop([], "set", T.fl[:], 1.0)
-    else:
-        W = 128 * nl
-        WV, H = W - 128, W // 2
-        total["kin"] = KE * nl
-        t_kin = ("kin", KE * nl)
-        t2 = sop([t_kin, t_ek], T.x1[:, H:W], T.kb[:, 0:4 * nl].indirect(T.expk[:, 4 * nl:8 * nl]), AF.Copy)
-        t = vop([t_kin], "copy", T.x1[:, 0:H], T.kb[:, 0:4 * nl].indirect(T.expk[:, 0:4 * nl]))
-        t_b = vop([t, t2], "tr", T.b1[:, 0:W], T.x1[:, 0:W])
-        for c in range(16):
-            t_s = sop([t_b, t_at], T.js[:, 128 * c:128 * c + 128], T.b1[:, WV:W], AF.Sign, bias=T.at[:, c:c + 1], scale=-1.0, accum_out=T.rc[:, c:c + 1])
-        if nl > 1:
-            H = WV // 2
-            t = vop([t_b], "copy", T.b1u[:, 0:WV], T.b1[:, 0:WV])
-            for c in range(16):
-                t = vop([t] if c == 0 else [], "ts", T.cmp[:, WV * c:WV * (c + 1)], T.b1u[:, 0:WV], T.at[:, c:c + 1], None, OP.is_equal)
-            t = vop([t], "scan", T.sc[:, 1:16 * H + 1], T.cmp[:, 0:16 * WV:2], T.cmp[:, 1:16 * WV:2], 0.0, OP.add, OP.add)
-            t = vop([t], "copy", T.rc[:, 16:33], T.sc[:, 0:16 * H + 1:H])
-        need("v", [t_s])
-        t = quads(t, T.rc, T.qu, T.qo, 33 if nl > 1 else 16)
-        t_p = vop([t], "ts", T.par[:], T.qo[:, 0:16], 1, None, OP.bitwise_and)
-        if nl > 1:
-            t = vop([], "tt", T.fv[:], T.qo[:, 17:33], T.qo[:, 16:32], OP.is_equal)
-            t_f = vop([t, t_p], "tt", T.fl[:], T.fv[:], T.par[:], OP.is_gt)
-        else:
-            t_f = vop([t_p], "ts", T.fl[:], T.par[:], 0.0, None, OP.is_equal)
-
-    t_tot = sop([t_f], T.js[:, 0:16], T.fl[:], AF.Copy, accum_out=T.tot[:])
-    t_q = vop([t_f, t_rr], "scan", T.q0[:], T.rr[:], T.fl[:], -1.0, OP.max, OP.add)
-    t_e = vop([t_c], "ts", T.e1[:], T.fl[:], 0.0, None, OP.is_equal)
-    vop([t_q], "ts", T.ct[:, 0:32], T.ones[:], T.q0[:, 15:16], None, OP.mult)
-    t = vop([t_tot], "ts", T.ct[:, 32:64], T.ones[:], T.tot[:], None, OP.mult)
-    t2 = vop([t_e], "tt", T.e2[:], T.d3[:, 0:16], T.e1[:], OP.mult)
-    t = vop([t], "tr", T.ctt[:], T.ct[:])
-    t = vop([t], "scan", T.st[:, 1:33], T.ctt[:, 32:64], T.ctt[:, 0:32], -1.0, OP.add, OP.max)
-    t = vop([t], "tr", T.bt[:], T.st[:, 0:32])
-    t = vop([t], "scan", T.qq[:], T.rr[:], T.fl[:], T.bt[:, 0:1], OP.max, OP.add)
-    t = vop([t, t2], "tt", T.o2[:], T.qq[:], T.e2[:], OP.max)
-    t_off = vop([t], "copy", T.off[:], T.o2[:])
-
-    t = vop([t_off, t_vk, t_wk], "copy", T.wk[:].indirect(T.off[:]), T.vk[:])
-    t = vop([t], "tr", T.tk[:], T.wk[:, 0:NS])
-    te, to = T.tk[:, 0:NS:32], T.tk[:, 16:NS:32]
-    t_zi = vop([t], "tt", T.zi[:], te, to, OP.add)
-    vop([t_zi], "ts", T.ki[:], T.zi[:], 65535, None, OP.bitwise_and)
-    t = vop([], "ts", T.bz[:], T.zi[:], 0.0, BIG, OP.is_lt, OP.mult)
-    t_kz = vop([t], "tt", T.kz[:], T.ki[:], T.bz[:], OP.add)
-    need("g", [t_kz])
-    send(others, "slk", lambda d: T.kz[:, NB * d:NB * (d + 1)], lambda d: T.ap[:, NB * r:NB * (r + 1)], True)
-    t_own = dma("y", [t_kz], T.ap[:, NB * r:NB * (r + 1)], T.kz[:, NB * r:NB * (r + 1)], "own")
-
-    def lists(tok, z, s1, s2, s3, out):
-        t = vop([tok], "tr", s1[:], z[:])
-        t = vop([t], "copy", s2[:], s1[:].indirect(T.dup[:]))
+    def lists(tok, n, s1, s2, s3, out, *conv):
+        t = vop([tok], "copy", s2[:], s1[:, 0:32].indirect(T.dup[:]))
         t = vop([t], "tr", s3[:], s2[:])
-        return vop([t], "copy", out[:], s3[:].indirect(T.il[:]))
+        vop([t], "ts", out[:, 0:2 * n:2], s3[:, 0:n], *conv)
+        return vop([], "ts", out[:, 1:2 * n:2], s3[:, 32:32 + n], *conv)
 
-    vop([], "ts", T.ji[:], T.zi[:], 16, None, OP.arith_shift_right)
-    t = vop([], "ts", T.ho[:], to, 0.0, 256.0, OP.is_ge, OP.mult)
-    t = vop([t], "tt", T.zj[:, 0:24], T.ji[:], T.ho[:], OP.add)
-    t_lj = lists(t, T.zj, T.sw1, T.sw2, T.sw3, T.lj)
+    NZ = N * NB
+    t = vop([t, t_vk, t_wk], "copy", T.wk[:].indirect(T.off[:]), T.vk[:])
+    t = vop([t], "tr", T.tk[:], T.wk[:, 1:NS + 1])
+    t_zz = groups(t, T.tk, NZ, T.z2, T.z4, T.zz, OP.min)
+    need("g", [t_zz])
+    send(others, "slk", lambda d: T.zz[:, NZ + NB * d:NZ + NB * d + 8], lambda d: T.ap[:, 8 * r:8 * r + 8], True)
+    t_own = sop([t_zz], T.ap[:, 8 * r:8 * r + 8], T.zz[:, NZ + NB * r:NZ + NB * r + 8], AF.Copy)
+    t = vop([t_zz], "tr", T.sw1[:], T.zz[:, 0:32])
+    t_lj = lists(t, NZ, T.sw1, T.sw2, T.sw3, T.lj, float(2 * C), float(C - 1), OP.add, OP.min)
 
     def pick(d, oc, osc):
-        L = T.lj[:, 12 * d:12 * d + CAPP // 16]
+        L = T.lj[:, 2 * NB * d:2 * NB * d + CAPP // 16]
         return (vop([t_lj, t_k], "copy", oc.bitcast(dt.uint32), T.kcs[:].bitcast(dt.uint32).indirect(L)),
                 sop([t_lj, t_k], osc, T.kss[:].indirect(L), AF.Copy))
     for d in far + near:
         t_pv, t_ps = pick(d, T["pc%d" % d][:], T["ps%d" % d][:])
-    w0 = Z0 + SL * r
+    w0 = LW * (r + 1)
     need("g", [t_pv])
     send(far + near, "colc", lambda d: T["pc%d" % d][:].bitcast(dt.uint8), lambda d: T.fw[:, w0:w0 + CAPP].bitcast(dt.uint8), False)
     need("g", [t_ps])
     send(far + near, "cols", lambda d: T["ps%d" % d][:], lambda d: T.fsc[:, w0:w0 + CAPP], False)
+    if r == 0:
+        t_c = late_constants()
 
     tk = {}
 
     def own():
         tk["v"], tk["s"] = pick(r, T.fw[:, w0:w0 + CAPP], T.fsc[:, w0:w0 + CAPP])
-        t = vop([t_zt], "q", T.zc[:], T.zs[:], T.zt[:])
-        dma("y", [t], T.fw[:, 0:Z0].bitcast(dt.uint8), T.zc[:, 0:Z0].bitcast(dt.uint8), "dz")
-        tk["z"] = dma("y", [t], T.fsc[:, 0:Z0], T.zs[:, 0:Z0], "dz")
         tk["w"] = vop([t_w], "q", T.wq[:], T.wsc[:], T.wt[:])
     if r:
         own()
 
     total["slk"] = KE * (N - 1)
     total["colc"] = total["cols"] = sum(len(eng[d]) for d in others)
-    t_in = [("slk", total["slk"]), t_own]
+    t_in = [("slk", total["slk"]), t_own, t_c]
     H = SL // 2
-    t2 = sop(t_in + [t_c], T.x3[:, H:SL], T.ap[:].indirect(T.exp3[:, NB:2 * NB]), AF.Copy)
+    t2 = sop(t_in, T.x3[:, H:SL], T.ap[:].indirect(T.exp3[:, NB:2 * NB]), AF.Copy)
     t = vop(t_in, "copy", T.x3[:, 0:H], T.ap[:].indirect(T.exp3[:, 0:NB]))
+    t_ax = vop([], "copy", T.apx[:], T.ap[:].indirect(T.rot[:]))
     t_b3 = vop([t, t2], "tr", T.b3[:], T.x3[:])
-    for x in range(A3):
-        t_s = sop(t_in + [t_b3], T.j3[:, SL * x:SL * (x + 1)], T.b3[:], AF.Sign, bias=T.ap[:, x:x + 1], scale=-1.0, accum_out=T.rs3[:, x:x + 1])
-    t = vop([t_b3], "copy", T.b3u[:], T.b3[:])
+
+    def scal(c):
+        a = 8 * (1 + c // NB) + c % NB
+        return T.apx[:, a:a + 1]
+    for c in range(A3):
+        t_s = sop([t_b3, t_ax], T.j3[:, CAPP * c:CAPP * (c + 1)], T.b3[:, 0:CAPP], AF.Sign, bias=scal(c), scale=-1.0, accum_out=T.rc[:, NB + c:NB + c + 1])
+    t = vop([t_b3], "copy", T.b3u[:], T.b3[:, 0:CAPP])
+    t_em = vop([t_ax], "ts", T.em[:], T.apx[:, 0:NB], float(2 * S - EMPTY), 0.0, OP.add, OP.max)
     need("v", [t])
     for x in range(M3):
-        t = vop([], "ts", T.cmp3[:, SL * x:SL * (x + 1)], T.b3u[:], T.ap[:, A3 + x:A3 + x + 1], None, OP.is_lt)
-    t_vs = vop([], "ts", T.vs[:], T.ap[:], 65536.0, None, OP.is_ge)
-    t = vop([t], "scan", T.sc3[:, 1:M3 * H + 1], T.cmp3[:, 0:M3 * SL:2], T.cmp3[:, 1:M3 * SL:2], R0, OP.add, OP.add)
-    t_vd = vop([t_vs], "tt", T.vd[:], T.d3[:], T.vs[:], OP.mult)
-    t = vop([t], "tt", T.rc3[:, A3:24], T.sc3[:, H:M3 * H + 1:H], T.sc3[:, 0:(M3 - 1) * H + 1:H], OP.subtract)
+        t = vop([], "ts", T.cmp3[:, CAPP * x:CAPP * (x + 1)], T.b3u[:], scal(A3 + x), 2.0, OP.is_lt, OP.mult)
+    H = CAPP // 2
+    vop([t_em], "tt", T.rc[:, 0:NB], T.em[:], T.oc6[:], OP.add)
+    t = vop([t], "scan", T.sc3[:, 1:M3 * H + 1], T.cmp3[:, 0:M3 * CAPP:2], T.cmp3[:, 1:M3 * CAPP:2], R0, OP.add, OP.add)
+    t_v3 = vop([], "tt", T.v3[:], T.b3[:].indirect(T.sel[:]), T.v3c[:], OP.max)
+    t = vop([t], "tt", T.rc[:, NB + A3:4 * NB], T.sc3[:, H:M3 * H + 1:H], T.sc3[:, 0:(M3 - 1) * H + 1:H], OP.subtract)
     if r == 0:
         own()
-    t = vop([t, t_s], "ts", T.rc3[:, 0:A3], T.rs3[:, 0:A3], 0.5, SL / 2 - 0.125, OP.mult, OP.add)
-    t_v3 = sop([t_iv3, t_pf], T.v3[:], T.i_v3[:], AF.Identity, bias=T.pf[:, 2:3])
-    for s in range(N):
-        t_kc = sop([t_kf], T.kf[0:32, Z0 + SL * s:Z0 + SL * (s + 1)], T.b3[32 * s:32 * s + 32, :], AF.Copy)
     for s in [r] + others:
-        a = Z0 + SL * s
+        a = LW * (s + 1)
         need("t", [tk["w"]] + ([tk["v"], tk["s"]] if s == r else [("colc", total["colc"]), ("cols", total["cols"])]))
         t_t = done(g.tensor.matmul_mx(T.pz[:, 512 * s:512 * s + CAPP], T.wq[:], T.wsc[:], T.fw[:, a:a + CAPP], T.fsc[:, a:a + CAPP], True, True), "t")
-        t_y = sop([t_t, t_yw], T.yw[:, a:a + CAPP], T.pz[:, 512 * s:512 * s + CAPP], AF.Copy)
-    t = quads(t, T.rc3, T.qu3, T.qo3, 24)
-    t = vop([t, t_vd], "tt", T.p2[:], T.qo3[:], T.vd[:], OP.max)
-    t = vop([t], "copy", T.off3[:], T.p2[:])
+        t_y = sop([t_t], T.yw[:, a:a + CAPP], T.pz[:, 512 * s:512 * s + CAPP], AF.Copy)
+    W = 2 * NB
+    vop([t, t_s], "tt", T.u3[0:64, 0:W], T.rc[0:64, 0:W], T.rc[64:128, W:2 * W], OP.add)
+    t = vop([], "tt", T.u3[0:64, W:2 * W], T.rc[0:64, W:2 * W], T.rc[64:128, 0:W], OP.add)
+    need("v", [t])
+    for s in range(N):
+        k = (s - 1) % N
+        t = vop([], "tt", T.p3[quad(s), :], T.u3[0:32, NB * s:NB * (s + 1)], T.u3[32:64, NB * k:NB * (k + 1)], OP.add)
+    t = vop([t], "ts", T.off3[:], T.p3[:], 0.5, 0.25, OP.mult, OP.add)
     t = vop([t, t_v3, t_wo], "copy", T.wo[:].indirect(T.off3[:]), T.v3[:])
     t = vop([t], "tr", T.to[:], T.wo[:, 0:S])
-    t = vop([t], "tt", T.zo[:, 0:20], T.to[:, 0:S:32], T.to[:, 16:S:32], OP.add)
-    t_lf = lists(t, T.zo, T.so1, T.so2, T.so3, T.lf)
+    NO = S // 32
+    t = groups(t, T.to, NO, T.y2, T.y4, T.zo, OP.max)
+    t_so = vop([t], "tr", T.so1[:], T.zo[:])
+    t_lf = lists(t_so, NO, T.so1, T.so2, T.so3, T.lf, float(KEYS), None, OP.subtract)
+    n1 = 32 - NO
+    dma("y", [t_so], T.ok[0:1, 0:32 * n1], T.so1[NO:32, 0:32], "st1")
+    dma("y", [], T.ok[0:1, 32 * n1:S], T.so1[0:NO - n1, 32:64], "st1")
 
-    t_sc = sop([t_lf, ("cols", total["cols"]), tk["s"], tk["z"]], T.os_[:], T.fsc[:].indirect(T.lf[:, 0:S // 16]), AF.Copy)
-    for c in range(S // CH):
-        lo, hi = c * CH, (c + 1) * CH
-        t = vop([t_lf, ("colc", total["colc"]), tk["v"], tk["z"]], "copy", T.oq[:, lo:hi].bitcast(dt.uint32), T.fw[:].bitcast(dt.uint32).indirect(T.lf[:, lo // 16:hi // 16]))
-        dma("y", [t], T.oc[:, 4 * lo:4 * hi], T.oq[:, lo:hi].bitcast(dt.uint8), "st1")
+    def at(lo, hi):
+        return T.lf[:, lo // 16:hi // 16]
+    lo = ly = 0
+    for n, m in zip(CHC, CHY):
+        t = vop([t_lf, ("colc", total["colc"]), tk["v"], t_zq], "copy", T.oq[:, lo:lo + n].bitcast(dt.uint32), T.fw[:].bitcast(dt.uint32).indirect(at(lo, lo + n)))
+        t2 = sop([t_y, t_lf], T.ys[:, ly:ly + m], T.yw[:].indirect(at(ly, ly + m)), AF.Copy)
+        dma("y", [t], T.oc[:, 4 * lo:4 * (lo + n)], T.oq[:, lo:lo + n].bitcast(dt.uint8), "st1")
+        dma("y", [t2], T.y[:, ly:ly + m], T.ys[:, ly:ly + m], "st1")
+        lo, ly = lo + n, ly + m
+    H = S // 2
+    t2 = sop([("cols", total["cols"]), tk["s"], t_zq], T.os_[:, H:S], T.fsc[:].indirect(at(H, S)), AF.Copy)
+    t = vop([("cols", total["cols"]), tk["s"]], "copy", T.os_[:, 0:H], T.fsc[:].indirect(at(0, H)))
+    t3 = vop([], "ts", T.rki[0:32, :], T.so1[0:32, 0:32], 1.0 / LW, -(KEYS / LW + 1.35), OP.mult, OP.add)
+    t3 = vop([t3], "ts", T.rkf[0:32, :], T.rki[0:32, :], -1.0, None, OP.max)
     for i in range(4):
-        dma("y", [t_sc], T.osc[4 * i:4 * i + 4, :], T.os_[32 * i:32 * i + 4, :], "st1")
-    t = vop([t_y], "copy", T.ys[:, 0:YV], T.yw[:].indirect(T.lf[:, 0:YV // 16]))
-    dma("y", [t], T.y[:, 0:YV], T.ys[:, 0:YV], "st1")
-    t = sop([t_y, t_lf], T.ys[:, YV:S], T.yw[:].indirect(T.lf[:, YV // 16:S // 16]), AF.Copy)
-    t2 = sop([t_kc], T.okf[:], T.kf[:].indirect(T.lf[:, 0:S // 16]), AF.Copy)
-    dma("y", [t], T.y[:, YV:S], T.ys[:, YV:S], "st1")
-    dma("s", [t2], T.ok[0:1, :], T.okf[0:1, :], "st2")
-    dma("s", [], T.ok[1:2, :], T.okf[32:33, :], "st2")
+        dma("ys"[i % 2], [t, t2], T.osc[4 * i:4 * i + 4, :], T.os_[32 * i:32 * i + 4, :], "st1")
+    dma("y", [t3], T.ok[1:2, :], T.rkf[0:NO, :], "st1")
     need("g", list(total.items()))

@@ -9,13 +9,12 @@ NS = N * SL
 LW = 256
 EMPTY = 2 * KEYS
 GAP = 576
-OFF = 2.0 ** 19
-GV = 256
-A3 = 7
+GV = 128
+A3 = 9
 M3 = 3 * NB - A3
 R0 = -float(M3 * CAPP)
-CHC = (192, 448)
-CHY = (192, 448)
+TAIL = [("c", 0, 192), ("y", 0, 192), ("c", 192, 640), ("y", 192, 640), ("s",)]
+SV = 320
 
 
 def _s(n, d="float32"):
@@ -24,15 +23,14 @@ def _s(n, d="float32"):
 
 X4, U8, U16, BF, I32, F16 = "float8_e4m3fn_x4", "uint8", "uint16", "bfloat16", "int32", "float16"
 SCRATCH = {
-    "kl": _s(4, I32), "klu": _s(4, U16), "lki": _s(40, I32), "wt": _s(512, BF), "kcs": _s(C, X4), "kss": _s(C, U8),
-    "pidx": _s(1, I32), "pm": _s(5, I32), "pf": _s(5), "m0": _s(1), "sa": _s(1), "sb": _s(1),
-    "i_dup": _s(4), "dup": _s(4, U16), "i_sel": _s(NB), "sel": _s(NB, U16), "i_exp": _s(2 * NB), "xe": _s(8, U16), "exp3": _s(2 * NB, U16),
+    "lki": _s(32, I32), "spi": _s(1, I32), "klu": _s(8, U16), "wt": _s(512, BF), "wq": _s(128, X4), "wsc": _s(128, U8), "kcs": _s(C, X4), "kss": _s(C, U8),
+    "pidx": _s(1, I32), "pm": _s(7, I32), "pf": _s(7), "cv": _s(2), "cs": _s(8),
+    "i_dup": _s(4), "dup": _s(4, U16), "osel": _s(2, U16), "asel": _s(2, U16), "i_xe": _s(4), "xe": _s(4, U16), "i_yc": _s(64),
+    "i_sel": _s(NB), "sel": _s(NB, U16), "i_exp": _s(2 * NB), "exp3": _s(2 * NB, U16),
     "i_16": _s(16), "rot1": _s(2, I32), "rot2": _s(2, I32), "rot": _s(2, U16), "dmp": _s(16),
-    "i_cj": _s(64), "cj": _s(64), "i_v3": _s(96), "v3c": _s(96), "i_oc": _s(NB), "oc6": _s(NB),
-    "ones": _s(C, BF), "zt": _s(C, BF),
-    "xd": _s(64), "yd": _s(64), "ol": _s(32, U16), "spf": _s(1), "lkf": _s(32), "at": _s(32), "r4": _s(64), "rr": _s(32),
-    "xa": _s(128), "fa": _s(128), "vk": _s(64),
-    "kb": _s(12, U16), "tab": _s(KEYS, BF), "hit": _s(C, BF), "hitt": _s(C, BF), "h2": _s(16), "h4": _s(16), "fl": _s(16),
+    "i_v3": _s(96), "v3c": _s(96), "oc6": _s(NB), "ones": _s(C // 2, BF), "zt": _s(C, BF),
+    "spf": _s(1), "xd": _s(64), "yd": _s(128), "ol": _s(16, U16), "at": _s(16), "sg": _s(48), "r4": _s(64), "rr": _s(32), "xa": _s(64), "vk": _s(64),
+    "kb": _s(24, U16), "tab": _s(KEYS, BF), "hit": _s(C // 2, BF), "hitt": _s(C // 2, BF), "h4": _s(16), "fl": _s(16),
     "zq": _s(64), "zqt": _s(64), "st": _s(64), "bt": _s(32), "qq": _s(16), "e1": _s(16), "e2": _s(16), "o2": _s(16), "off": _s(4, U16),
     "wk": _s(NS + 264), "tk": _s(NS), "z2": _s(48), "z4": _s(48), "zz": _s(56),
     "sw1": _s(32), "sw2": _s(64), "sw3": _s(64), "lj": _s(48, U16),
@@ -41,11 +39,11 @@ SCRATCH = {
     "ap": _s(32), "apx": _s(32), "x3": _s(SL), "b3": _s(SL), "b3u": _s(CAPP, U16), "cmp3": _s(M3 * CAPP, F16), "sc3": _s(M3 * CAPP // 2 + 1, F16),
     "j3": _s(A3 * CAPP, BF), "em": _s(NB), "rc": _s(4 * NB), "u3": _s(4 * NB), "p3": _s(NB), "off3": _s(NB, U16), "v3": _s(96),
     "wo": _s(S + NB * (GAP + 64)), "to": _s(S), "y2": _s(40), "y4": _s(40), "zo": _s(64), "so1": _s(64), "so2": _s(64), "so3": _s(64), "lf": _s(S // 16, U16),
-    "rki": _s(32, I32), "rkf": _s(32),
-    "fw": _s(LW * (N + 1), X4), "fsc": _s(LW * (N + 1), U8), "oq": _s(S, X4), "os_": _s(S, U8), "wq": _s(128, X4), "wsc": _s(128, U8),
+    "rki": _s(32, U16), "rkf": _s(32),
+    "fw": _s(LW * (N + 1), X4), "fsc": _s(LW * (N + 1), U8), "oq": _s(S, X4), "os_": _s(S, U8),
     "yw": _s(LW * (N + 1)), "ys": _s(S), "pz": ("psum", [128, 512 * N], "float32"),
 }
-SEMAPHORES = ["v", "s", "t", "gi", "dkl", "dlk", "dsp", "dw", "dk", "kin", "slk", "colc", "cols", "ksent", "lsent", "st1"]
+SEMAPHORES = ["v", "s", "t", "gi", "dlk", "dsp", "dw", "dk", "kin1", "kin2", "kin3", "slk", "colc", "cols", "ksent", "lsent", "st1"]
 
 
 def rank_program(g, core, T, topo):
@@ -78,9 +76,20 @@ def rank_program(g, core, T, topo):
         need("s", deps)
         return done(act.activation(*a, **k), "s")
 
+    def lin(deps, out, in_, scale=1.0, bias=0.0):
+        return sop(deps, out, in_, AF.Identity, bias=bias, scale=scale)
+
     def dma(q, deps, out, in_, sem):
         need(q, deps)
         return done(Q[q].dma_start(out, in_), sem, 16)
+
+    def iota(out, pat, base, cm=0, i32=False):
+        if i32:
+            return done(g.iota(out, pat, base, cm), "gi")
+        return done(g.iota(out, pat, base, cm, allow_small_or_imprecise_dtypes=True), "gi")
+
+    def fill(out, value=0):
+        return iota(out, [[0, out.shape[1]]], value)
 
     def quad(b):
         return slice(32 * b, 32 * b + 32)
@@ -94,182 +103,187 @@ def rank_program(g, core, T, topo):
     for d in near:
         eng[d] = [e for e in topo.engines(core, T.cores[d]) if e not in fe]
 
-    def send(dests, sem, src, dst, few, local="lsent"):
+    def short(d):
+        return eng[d][:KE]
+
+    def send(dests, sem, src, dst, engines, local="lsent"):
         tr = []
         for d in dests:
             rid, pid, _ = topo.addr(T.cores[d])
-            m = sum(1 << e for e in (eng[d][:KE] if few else eng[d]))
-            tr.append(RemoteDMATransfer(dst_ids=[DstId(rid=rid, pnc=pid)], dma_engine_mask=m, remote_sem=T.sem[sem], src=src(d), dst=dst(d)))
-            total[local] = total.get(local, 0) + (KE if few else len(eng[d]))
+            tr.append(RemoteDMATransfer(dst_ids=[DstId(rid=rid, pnc=pid)], dma_engine_mask=sum(1 << e for e in engines(d)), remote_sem=T.sem[sem],
+                                        src=src(d), dst=dst(d)))
+            total[local] = total.get(local, 0) + len(engines(d))
         g.remote_dma_fused(tr, local_sem=T.sem[local])
         return (local, total[local])
 
     low = [d for d in others if d < r]
     nl = N - 1 - r
 
-    t_0 = vop([], "set", T.lki[:], 0)
-    if low:
-        t_kl = dma("y", [], T.kl[:], T.ky[:], "dkl")
-    for a in range(4):
-        t_lk = dma("sy"[a % 2], [t_0], T.lki[32 * a:32 * a + 16, 0:32], T.ky[:], "dlk")
-    for a in range(4):
-        t_sp = dma("sy"[a % 2], [], T.lki[32 * a + 16:32 * a + 32, 32:33], T.sp[:], "dsp")
+    for a in range(2):
+        t_sp = dma("ys"[a], [], T.spi[16 * a:16 * a + 16, :], T.sp[:], "dsp")
+    for a in range(8):
+        t_lk = dma("ys"[a % 2], [], T.lki[16 * a:16 * a + 16, :], T.ky[:], "dlk")
 
-    def iota(out, pat, base, cm=0, i32=False):
-        if i32:
-            return done(g.iota(out, pat, base, cm), "gi")
-        return done(g.iota(out, pat, base, cm, allow_small_or_imprecise_dtypes=True), "gi")
     t_pi = iota(T.pidx[:], [[0, 1]], 0, 1, True)
     t_id = iota(T.i_dup[:], [[16, 2], [0, 2]], 0)
-    iota(T.i_exp[:], [[1, NB], [0, 2]], 0)
-    iota(T.i_sel[:], [[32, NB]], 0)
-    iota(T.i_16[:], [[16, 16]], 0)
-    t_ic = iota(T.i_cj[:], [[1, 4], [16, 16]], -2 * C)
-    iota(T.i_oc[:], [[64, NB]], CAPP)
-    if A3 > NB:
-        need("g", [("gi", total["gi"])])
-        iota(T.i_oc[:, 0:A3 - NB], [[64, A3 - NB]], 2 * CAPP)
-    t_iv = iota(T.i_v3[:], [[32, NB], [1, 16]], KEYS + LW)
+    iota(T.i_xe[:], [[2, 2], [32, 2]], 0)
+    iota(T.i_yc[:], [[-256, 2], [-1, 32]], 0)
+    t_r4 = fill(T.r4[:, 3:64:4])
+    t_z1 = fill(T.zt[:, 0:128])
 
-    t_one = vop([], "set", T.ones[:], 1.0)
-    t_zt = vop([], "set", T.zt[:], 0.0)
-    vop([], "set", T.r4[:], 0.0)
-    vop([], "set", T.zq[:], 0.0)
-    vop([], "set", T.st[:], 0.0)
-    vop([], "set", T.zz[:], 0.0)
+    vop([], "set", T.spf[:], 0.0)
     need("v", [t_pi])
-    for i, b in enumerate((15, 31, 16)):
-        vop([], "ts", T.pm[:, i:i + 1], T.pidx[:], b, None, OP.bitwise_and)
-    vop([], "ts", T.pm[:, 3:4], T.pidx[:], 3, 12, OP.arith_shift_right, OP.bitwise_and)
-    t = vop([], "ts", T.pm[:, 4:5], T.pidx[:], 2, 24, OP.arith_shift_right, OP.bitwise_and)
+    for i, (sh, b) in enumerate(((0, 15), (0, 16), (0, 1), (1, 15), (0, 31), (3, 12), (2, 24))):
+        t = vop([], "ts", T.pm[:, i:i + 1], T.pidx[:], sh, b, OP.arith_shift_right, OP.bitwise_and)
     t_pf = vop([t], "copy", T.pf[:], T.pm[:])
-    p15, p31, p16, q4, q8 = [T.pf[:, i:i + 1] for i in range(5)]
-    if low:
-        t_klu = vop([t_kl], "copy", T.klu[:], T.kl[:])
-    t_zq = vop([t_zt], "q", T.fw[:, 0:128], T.fsc[:, 0:128], T.zt[:])
-    t_dup = vop([t_pf, t_id], "ts", T.dup[:], T.i_dup[:], p15, None, OP.add)
-    need("v", [t_ic])
-    t_xe = vop([], "ts", T.xe[:], T.i_exp[:, 0:8], q4, None, OP.add)
-    vop([], "ts", T.sel[:], T.i_sel[:], p31, None, OP.add)
-    vop([], "ts", T.dmp[:], T.i_16[:], p15, float(NS + 1), OP.add, OP.add)
-    vop([], "ts", T.m0[:], p15, 0.0, OFF, OP.is_equal, OP.mult)
-    t = vop([], "ts", T.sa[:], p16, 16.0, q4, OP.mult, OP.add)
-    t_cj = vop([t], "ts", T.cj[:], T.i_cj[:], T.sa[:], T.m0[:], OP.add, OP.add)
-
-    def late_constants():
-        t1 = vop([t_iv], "ts", T.rot1[:], T.i_16[:, 0:2], p15, q8, OP.add, OP.add)
-        t2 = vop([], "ts", T.sb[:], q8, 32.0, p16, OP.mult, OP.add)
-        vop([], "ts", T.exp3[:], T.i_exp[:], q8, None, OP.add)
-        vop([], "ts", T.oc6[:], T.i_oc[:], p31, p31, OP.add, OP.add)
-        t1 = vop([t1], "ts", T.rot2[:], T.rot1[:], 31, None, OP.bitwise_and)
-        vop([t2], "ts", T.v3c[:], T.i_v3[:], T.sb[:], T.m0[:], OP.add, OP.subtract)
-        vop([], "ts", T.sc3[:, 0:1], p15, 0.0, R0, OP.mult, OP.add)
-        vop([], "set", T.zo[:], 0.0)
-        vop([], "set", T.yw[:, 0:8], 0.0)
-        return vop([t1], "copy", T.rot[:], T.rot2[:])
+    p15, p16, p1, ph, p31, q4, q8 = [T.pf[:, i:i + 1] for i in range(7)]
+    second, first = T.cv[:, 0:1], T.cv[:, 1:2]
+    m64, aq, u64, p15n, sb, sb2, p31q = [T.cs[:, i:i + 1] for i in range(7)]
+    t_2 = vop([t_pf], "ts", second, p16, 1.0 / 16, None, OP.mult)
+    vop([], "ts", first, p16, -1.0 / 16, 1.0, OP.mult, OP.add)
+    t_dup = vop([t_id], "ts", T.dup[:], T.i_dup[:], p15, None, OP.add)
+    if nl:
+        vop([], "ts", T.osel[:, 0:1], p1, 32.0, ph, OP.mult, OP.add)
+        t_one = vop([], "set", T.ones[:], 1.0)
+    t_as = lin([t_pf], T.asel[:, 0:1], p16, 2.0, p15)
 
     t_ks = None
     if low:
-        need("g", [t_klu])
-        t_ks = send(low, "kin", lambda d: T.klu[:], lambda d: T.kb[:, 4 * (r - d - 1):4 * (r - d)], True, "ksent")
-    t_wk = iota(T.wk[:, 1:NS + 1], [[0, N], [2 * GAP, NB], [0, 32]], EMPTY)
-    t_wo = iota(T.wo[:, 0:S], [[0, S]], -1)
+        for b in range(2):
+            t = vop([t_lk], "copy", T.klu[quad(b), :], T.lki[quad(b), 8 * b:8 * b + 8])
+            t2 = sop([t_lk], T.klu[quad(b + 2), :], T.lki[quad(b + 2), 8 * b + 16:8 * b + 24], AF.Copy)
+        need("g", [t, t2])
+        t_ks = send(low, "kin%d" % r, lambda d: T.klu[:], lambda d: T.kb[:, 8 * (r - d - 1):8 * (r - d)], short, "ksent")
     dma("y", [t_ks, t_lk], T.kcs[:].bitcast(dt.uint8), T.kc[:], "dk")
     t_k = dma("y", [], T.kss[:], T.ks[:], "dk")
     t_w = dma("y", [], T.wt[:], T.w[:], "dw")
+    t = vop([], "ts", T.rot1[:], T.i_dup[:, 0:4:2], p15, q8, OP.add, OP.add)
+    t_rot = vop([t], "ts", T.rot2[:], T.rot1[:], 31, None, OP.bitwise_and)
 
+    t_i16 = iota(T.i_16[:], [[16, 16]], NS + 1)
+    fill(T.zq[:, 16:64])
+    t_zs = fill(T.st[:, 0:1])
+    fill(T.zz[:, 48:56])
+    t_wk = iota(T.wk[:, 1:NS + 1], [[0, N], [2 * GAP, NB], [0, 32]], EMPTY)
+    iota(T.i_exp[:], [[1, NB], [0, 2]], 0)
+    iota(T.i_sel[:], [[32, NB]], 0)
+    t_iv = iota(T.i_v3[:], [[32, NB], [1, 16]], KEYS + LW)
+    iota(T.oc6[:, 0:A3 - NB], [[64, A3 - NB]], 2 * CAPP)
+    iota(T.oc6[:, A3 - NB:NB], [[64, 2 * NB - A3]], CAPP + 64 * (A3 - NB))
+    fill(T.zo[:, 40:64])
+    fill(T.yw[:, 0:8])
+    fill(T.zt[:, 128:C])
+    t_wo = fill(T.wo[:, 0:S], -1)
+
+    t = lin([t_sp, t_2], T.spf[0:32, :], T.spi[0:32, :], T.cv[0:32, 0:1])
+    t = lin([t, t_lk, t_dup], T.xd[:], T.lki[:].indirect(T.dup[:]), first, T.spf[:])
+    t_yd = vop([t], "tr", T.yd[:, 0:64], T.xd[:])
     if nl:
-        t = sop([t_lk, t_dup], T.xd[:], T.lki[:, 0:32].indirect(T.dup[:]), AF.Copy)
-        t = vop([t], "tr", T.yd[:], T.xd[:])
-        vop([t], "copy", T.ol[:, 0:32:2], T.yd[:, 0:16])
-        t_ol = vop([], "copy", T.ol[:, 1:32:2], T.yd[:, 32:48])
-    t = sop([t_sp], T.spf[:], T.lki[:, 32:33], AF.Copy)
-    t = sop([t, t_lk], T.lkf[:], T.lki[:, 0:32], AF.Identity, bias=T.spf[:])
-    t_at = vop([t], "tr", T.at[:], T.lkf[:])
-    t_xa = sop([t_at, t_xe], T.xa[:], T.at[:].indirect(T.xe[:]), AF.Copy)
-    if nl:
+        t_ol = vop([t_yd], "copy", T.ol[:], T.yd[:, 0:64].indirect(T.osel[:, 0:1]))
         t_tab = vop([t_ol, t_one], "copy", T.tab[:].indirect(T.ol[:]), T.ones[:])
-    need("v", [t_at])
+    t = lin([t_yd, t_as], T.at[:], T.yd[:, 0:64].indirect(T.asel[:, 0:1]), 1.0, 0.5)
+    need("s", [t, t_r4])
     for j in range(N - 1):
-        t = vop([], "ts", T.r4[0:32, j:64:4], T.at[0:32, 0:16], T.at[0:32, 16 + j:17 + j], float(SL * (j + 1)), OP.is_ge, OP.mult)
-    t_fa = vop([t_xa], "tr", T.fa[:], T.xa[:])
-    t_rr = vop([t], "scan", T.rr[0:32, :], T.r4[0:32, 0:64:2], T.r4[0:32, 1:64:2], 0.0, OP.max, OP.max)
+        t = sop([], T.sg[0:32, 16 * j:16 * j + 16], T.at[0:32, :], AF.Sign, bias=T.yd[0:32, 16 + j:17 + j], scale=-1.0)
+    t_m = sop([], m64, p15, AF.Relu, bias=64.0, scale=-64.0)
+    lin([], aq, q4, 1.0, second)
+    t2 = lin([], p15n, p15, -16.0)
+    need("s", [t])
+    for j in range(N - 1):
+        t_r = lin([], T.r4[0:32, j:64:4], T.sg[0:32, 16 * j:16 * j + 16], -SL * (j + 1) / 2.0, SL * (j + 1) / 2.0)
     rr = T.rr[0:32, 1:32:2]
-    t_vk = vop([t_fa, t_cj], "tt", T.vk[:], T.fa[:].indirect(T.sel[:, 0:4]), T.cj[:], OP.min)
-    if r:
-        t_c = late_constants()
+    t = lin([t2], u64, m64, 1.0, aq)
+    t2 = lin([t_z1], T.yd[:, 64:128], T.i_yc[:], 1.0, p15n)
+    t = lin([t], T.xe[:], T.i_xe[:], 1.0, u64)
+    t_xa = sop([t, t2], T.xa[:], T.yd[:].indirect(T.xe[:]), AF.Copy)
 
     fl = T.fl[0:32, :]
+
+    def ranges():
+        return vop([t_r], "scan", T.rr[0:32, :], T.r4[0:32, 0:64:2], T.r4[0:32, 1:64:2], 0.0, OP.max, OP.max)
     if nl == 0:
+        ranges()
         t_f = vop([], "set", fl, 1.0)
     else:
-        total["kin"] = KE * nl
         t = t_tab
         for a in range(nl):
-            t = vop([t, ("kin", KE * nl)], "copy", T.tab[:].indirect(T.kb[:, 4 * a:4 * a + 4]), T.zt[:, 0:64])
-        t2 = sop([t], T.hit[:, GV:C], T.tab[:].indirect(T.ol[:, GV // 16:C // 16]), AF.Copy)
+            kin = "kin%d" % (r + 1 + a)
+            total[kin] = KE
+            t = vop([t, (kin, KE), t_z1], "copy", T.tab[:].indirect(T.kb[:, 8 * a:8 * a + 8]), T.zt[:, 0:128])
+        t2 = sop([t], T.hit[:, GV:C // 2], T.tab[:].indirect(T.ol[:, GV // 16:16]), AF.Copy)
         t = vop([t], "copy", T.hit[:, 0:GV], T.tab[:].indirect(T.ol[:, 0:GV // 16]))
+        ranges()
         t = vop([t, t2], "tr", T.hitt[:], T.hit[:])
-        t = vop([t], "tt", T.h2[:], T.hitt[:, 0:C:32], T.hitt[:, 16:C:32], OP.min)
-        t = vop([t], "tt", T.h4[0:64, :], T.h2[0:64, :], T.h2[64:128, :], OP.min)
+        need("v", [t])
+        for h in range(2):
+            t = vop([], "tt", T.h4[0:64, 8 * h:8 * h + 8], T.hitt[0:64, 16 * h:C // 2:32], T.hitt[64:128, 16 * h:C // 2:32], OP.min)
         t_f = vop([t], "tt", fl, T.h4[0:32, :], T.h4[32:64, :], OP.min)
 
+    t_dm = lin([t_i16], T.dmp[:], T.i_16[:], 1.0, p15)
     t_e = sop([t_f], T.e1[0:32, :], fl, AF.Copy, scale=float(2 * NS))
-    vop([t_f, t_rr], "scan", T.zq[0:32, 0:16], rr, fl, 0.0, OP.max, OP.add)
+    vop([t_f, t_zs], "scan", T.zq[0:32, 0:16], rr, fl, 0.0, OP.max, OP.add)
     t = vop([], "scan", T.zq[0:32, 32:48], T.zq[0:32, 16:32], fl, 0.0, OP.add, OP.add)
     t = vop([t], "tr", T.zqt[0:32, :], T.zq[0:32, :])
+    t_vk = vop([t_xa], "tr", T.vk[:], T.xa[:])
     t = vop([t], "scan", T.st[0:32, 1:33], T.zqt[0:32, 32:64], T.zqt[0:32, 0:32], 0.0, OP.add, OP.max)
     t2 = vop([t_e], "tt", T.e2[0:32, :], T.dmp[0:32, :], T.e1[0:32, :], OP.subtract)
     t = vop([t], "tr", T.bt[0:32, :], T.st[0:32, 0:32])
     t = vop([t], "scan", T.qq[0:32, :], rr, fl, T.bt[0:32, 15:16], OP.max, OP.add)
-    t = vop([t, t2], "tt", T.o2[0:32, :], T.qq[0:32, :], T.e2[0:32, :], OP.max)
-    need("v", [t])
-    for b in range(4):
-        t = vop([], "copy", T.off[quad(b), :], T.o2[0:32, 4 * b:4 * b + 4])
+    t_o = vop([t, t2], "tt", T.o2[0:32, :], T.qq[0:32, :], T.e2[0:32, :], OP.max)
+    t_sb = lin([t_m], sb, m64, -8192.0, p16)
+    lin([], p31q, p31, 1.0, 0.25)
+    lin([], T.sc3[:, 0:1], p15, 0.0, R0)
+    sop([t_rot], T.rot[:], T.rot2[:], AF.Copy)
+    t2 = sop([t_o], T.off[quad(3), :], T.o2[0:32, 12:16], AF.Copy)
+    for b in range(3):
+        t = vop([t_o], "copy", T.off[quad(b), :], T.o2[0:32, 4 * b:4 * b + 4])
+    t_sb = lin([t_sb], sb2, q8, 32.0, sb)
+    lin([t_iv], T.exp3[:], T.i_exp[:], 1.0, q8)
+    lin([], T.sel[:], T.i_sel[:], 1.0, p31)
+    t_c = lin([t_sb], T.v3c[:], T.i_v3[:], 1.0, sb2)
 
-    def groups(tok, turned, n, two, four, out, op):
-        vop([tok], "tt", two[:, 0:n], turned[:, 1:32 * n:32], turned[:, 17:32 * n:32], op)
-        t = vop([], "tt", two[:, n:2 * n], turned[:, 0:32 * n:32], turned[:, 16:32 * n:32], op)
+    def groups(tok, turned, n, rows, two, four, out, op):
+        need("v", [tok])
+        for i, row in enumerate(rows):
+            t = vop([], "tt", two[:, n * i:n * (i + 1)], turned[:, row:32 * n:32], turned[:, 16 + row:32 * n:32], op)
         t = vop([t], "tt", four[0:64, :], two[0:64, :], two[64:128, :], op)
         need("v", [t])
         for b in range(4):
             t = vop([], "tt", out[quad(b), 0:2 * n], four[0:32, :], four[32:64, :], op)
         return t
 
-    def lists(tok, n, s1, s2, s3, out, *conv):
+    def lists(tok, n, s1, s2, s3, out, scale, shift):
         t = vop([tok], "copy", s2[:], s1[:, 0:32].indirect(T.dup[:]))
         t = vop([t], "tr", s3[:], s2[:])
-        vop([t], "ts", out[:, 0:2 * n:2], s3[:, 0:n], *conv)
-        return vop([], "ts", out[:, 1:2 * n:2], s3[:, 32:32 + n], *conv)
+        return [vop([t], "ts", out[:, 0:2 * n:2], s3[:, 0:n], scale, shift, OP.mult, OP.add), lin([t], out[:, 1:2 * n:2], s3[:, 32:32 + n], scale, shift)]
 
     NZ = N * NB
-    t = vop([t, t_vk, t_wk], "copy", T.wk[:].indirect(T.off[:]), T.vk[:])
+    t = vop([t, t2, t_vk, t_wk], "copy", T.wk[:].indirect(T.off[:]), T.vk[:])
     t = vop([t], "tr", T.tk[:], T.wk[:, 1:NS + 1])
-    t_zz = groups(t, T.tk, NZ, T.z2, T.z4, T.zz, OP.min)
+    t_zz = groups(t, T.tk, NZ, (0, 1), T.z2, T.z4, T.zz, OP.min)
     need("g", [t_zz])
-    send(others, "slk", lambda d: T.zz[:, NZ + NB * d:NZ + NB * d + 8], lambda d: T.ap[:, 8 * r:8 * r + 8], True)
-    t_own = sop([t_zz], T.ap[:, 8 * r:8 * r + 8], T.zz[:, NZ + NB * r:NZ + NB * r + 8], AF.Copy)
+    send(others, "slk", lambda d: T.zz[:, NZ + NB * d:NZ + NB * d + 8], lambda d: T.ap[:, 8 * r:8 * r + 8], short)
+    t_own = sop([t_zz, t_wk], T.ap[:, 8 * r:8 * r + 8], T.zz[:, NZ + NB * r:NZ + NB * r + 8], AF.Copy)
     t = vop([t_zz], "tr", T.sw1[:], T.zz[:, 0:32])
-    t_lj = lists(t, NZ, T.sw1, T.sw2, T.sw3, T.lj, float(2 * C), float(C - 1), OP.add, OP.min)
+    t_lj = lists(t, NZ, T.sw1, T.sw2, T.sw3, T.lj, -1.0, 0.0)
 
     def pick(d, oc, osc):
         L = T.lj[:, 2 * NB * d:2 * NB * d + CAPP // 16]
-        return (vop([t_lj, t_k], "copy", oc.bitcast(dt.uint32), T.kcs[:].bitcast(dt.uint32).indirect(L)),
-                sop([t_lj, t_k], osc, T.kss[:].indirect(L), AF.Copy))
+        return (vop(t_lj + [t_k], "copy", oc.bitcast(dt.uint32), T.kcs[:].bitcast(dt.uint32).indirect(L)),
+                sop(t_lj + [t_k], osc, T.kss[:].indirect(L), AF.Copy))
     for d in far + near:
         t_pv, t_ps = pick(d, T["pc%d" % d][:], T["ps%d" % d][:])
     w0 = LW * (r + 1)
     need("g", [t_pv])
-    send(far + near, "colc", lambda d: T["pc%d" % d][:].bitcast(dt.uint8), lambda d: T.fw[:, w0:w0 + CAPP].bitcast(dt.uint8), False)
+    send(far + near, "colc", lambda d: T["pc%d" % d][:].bitcast(dt.uint8), lambda d: T.fw[:, w0:w0 + CAPP].bitcast(dt.uint8), eng.get)
     need("g", [t_ps])
-    send(far + near, "cols", lambda d: T["ps%d" % d][:], lambda d: T.fsc[:, w0:w0 + CAPP], False)
-    if r == 0:
-        t_c = late_constants()
+    send(far + near, "cols", lambda d: T["ps%d" % d][:], lambda d: T.fsc[:, w0:w0 + CAPP], eng.get)
 
     tk = {}
 
     def own():
         tk["v"], tk["s"] = pick(r, T.fw[:, w0:w0 + CAPP], T.fsc[:, w0:w0 + CAPP])
+        vop([t_wo], "q", T.fw[:, 0:128], T.fsc[:, 0:128], T.zt[:])
         tk["w"] = vop([t_w], "q", T.wq[:], T.wsc[:], T.wt[:])
     if r:
         own()
@@ -277,24 +291,24 @@ def rank_program(g, core, T, topo):
     total["slk"] = KE * (N - 1)
     total["colc"] = total["cols"] = sum(len(eng[d]) for d in others)
     t_in = [("slk", total["slk"]), t_own, t_c]
-    H = SL // 2
-    t2 = sop(t_in, T.x3[:, H:SL], T.ap[:].indirect(T.exp3[:, NB:2 * NB]), AF.Copy)
-    t = vop(t_in, "copy", T.x3[:, 0:H], T.ap[:].indirect(T.exp3[:, 0:NB]))
-    t_ax = vop([], "copy", T.apx[:], T.ap[:].indirect(T.rot[:]))
+    H = SL // 2 if r else SL
+    t2 = sop(t_in, T.x3[:, H:SL], T.ap[:].indirect(T.exp3[:, H // 16:SL // 16]), AF.Copy) if r else None
+    t_ax = sop(t_in, T.apx[:], T.ap[:].indirect(T.rot[:]), AF.Copy)
+    t = vop(t_in, "copy", T.x3[:, 0:H], T.ap[:].indirect(T.exp3[:, 0:H // 16]))
     t_b3 = vop([t, t2], "tr", T.b3[:], T.x3[:])
+    t_em = sop([t_ax], T.em[:], T.apx[:, 0:NB], AF.Relu, bias=float(2 * S - EMPTY))
 
     def scal(c):
         a = 8 * (1 + c // NB) + c % NB
         return T.apx[:, a:a + 1]
     for c in range(A3):
-        t_s = sop([t_b3, t_ax], T.j3[:, CAPP * c:CAPP * (c + 1)], T.b3[:, 0:CAPP], AF.Sign, bias=scal(c), scale=-1.0, accum_out=T.rc[:, NB + c:NB + c + 1])
+        t_s = sop([t_b3], T.j3[:, CAPP * c:CAPP * (c + 1)], T.b3[:, 0:CAPP], AF.Sign, bias=scal(c), scale=-1.0, accum_out=T.rc[:, NB + c:NB + c + 1])
     t = vop([t_b3], "copy", T.b3u[:], T.b3[:, 0:CAPP])
-    t_em = vop([t_ax], "ts", T.em[:], T.apx[:, 0:NB], float(2 * S - EMPTY), 0.0, OP.add, OP.max)
-    need("v", [t])
+    need("v", [t, t_ax])
     for x in range(M3):
         t = vop([], "ts", T.cmp3[:, CAPP * x:CAPP * (x + 1)], T.b3u[:], scal(A3 + x), 2.0, OP.is_lt, OP.mult)
     H = CAPP // 2
-    vop([t_em], "tt", T.rc[:, 0:NB], T.em[:], T.oc6[:], OP.add)
+    vop([t_em, t_wo], "tt", T.rc[:, 0:NB], T.em[:], T.oc6[:], OP.add)
     t = vop([t], "scan", T.sc3[:, 1:M3 * H + 1], T.cmp3[:, 0:M3 * CAPP:2], T.cmp3[:, 1:M3 * CAPP:2], R0, OP.add, OP.add)
     t_v3 = vop([], "tt", T.v3[:], T.b3[:].indirect(T.sel[:]), T.v3c[:], OP.max)
     t = vop([t], "tt", T.rc[:, NB + A3:4 * NB], T.sc3[:, H:M3 * H + 1:H], T.sc3[:, 0:(M3 - 1) * H + 1:H], OP.subtract)
@@ -312,32 +326,39 @@ def rank_program(g, core, T, topo):
     for s in range(N):
         k = (s - 1) % N
         t = vop([], "tt", T.p3[quad(s), :], T.u3[0:32, NB * s:NB * (s + 1)], T.u3[32:64, NB * k:NB * (k + 1)], OP.add)
-    t = vop([t], "ts", T.off3[:], T.p3[:], 0.5, 0.25, OP.mult, OP.add)
-    t = vop([t, t_v3, t_wo], "copy", T.wo[:].indirect(T.off3[:]), T.v3[:])
+    t = vop([t], "ts", T.off3[:], T.p3[:], 0.5, p31q, OP.mult, OP.add)
+    t = vop([t, t_v3], "copy", T.wo[:].indirect(T.off3[:]), T.v3[:])
     t = vop([t], "tr", T.to[:], T.wo[:, 0:S])
     NO = S // 32
-    t = groups(t, T.to, NO, T.y2, T.y4, T.zo, OP.max)
+    t = groups(t, T.to, NO, (1, 0), T.y2, T.y4, T.zo, OP.max)
     t_so = vop([t], "tr", T.so1[:], T.zo[:])
-    t_lf = lists(t_so, NO, T.so1, T.so2, T.so3, T.lf, float(KEYS), None, OP.subtract)
+    t = lin([t_so], T.rki[0:32, :], T.so1[0:32, 0:32], 1.0 / LW, -(KEYS / LW + 0.35))
+    t_rk = lin([t], T.rkf[0:32, :], T.rki[0:32, :], 1.0, -1.0)
+    t_lf = lists(t_so, NO, T.so1, T.so2, T.so3, T.lf, 1.0, -float(KEYS))
     n1 = 32 - NO
     dma("y", [t_so], T.ok[0:1, 0:32 * n1], T.so1[NO:32, 0:32], "st1")
     dma("y", [], T.ok[0:1, 32 * n1:S], T.so1[0:NO - n1, 32:64], "st1")
+    dma("y", [t_rk], T.ok[1:2, :], T.rkf[0:NO, :], "st1")
 
     def at(lo, hi):
         return T.lf[:, lo // 16:hi // 16]
-    lo = ly = 0
-    for n, m in zip(CHC, CHY):
-        t = vop([t_lf, ("colc", total["colc"]), tk["v"], t_zq], "copy", T.oq[:, lo:lo + n].bitcast(dt.uint32), T.fw[:].bitcast(dt.uint32).indirect(at(lo, lo + n)))
-        t2 = sop([t_y, t_lf], T.ys[:, ly:ly + m], T.yw[:].indirect(at(ly, ly + m)), AF.Copy)
-        dma("y", [t], T.oc[:, 4 * lo:4 * (lo + n)], T.oq[:, lo:lo + n].bitcast(dt.uint8), "st1")
-        dma("y", [t2], T.y[:, ly:ly + m], T.ys[:, ly:ly + m], "st1")
-        lo, ly = lo + n, ly + m
-    H = S // 2
-    t2 = sop([("cols", total["cols"]), tk["s"], t_zq], T.os_[:, H:S], T.fsc[:].indirect(at(H, S)), AF.Copy)
-    t = vop([("cols", total["cols"]), tk["s"]], "copy", T.os_[:, 0:H], T.fsc[:].indirect(at(0, H)))
-    t3 = vop([], "ts", T.rki[0:32, :], T.so1[0:32, 0:32], 1.0 / LW, -(KEYS / LW + 1.35), OP.mult, OP.add)
-    t3 = vop([t3], "ts", T.rkf[0:32, :], T.rki[0:32, :], -1.0, None, OP.max)
-    for i in range(4):
-        dma("ys"[i % 2], [t, t2], T.osc[4 * i:4 * i + 4, :], T.os_[32 * i:32 * i + 4, :], "st1")
-    dma("y", [t3], T.ok[1:2, :], T.rkf[0:NO, :], "st1")
+
+    def codes(lo, hi):
+        t = vop(t_lf + [("colc", total["colc"]), tk["v"], tk["w"]], "copy", T.oq[:, lo:hi].bitcast(dt.uint32), T.fw[:].bitcast(dt.uint32).indirect(at(lo, hi)))
+        dma("y", [t], T.oc[:, 4 * lo:4 * hi], T.oq[:, lo:hi].bitcast(dt.uint8), "st1")
+
+    def products(lo, hi):
+        t = sop(t_lf + [t_y], T.ys[:, lo:hi], T.yw[:].indirect(at(lo, hi)), AF.Copy)
+        dma("y", [t], T.y[:, lo:hi], T.ys[:, lo:hi], "st1")
+
+    def scales():
+        t2 = sop([("cols", total["cols"]), tk["s"], tk["w"]], T.os_[:, SV:S], T.fsc[:].indirect(at(SV, S)), AF.Copy)
+        t = vop([("cols", total["cols"]), tk["s"]], "copy", T.os_[:, 0:SV], T.fsc[:].indirect(at(0, SV)))
+        for i in range(4):
+            dma("ys"[i % 2], [t, t2], T.osc[4 * i:4 * i + 4, :], T.os_[32 * i:32 * i + 4, :], "st1")
+    for step in TAIL:
+        if step[0] == "s":
+            scales()
+        else:
+            (codes if step[0] == "c" else products)(step[1], step[2])
     need("g", list(total.items()))

@@ -10,9 +10,7 @@ LW = 256
 EMPTY = 2 * KEYS
 GAP = 576
 GV = 128
-A3 = 9
-M3 = 3 * NB - A3
-R0 = -float(M3 * CAPP)
+SIGNS = (8, 6, 6, 6)
 TAIL = [("c", 0, 192), ("y", 0, 192), ("c", 192, 640), ("y", 192, 640), ("s",)]
 SV = 320
 
@@ -24,26 +22,26 @@ def _s(n, d="float32"):
 X4, U8, U16, BF, I32, F16 = "float8_e4m3fn_x4", "uint8", "uint16", "bfloat16", "int32", "float16"
 SCRATCH = {
     "lki": _s(32, I32), "spi": _s(1, I32), "klu": _s(8, U16), "wt": _s(512, BF), "wq": _s(128, X4), "wsc": _s(128, U8), "kcs": _s(C, X4), "kss": _s(C, U8),
-    "pidx": _s(1, I32), "pm": _s(7, I32), "pf": _s(7), "cv": _s(2), "cs": _s(8),
-    "i_dup": _s(4), "dup": _s(4, U16), "osel": _s(2, U16), "asel": _s(2, U16), "i_xe": _s(4), "xe": _s(4, U16), "i_yc": _s(64),
+    "pidx": _s(2, I32), "pm": _s(8, I32), "pf": _s(8), "cs": _s(8),
+    "i_dup": _s(4), "dup": _s(4, U16), "osel": _s(2, U16), "asel": _s(2, U16), "i_xe": _s(8), "xe": _s(8, U16), "i_yc": _s(64),
     "i_sel": _s(NB), "sel": _s(NB, U16), "i_exp": _s(2 * NB), "exp3": _s(2 * NB, U16),
     "i_16": _s(16), "rot1": _s(2, I32), "rot2": _s(2, I32), "rot": _s(2, U16), "dmp": _s(16),
-    "i_v3": _s(96), "v3c": _s(96), "oc6": _s(NB), "ones": _s(C // 2, BF), "zt": _s(C, BF),
-    "spf": _s(1), "xd": _s(64), "yd": _s(128), "ol": _s(16, U16), "at": _s(16), "sg": _s(48), "r4": _s(64), "rr": _s(32), "xa": _s(64), "vk": _s(64),
+    "i_v3": _s(96), "v3c": _s(96), "i_oc": _s(NB), "oc6": _s(NB), "ones": _s(C // 2, BF), "zt": _s(C, BF),
+    "spf": _s(1), "xd": _s(64), "yd": _s(128), "ol": _s(16, U16), "at": _s(16), "sg": _s(48), "r4": _s(64), "rr": _s(32), "xa": _s(128), "vk": _s(128),
     "kb": _s(24, U16), "tab": _s(KEYS, BF), "hit": _s(C // 2, BF), "hitt": _s(C // 2, BF), "h4": _s(16), "fl": _s(16),
-    "zq": _s(64), "zqt": _s(64), "st": _s(64), "bt": _s(32), "qq": _s(16), "e1": _s(16), "e2": _s(16), "o2": _s(16), "off": _s(4, U16),
-    "wk": _s(NS + 264), "tk": _s(NS), "z2": _s(48), "z4": _s(48), "zz": _s(56),
-    "sw1": _s(32), "sw2": _s(64), "sw3": _s(64), "lj": _s(48, U16),
+    "zq": _s(64), "zqt": _s(64), "st": _s(64), "bt": _s(32), "qq": _s(16), "e1": _s(16), "e2": _s(16), "off": _s(8, U16),
+    "wk": _s(NS + 264), "tk": _s(NS), "z2": _s(48), "zz": _s(56),
+    "sw1": _s(32), "sw2": _s(64, U16), "lj": _s(64, U16),
     "pc0": _s(CAPP, X4), "pc1": _s(CAPP, X4), "pc2": _s(CAPP, X4), "pc3": _s(CAPP, X4),
     "ps0": _s(CAPP, U8), "ps1": _s(CAPP, U8), "ps2": _s(CAPP, U8), "ps3": _s(CAPP, U8),
-    "ap": _s(32), "apx": _s(32), "x3": _s(SL), "b3": _s(SL), "b3u": _s(CAPP, U16), "cmp3": _s(M3 * CAPP, F16), "sc3": _s(M3 * CAPP // 2 + 1, F16),
-    "j3": _s(A3 * CAPP, BF), "em": _s(NB), "rc": _s(4 * NB), "u3": _s(4 * NB), "p3": _s(NB), "off3": _s(NB, U16), "v3": _s(96),
-    "wo": _s(S + NB * (GAP + 64)), "to": _s(S), "y2": _s(40), "y4": _s(40), "zo": _s(64), "so1": _s(64), "so2": _s(64), "so3": _s(64), "lf": _s(S // 16, U16),
+    "ap": _s(32), "apx": _s(32), "x3": _s(SL, U16), "b3": _s(SL, U16), "b3f": _s(SL), "cmp3": _s((3 * NB - min(SIGNS)) * CAPP, F16),
+    "sc3": _s((3 * NB - min(SIGNS)) * CAPP // 2 + 1, F16), "j3": _s(max(SIGNS) * CAPP, BF), "em": _s(NB), "rc": _s(4 * NB), "u3": _s(4 * NB), "p3": _s(NB), "off3": _s(NB, U16), "v3": _s(96),
+    "wo": _s(2 * (S + NB * (GAP + 64))), "to": _s(S), "y2": _s(40), "y4": _s(40), "zo": _s(64), "so1": _s(64), "so2": _s(64, U16), "lf": _s(64, U16),
     "rki": _s(32, U16), "rkf": _s(32),
     "fw": _s(LW * (N + 1), X4), "fsc": _s(LW * (N + 1), U8), "oq": _s(S, X4), "os_": _s(S, U8),
     "yw": _s(LW * (N + 1)), "ys": _s(S), "pz": ("psum", [128, 512 * N], "float32"),
 }
-SEMAPHORES = ["v", "s", "t", "gi", "dlk", "dsp", "dw", "dk", "kin1", "kin2", "kin3", "slk", "colc", "cols", "ksent", "lsent", "st1"]
+SEMAPHORES = ["v", "s", "t", "gi", "dlk", "dl2", "dsp", "dw", "dk", "kin1", "kin2", "kin3", "slk", "colc", "cols", "ksent", "lsent", "st1"]
 
 
 def rank_program(g, core, T, topo):
@@ -118,48 +116,62 @@ def rank_program(g, core, T, topo):
 
     low = [d for d in others if d < r]
     nl = N - 1 - r
+    A3 = SIGNS[r]
+    M3 = 3 * NB - A3
+    R0 = -float(M3 * CAPP)
 
     for a in range(2):
+        t_lk = dma("ys"[a], [], T.lki[16 * a:16 * a + 16, :], T.ky[:], "dlk")
+    for a in range(2, 4):
+        t_l2 = dma("ys"[a % 2], [], T.lki[16 * a:16 * a + 16, :], T.ky[:], "dl2")
+    for a in range(2):
         t_sp = dma("ys"[a], [], T.spi[16 * a:16 * a + 16, :], T.sp[:], "dsp")
-    for a in range(8):
-        t_lk = dma("ys"[a % 2], [], T.lki[16 * a:16 * a + 16, :], T.ky[:], "dlk")
 
-    t_pi = iota(T.pidx[:], [[0, 1]], 0, 1, True)
+    t_pi = iota(T.pidx[:, 0:2], [[16, 2]], 0, 1, True)
     t_id = iota(T.i_dup[:], [[16, 2], [0, 2]], 0)
-    iota(T.i_xe[:], [[2, 2], [32, 2]], 0)
+    iota(T.i_xe[:], [[2, 4], [32, 2]], 0)
     iota(T.i_yc[:], [[-256, 2], [-1, 32]], 0)
     t_r4 = fill(T.r4[:, 3:64:4])
     t_z1 = fill(T.zt[:, 0:128])
 
+    def bits(deps, a, b, src, shift, mask):
+        return vop(deps, "ts", T.pm[:, a:b], src, shift, mask, OP.arith_shift_right, OP.bitwise_and)
+    p15, second, first, p31, h8, q8 = [T.pf[:, i:i + 1] for i in range(6)]
+    m64, aq, u64, p15n, sb, sb2, p62, p16 = [T.cs[:, i:i + 1] for i in range(8)]
     vop([], "set", T.spf[:], 0.0)
-    need("v", [t_pi])
-    for i, (sh, b) in enumerate(((0, 15), (0, 16), (0, 1), (1, 15), (0, 31), (3, 12), (2, 24))):
-        t = vop([], "ts", T.pm[:, i:i + 1], T.pidx[:], sh, b, OP.arith_shift_right, OP.bitwise_and)
-    t_pf = vop([t], "copy", T.pf[:], T.pm[:])
-    p15, p16, p1, ph, p31, q4, q8 = [T.pf[:, i:i + 1] for i in range(7)]
-    second, first = T.cv[:, 0:1], T.cv[:, 1:2]
-    m64, aq, u64, p15n, sb, sb2, p31q = [T.cs[:, i:i + 1] for i in range(7)]
-    t_2 = vop([t_pf], "ts", second, p16, 1.0 / 16, None, OP.mult)
-    vop([], "ts", first, p16, -1.0 / 16, 1.0, OP.mult, OP.add)
-    t_dup = vop([t_id], "ts", T.dup[:], T.i_dup[:], p15, None, OP.add)
+    bits([t_pi], 0, 1, T.pidx[:, 0:1], 0, 15)
+    t = bits([], 1, 3, T.pidx[:, 0:2], 4, 1)
+    bits([], 3, 4, T.pidx[:, 0:1], 0, 31)
+    t_2 = vop([t], "copy", T.pf[:, 0:3], T.pm[:, 0:3])
+    bits([], 4, 5, T.pidx[:, 0:1], 3, 8)
+    t_dup = vop([t_2, t_id], "ts", T.dup[:], T.i_dup[:], p15, None, OP.add)
+    t = bits([], 5, 6, T.pidx[:, 0:1], 2, 24)
     if nl:
-        vop([], "ts", T.osel[:, 0:1], p1, 32.0, ph, OP.mult, OP.add)
-        t_one = vop([], "set", T.ones[:], 1.0)
-    t_as = lin([t_pf], T.asel[:, 0:1], p16, 2.0, p15)
+        bits([], 6, 7, T.pidx[:, 0:1], 0, 1)
+        t = bits([], 7, 8, T.pidx[:, 0:1], 1, 15)
+    n = 8 if nl else 6
+    need("v", [t])
+    t_as = lin([t_2], T.asel[:, 0:1], second, 32.0, p15)
+    t_sf = lin([t_sp], T.spf[0:32, :], T.spi[0:32, :], T.pf[0:32, 1:2])
 
     t_ks = None
     if low:
-        for b in range(2):
-            t = vop([t_lk], "copy", T.klu[quad(b), :], T.lki[quad(b), 8 * b:8 * b + 8])
-            t2 = sop([t_lk], T.klu[quad(b + 2), :], T.lki[quad(b + 2), 8 * b + 16:8 * b + 24], AF.Copy)
-        need("g", [t, t2])
+        for b in range(3):
+            t = vop([t_lk], "copy", T.klu[quad(b), :], T.lki[0:32, 8 * b:8 * b + 8])
+        need("g", [t, sop([t_lk], T.klu[quad(3), :], T.lki[0:32, 24:32], AF.Copy)])
         t_ks = send(low, "kin%d" % r, lambda d: T.klu[:], lambda d: T.kb[:, 8 * (r - d - 1):8 * (r - d)], short, "ksent")
-    dma("y", [t_ks, t_lk], T.kcs[:].bitcast(dt.uint8), T.kc[:], "dk")
+    t_w = dma("y", [t_ks, t_lk], T.wt[:], T.w[:], "dw")
+    dma("y", [], T.kcs[:].bitcast(dt.uint8), T.kc[:], "dk")
     t_k = dma("y", [], T.kss[:], T.ks[:], "dk")
-    t_w = dma("y", [], T.wt[:], T.w[:], "dw")
-    t = vop([], "ts", T.rot1[:], T.i_dup[:, 0:4:2], p15, q8, OP.add, OP.add)
-    t_rot = vop([t], "ts", T.rot2[:], T.rot1[:], 31, None, OP.bitwise_and)
+    t_l4 = vop([t_lk, t_l2], "copy", T.lki[64:128, :], T.lki[0:64, :])
+    t_pf = vop([], "copy", T.pf[:, 3:n], T.pm[:, 3:n])
+    if nl:
+        t_one = vop([], "set", T.ones[:], 1.0)
+        vop([t_pf], "ts", T.osel[:, 0:1], T.pf[:, 6:7], 32.0, T.pf[:, 7:8], OP.mult, OP.add)
+    t_rot = vop([t_pf], "ts", T.rot1[:], T.i_dup[:, 0:4:2], p15, q8, OP.add, OP.add)
 
+    if r == 0:
+        t_zt = fill(T.zt[:, 128:C])
     t_i16 = iota(T.i_16[:], [[16, 16]], NS + 1)
     fill(T.zq[:, 16:64])
     t_zs = fill(T.st[:, 0:1])
@@ -168,44 +180,55 @@ def rank_program(g, core, T, topo):
     iota(T.i_exp[:], [[1, NB], [0, 2]], 0)
     iota(T.i_sel[:], [[32, NB]], 0)
     t_iv = iota(T.i_v3[:], [[32, NB], [1, 16]], KEYS + LW)
-    iota(T.oc6[:, 0:A3 - NB], [[64, A3 - NB]], 2 * CAPP)
-    iota(T.oc6[:, A3 - NB:NB], [[64, 2 * NB - A3]], CAPP + 64 * (A3 - NB))
+    for a, b, n in ((0, A3 % NB, A3 // NB + 1), (A3 % NB, NB, A3 // NB)):
+        if a < b:
+            t_oc = iota(T.i_oc[:, a:b], [[64, b - a]], n * CAPP + 64 * a)
     fill(T.zo[:, 40:64])
     fill(T.yw[:, 0:8])
-    fill(T.zt[:, 128:C])
-    t_wo = fill(T.wo[:, 0:S], -1)
+    if r:
+        t_zt = fill(T.zt[:, 128:C])
+    t_wo = fill(T.wo[:, 0:2 * S:2], -1)
 
-    t = lin([t_sp, t_2], T.spf[0:32, :], T.spi[0:32, :], T.cv[0:32, 0:1])
-    t = lin([t, t_lk, t_dup], T.xd[:], T.lki[:].indirect(T.dup[:]), first, T.spf[:])
+    t = lin([t_sf, t_l4, t_dup], T.xd[:], T.lki[:].indirect(T.dup[:]), first, T.spf[:])
     t_yd = vop([t], "tr", T.yd[:, 0:64], T.xd[:])
     if nl:
         t_ol = vop([t_yd], "copy", T.ol[:], T.yd[:, 0:64].indirect(T.osel[:, 0:1]))
         t_tab = vop([t_ol, t_one], "copy", T.tab[:].indirect(T.ol[:]), T.ones[:])
+    tk = {}
+
+    def zeros():
+        vop([t_zt], "q", T.fw[:, 0:128], T.fsc[:, 0:128], T.zt[:])
+    if r == 0:
+        zeros()
     t = lin([t_yd, t_as], T.at[:], T.yd[:, 0:64].indirect(T.asel[:, 0:1]), 1.0, 0.5)
     need("s", [t, t_r4])
     for j in range(N - 1):
         t = sop([], T.sg[0:32, 16 * j:16 * j + 16], T.at[0:32, :], AF.Sign, bias=T.yd[0:32, 16 + j:17 + j], scale=-1.0)
     t_m = sop([], m64, p15, AF.Relu, bias=64.0, scale=-64.0)
-    lin([], aq, q4, 1.0, second)
+    lin([t_pf], aq, h8, 1.0, second)
     t2 = lin([], p15n, p15, -16.0)
     need("s", [t])
     for j in range(N - 1):
         t_r = lin([], T.r4[0:32, j:64:4], T.sg[0:32, 16 * j:16 * j + 16], -SL * (j + 1) / 2.0, SL * (j + 1) / 2.0)
-    rr = T.rr[0:32, 1:32:2]
+    rr = T.rr[0:64, 1:32:2]
     t = lin([t2], u64, m64, 1.0, aq)
     t2 = lin([t_z1], T.yd[:, 64:128], T.i_yc[:], 1.0, p15n)
     t = lin([t], T.xe[:], T.i_xe[:], 1.0, u64)
+    t_16 = lin([], p16, second, 16.0)
     t_xa = sop([t, t2], T.xa[:], T.yd[:].indirect(T.xe[:]), AF.Copy)
 
-    fl = T.fl[0:32, :]
+    fl = T.fl[0:64, :]
 
     def ranges():
-        return vop([t_r], "scan", T.rr[0:32, :], T.r4[0:32, 0:64:2], T.r4[0:32, 1:64:2], 0.0, OP.max, OP.max)
+        for b in range(2):
+            vop([t_r], "scan", T.rr[quad(b), :], T.r4[0:32, 0:64:2], T.r4[0:32, 1:64:2], 0.0, OP.max, OP.max)
     if nl == 0:
+        t_rot = vop([t_rot], "ts", T.rot2[:], T.rot1[:], 31, None, OP.bitwise_and)
         ranges()
         t_f = vop([], "set", fl, 1.0)
     else:
         t = t_tab
+        t_rot = vop([t_rot], "ts", T.rot2[:], T.rot1[:], 31, None, OP.bitwise_and)
         for a in range(nl):
             kin = "kin%d" % (r + 1 + a)
             total[kin] = KE
@@ -217,55 +240,55 @@ def rank_program(g, core, T, topo):
         need("v", [t])
         for h in range(2):
             t = vop([], "tt", T.h4[0:64, 8 * h:8 * h + 8], T.hitt[0:64, 16 * h:C // 2:32], T.hitt[64:128, 16 * h:C // 2:32], OP.min)
-        t_f = vop([t], "tt", fl, T.h4[0:32, :], T.h4[32:64, :], OP.min)
+        need("v", [t])
+        for b in range(2):
+            t_f = vop([], "tt", T.fl[quad(b), :], T.h4[0:32, :], T.h4[32:64, :], OP.min)
 
     t_dm = lin([t_i16], T.dmp[:], T.i_16[:], 1.0, p15)
-    t_e = sop([t_f], T.e1[0:32, :], fl, AF.Copy, scale=float(2 * NS))
-    vop([t_f, t_zs], "scan", T.zq[0:32, 0:16], rr, fl, 0.0, OP.max, OP.add)
-    t = vop([], "scan", T.zq[0:32, 32:48], T.zq[0:32, 16:32], fl, 0.0, OP.add, OP.add)
-    t = vop([t], "tr", T.zqt[0:32, :], T.zq[0:32, :])
+    t_e = sop([t_f], T.e1[0:64, :], fl, AF.Copy, scale=float(2 * NS))
+    vop([t_f, t_zs], "scan", T.zq[0:64, 0:16], rr, fl, 0.0, OP.max, OP.add)
+    t = vop([], "scan", T.zq[0:64, 32:48], T.zq[0:64, 16:32], fl, 0.0, OP.add, OP.add)
+    t = vop([t], "tr", T.zqt[0:64, :], T.zq[0:64, :])
+    t = vop([t], "scan", T.st[0:64, 1:33], T.zqt[0:64, 32:64], T.zqt[0:64, 0:32], 0.0, OP.add, OP.max)
+    t2 = vop([t_e], "tt", T.e2[0:64, :], T.dmp[0:64, :], T.e1[0:64, :], OP.subtract)
+    t = vop([t], "tr", T.bt[0:64, :], T.st[0:64, 0:32])
     t_vk = vop([t_xa], "tr", T.vk[:], T.xa[:])
-    t = vop([t], "scan", T.st[0:32, 1:33], T.zqt[0:32, 32:64], T.zqt[0:32, 0:32], 0.0, OP.add, OP.max)
-    t2 = vop([t_e], "tt", T.e2[0:32, :], T.dmp[0:32, :], T.e1[0:32, :], OP.subtract)
-    t = vop([t], "tr", T.bt[0:32, :], T.st[0:32, 0:32])
-    t = vop([t], "scan", T.qq[0:32, :], rr, fl, T.bt[0:32, 15:16], OP.max, OP.add)
-    t_o = vop([t, t2], "tt", T.o2[0:32, :], T.qq[0:32, :], T.e2[0:32, :], OP.max)
-    t_sb = lin([t_m], sb, m64, -8192.0, p16)
-    lin([], p31q, p31, 1.0, 0.25)
+    t = vop([t], "scan", T.qq[0:64, :], rr, fl, T.bt[0:64, 15:16], OP.max, OP.add)
+    need("v", [t, t2])
+    for b in range(2):
+        t = vop([], "tt", T.off[64 * b:64 * b + 64, :], T.qq[0:64, 8 * b:8 * b + 8], T.e2[0:64, 8 * b:8 * b + 8], OP.max)
+    t_sb = lin([t_16], sb, m64, -8192.0, p16)
+    t2 = lin([], p62, p31, 2.0)
     lin([], T.sc3[:, 0:1], p15, 0.0, R0)
     sop([t_rot], T.rot[:], T.rot2[:], AF.Copy)
-    t2 = sop([t_o], T.off[quad(3), :], T.o2[0:32, 12:16], AF.Copy)
-    for b in range(3):
-        t = vop([t_o], "copy", T.off[quad(b), :], T.o2[0:32, 4 * b:4 * b + 4])
     t_sb = lin([t_sb], sb2, q8, 32.0, sb)
+    lin([t2, t_oc], T.oc6[:], T.i_oc[:], 1.0, p62)
     lin([t_iv], T.exp3[:], T.i_exp[:], 1.0, q8)
     lin([], T.sel[:], T.i_sel[:], 1.0, p31)
     t_c = lin([t_sb], T.v3c[:], T.i_v3[:], 1.0, sb2)
 
-    def groups(tok, turned, n, rows, two, four, out, op):
+    def pairs(tok, turned, n, rows, two, op):
         need("v", [tok])
         for i, row in enumerate(rows):
             t = vop([], "tt", two[:, n * i:n * (i + 1)], turned[:, row:32 * n:32], turned[:, 16 + row:32 * n:32], op)
-        t = vop([t], "tt", four[0:64, :], two[0:64, :], two[64:128, :], op)
         need("v", [t])
-        for b in range(4):
-            t = vop([], "tt", out[quad(b), 0:2 * n], four[0:32, :], four[32:64, :], op)
-        return t
 
-    def lists(tok, n, s1, s2, s3, out, scale, shift):
-        t = vop([tok], "copy", s2[:], s1[:, 0:32].indirect(T.dup[:]))
-        t = vop([t], "tr", s3[:], s2[:])
-        return [vop([t], "ts", out[:, 0:2 * n:2], s3[:, 0:n], scale, shift, OP.mult, OP.add), lin([t], out[:, 1:2 * n:2], s3[:, 32:32 + n], scale, shift)]
+    def lists(tok, s1, s2, out, scale, shift):
+        t = vop([tok], "ts", s2[:], s1[:, 0:32].indirect(T.dup[:]), scale, shift, OP.mult, OP.add)
+        vop([t], "tr", out[:, 0:64:2], s2[:, 0:32])
+        return [vop([], "tr", out[:, 1:64:2], s2[:, 32:64])]
 
     NZ = N * NB
-    t = vop([t, t2, t_vk, t_wk], "copy", T.wk[:].indirect(T.off[:]), T.vk[:])
+    t = vop([t, t_vk, t_wk], "copy", T.wk[:].indirect(T.off[:]), T.vk[:])
     t = vop([t], "tr", T.tk[:], T.wk[:, 1:NS + 1])
-    t_zz = groups(t, T.tk, NZ, (0, 1), T.z2, T.z4, T.zz, OP.min)
+    pairs(t, T.tk, NZ, (0, 1), T.z2, OP.min)
+    for b in range(2):
+        t_zz = vop([], "tt", T.zz[64 * b:64 * b + 64, 0:2 * NZ], T.z2[0:64, :], T.z2[64:128, :], OP.min)
     need("g", [t_zz])
     send(others, "slk", lambda d: T.zz[:, NZ + NB * d:NZ + NB * d + 8], lambda d: T.ap[:, 8 * r:8 * r + 8], short)
     t_own = sop([t_zz, t_wk], T.ap[:, 8 * r:8 * r + 8], T.zz[:, NZ + NB * r:NZ + NB * r + 8], AF.Copy)
     t = vop([t_zz], "tr", T.sw1[:], T.zz[:, 0:32])
-    t_lj = lists(t, NZ, T.sw1, T.sw2, T.sw3, T.lj, -1.0, 0.0)
+    t_lj = lists(t, T.sw1, T.sw2, T.lj, -1.0, 0.0)
 
     def pick(d, oc, osc):
         L = T.lj[:, 2 * NB * d:2 * NB * d + CAPP // 16]
@@ -279,11 +302,10 @@ def rank_program(g, core, T, topo):
     need("g", [t_ps])
     send(far + near, "cols", lambda d: T["ps%d" % d][:], lambda d: T.fsc[:, w0:w0 + CAPP], eng.get)
 
-    tk = {}
-
     def own():
         tk["v"], tk["s"] = pick(r, T.fw[:, w0:w0 + CAPP], T.fsc[:, w0:w0 + CAPP])
-        vop([t_wo], "q", T.fw[:, 0:128], T.fsc[:, 0:128], T.zt[:])
+        if r:
+            zeros()
         tk["w"] = vop([t_w], "q", T.wq[:], T.wsc[:], T.wt[:])
     if r:
         own()
@@ -293,24 +315,24 @@ def rank_program(g, core, T, topo):
     t_in = [("slk", total["slk"]), t_own, t_c]
     H = SL // 2 if r else SL
     t2 = sop(t_in, T.x3[:, H:SL], T.ap[:].indirect(T.exp3[:, H // 16:SL // 16]), AF.Copy) if r else None
-    t_ax = sop(t_in, T.apx[:], T.ap[:].indirect(T.rot[:]), AF.Copy)
+    t_ax = lin(t_in, T.apx[:], T.ap[:].indirect(T.rot[:]), 1.0, -0.5)
     t = vop(t_in, "copy", T.x3[:, 0:H], T.ap[:].indirect(T.exp3[:, 0:H // 16]))
     t_b3 = vop([t, t2], "tr", T.b3[:], T.x3[:])
-    t_em = sop([t_ax], T.em[:], T.apx[:, 0:NB], AF.Relu, bias=float(2 * S - EMPTY))
+    t_em = sop([t_ax], T.em[:], T.apx[:, 0:NB], AF.Relu, bias=2 * S - EMPTY + 0.5)
 
     def scal(c):
         a = 8 * (1 + c // NB) + c % NB
         return T.apx[:, a:a + 1]
+    t_bf = sop([t_b3], T.b3f[:], T.b3[:], AF.Copy)
     for c in range(A3):
-        t_s = sop([t_b3], T.j3[:, CAPP * c:CAPP * (c + 1)], T.b3[:, 0:CAPP], AF.Sign, bias=scal(c), scale=-1.0, accum_out=T.rc[:, NB + c:NB + c + 1])
-    t = vop([t_b3], "copy", T.b3u[:], T.b3[:, 0:CAPP])
-    need("v", [t, t_ax])
+        t_s = sop([], T.j3[:, CAPP * c:CAPP * (c + 1)], T.b3[:, 0:CAPP], AF.Sign, bias=scal(c), scale=-1.0, accum_out=T.rc[:, NB + c:NB + c + 1])
+    need("v", [t_b3, t_ax])
     for x in range(M3):
-        t = vop([], "ts", T.cmp3[:, CAPP * x:CAPP * (x + 1)], T.b3u[:], scal(A3 + x), 2.0, OP.is_lt, OP.mult)
+        t = vop([], "ts", T.cmp3[:, CAPP * x:CAPP * (x + 1)], T.b3[:, 0:CAPP], scal(A3 + x), 2.0, OP.is_lt, OP.mult)
     H = CAPP // 2
     vop([t_em, t_wo], "tt", T.rc[:, 0:NB], T.em[:], T.oc6[:], OP.add)
     t = vop([t], "scan", T.sc3[:, 1:M3 * H + 1], T.cmp3[:, 0:M3 * CAPP:2], T.cmp3[:, 1:M3 * CAPP:2], R0, OP.add, OP.add)
-    t_v3 = vop([], "tt", T.v3[:], T.b3[:].indirect(T.sel[:]), T.v3c[:], OP.max)
+    t_v3 = vop([t_bf], "tt", T.v3[:], T.b3f[:].indirect(T.sel[:]), T.v3c[:], OP.max)
     t = vop([t], "tt", T.rc[:, NB + A3:4 * NB], T.sc3[:, H:M3 * H + 1:H], T.sc3[:, 0:(M3 - 1) * H + 1:H], OP.subtract)
     if r == 0:
         own()
@@ -325,16 +347,18 @@ def rank_program(g, core, T, topo):
     need("v", [t])
     for s in range(N):
         k = (s - 1) % N
-        t = vop([], "tt", T.p3[quad(s), :], T.u3[0:32, NB * s:NB * (s + 1)], T.u3[32:64, NB * k:NB * (k + 1)], OP.add)
-    t = vop([t], "ts", T.off3[:], T.p3[:], 0.5, p31q, OP.mult, OP.add)
+        t = vop([], "tt", T.off3[quad(s), :], T.u3[0:32, NB * s:NB * (s + 1)], T.u3[32:64, NB * k:NB * (k + 1)], OP.add)
     t = vop([t, t_v3], "copy", T.wo[:].indirect(T.off3[:]), T.v3[:])
-    t = vop([t], "tr", T.to[:], T.wo[:, 0:S])
+    t = vop([t], "tr", T.to[:], T.wo[:, 0:2 * S:2])
     NO = S // 32
-    t = groups(t, T.to, NO, (1, 0), T.y2, T.y4, T.zo, OP.max)
+    pairs(t, T.to, NO, (1, 0), T.y2, OP.max)
+    need("v", [vop([], "tt", T.y4[0:64, :], T.y2[0:64, :], T.y2[64:128, :], OP.max)])
+    for b in range(4):
+        t = vop([], "tt", T.zo[quad(b), 0:2 * NO], T.y4[0:32, :], T.y4[32:64, :], OP.max)
     t_so = vop([t], "tr", T.so1[:], T.zo[:])
     t = lin([t_so], T.rki[0:32, :], T.so1[0:32, 0:32], 1.0 / LW, -(KEYS / LW + 0.35))
     t_rk = lin([t], T.rkf[0:32, :], T.rki[0:32, :], 1.0, -1.0)
-    t_lf = lists(t_so, NO, T.so1, T.so2, T.so3, T.lf, 1.0, -float(KEYS))
+    t_lf = lists(t_so, T.so1, T.so2, T.lf, 1.0, -float(KEYS))
     n1 = 32 - NO
     dma("y", [t_so], T.ok[0:1, 0:32 * n1], T.so1[NO:32, 0:32], "st1")
     dma("y", [], T.ok[0:1, 32 * n1:S], T.so1[0:NO - n1, 32:64], "st1")

@@ -10,8 +10,8 @@ LW = 256
 EMPTY = 2 * KEYS
 GAP = 576
 GV = 128
-SIGNS = (8, 6, 6, 6)
-TAIL = [("c", 0, 192), ("y", 0, 192), ("c", 192, 640), ("y", 192, 640), ("s",)]
+SIGNS = (9, 8, 8, 8)
+TAIL = [("c", 0, 96), ("y", 0, 96), ("c", 96, 352), ("y", 96, 352), ("c", 352, 640), ("y", 352, 640), ("s",)]
 SV = 320
 
 
@@ -21,27 +21,27 @@ def _s(n, d="float32"):
 
 X4, U8, U16, BF, I32, F16 = "float8_e4m3fn_x4", "uint8", "uint16", "bfloat16", "int32", "float16"
 SCRATCH = {
-    "lki": _s(32, I32), "spi": _s(1, I32), "klu": _s(8, U16), "wt": _s(512, BF), "wq": _s(128, X4), "wsc": _s(128, U8), "kcs": _s(C, X4), "kss": _s(C, U8),
-    "pidx": _s(2, I32), "pm": _s(8, I32), "pf": _s(8), "cs": _s(8),
+    "lki": _s(32, I32), "spi": _s(1, I32), "kl": _s(8, I32), "klu": _s(8, U16), "wt": _s(512, BF), "wq": _s(128, X4), "wsc": _s(128, U8), "kcs": _s(C, X4), "kss": _s(C, U8),
+    "pidx": _s(1, I32), "pm": _s(6, I32), "pf": _s(6), "cs": _s(10), "spx": _s(32), "spb": _s(32),
     "i_dup": _s(4), "dup": _s(4, U16), "osel": _s(2, U16), "asel": _s(2, U16), "i_xe": _s(8), "xe": _s(8, U16), "i_yc": _s(64),
     "i_sel": _s(NB), "sel": _s(NB, U16), "i_exp": _s(2 * NB), "exp3": _s(2 * NB, U16),
-    "i_16": _s(16), "rot1": _s(2, I32), "rot2": _s(2, I32), "rot": _s(2, U16), "dmp": _s(16),
+    "i_16": _s(16), "rot1": _s(2), "rot2": _s(2), "rot": _s(2, U16), "dmp": _s(16),
     "i_v3": _s(96), "v3c": _s(96), "i_oc": _s(NB), "oc6": _s(NB), "ones": _s(C // 2, BF), "zt": _s(C, BF),
     "spf": _s(1), "xd": _s(64), "yd": _s(128), "ol": _s(16, U16), "at": _s(16), "sg": _s(48), "r4": _s(64), "rr": _s(32), "xa": _s(128), "vk": _s(128),
-    "kb": _s(24, U16), "tab": _s(KEYS, BF), "hit": _s(C // 2, BF), "hitt": _s(C // 2, BF), "h4": _s(16), "fl": _s(16),
+    "kb": _s(24, U16), "tab": _s(KEYS, BF), "hit": _s(C // 2, BF), "hitt": _s(C // 2, BF), "h4": _s(32), "fl": _s(16),
     "zq": _s(64), "zqt": _s(64), "st": _s(64), "bt": _s(32), "qq": _s(16), "e1": _s(16), "e2": _s(16), "off": _s(8, U16),
     "wk": _s(NS + 264), "tk": _s(NS), "z2": _s(48), "zz": _s(56),
     "sw1": _s(32), "sw2": _s(64, U16), "lj": _s(64, U16),
     "pc0": _s(CAPP, X4), "pc1": _s(CAPP, X4), "pc2": _s(CAPP, X4), "pc3": _s(CAPP, X4),
     "ps0": _s(CAPP, U8), "ps1": _s(CAPP, U8), "ps2": _s(CAPP, U8), "ps3": _s(CAPP, U8),
     "ap": _s(32), "apx": _s(32), "x3": _s(SL, U16), "b3": _s(SL, U16), "b3f": _s(SL), "cmp3": _s((3 * NB - min(SIGNS)) * CAPP, F16),
-    "sc3": _s((3 * NB - min(SIGNS)) * CAPP // 2 + 1, F16), "j3": _s(max(SIGNS) * CAPP, BF), "em": _s(NB), "rc": _s(4 * NB), "u3": _s(4 * NB), "p3": _s(NB), "off3": _s(NB, U16), "v3": _s(96),
+    "sc3": _s((3 * NB - min(SIGNS)) * CAPP // 2 + 1, F16), "j3": _s(max(SIGNS) * CAPP, BF), "em": _s(16), "rc": _s(4 * NB), "u3": _s(4 * NB), "p3": _s(NB), "off3": _s(NB, U16), "v3": _s(96),
     "wo": _s(2 * (S + NB * (GAP + 64))), "to": _s(S), "y2": _s(40), "y4": _s(40), "zo": _s(64), "so1": _s(64), "so2": _s(64, U16), "lf": _s(64, U16),
     "rki": _s(32, U16), "rkf": _s(32),
     "fw": _s(LW * (N + 1), X4), "fsc": _s(LW * (N + 1), U8), "oq": _s(S, X4), "os_": _s(S, U8),
     "yw": _s(LW * (N + 1)), "ys": _s(S), "pz": ("psum", [128, 512 * N], "float32"),
 }
-SEMAPHORES = ["v", "s", "t", "gi", "dlk", "dl2", "dsp", "dw", "dk", "kin1", "kin2", "kin3", "slk", "colc", "cols", "ksent", "lsent", "st1"]
+SEMAPHORES = ["v", "s", "t", "gi", "dkl", "dlk", "dsp", "dw", "dk", "kin1", "kin2", "kin3", "slk", "colc", "cols", "ksent", "lsent", "st1"]
 
 
 def rank_program(g, core, T, topo):
@@ -120,58 +120,49 @@ def rank_program(g, core, T, topo):
     M3 = 3 * NB - A3
     R0 = -float(M3 * CAPP)
 
-    for a in range(2):
-        t_lk = dma("ys"[a], [], T.lki[16 * a:16 * a + 16, :], T.ky[:], "dlk")
-    for a in range(2, 4):
-        t_l2 = dma("ys"[a % 2], [], T.lki[16 * a:16 * a + 16, :], T.ky[:], "dl2")
-    for a in range(2):
-        t_sp = dma("ys"[a], [], T.spi[16 * a:16 * a + 16, :], T.sp[:], "dsp")
+    for a in range(2 if low else 0):
+        t_kl = dma("ys"[a], [], T.kl[64 * a:64 * a + 64, :], T.ky[:], "dkl")
+    for a in range(4):
+        t_lk = dma("ys"[a % 2], [], T.lki[16 * a:16 * a + 16, :], T.ky[:], "dlk")
+    t_sp = dma("s", [], T.spi[0:16, :], T.sp[:], "dsp")
 
-    t_pi = iota(T.pidx[:, 0:2], [[16, 2]], 0, 1, True)
+    t_pi = iota(T.pidx[:], [[0, 1]], 0, 1, True)
     t_id = iota(T.i_dup[:], [[16, 2], [0, 2]], 0)
-    iota(T.i_xe[:], [[2, 4], [32, 2]], 0)
-    iota(T.i_yc[:], [[-256, 2], [-1, 32]], 0)
+    t_yc = iota(T.i_yc[:], [[-256, 2], [-1, 32]], 0)
+    t_xe = iota(T.i_xe[:], [[2, 4], [32, 2]], 0)
     t_r4 = fill(T.r4[:, 3:64:4])
-    t_z1 = fill(T.zt[:, 0:128])
 
-    def bits(deps, a, b, src, shift, mask):
-        return vop(deps, "ts", T.pm[:, a:b], src, shift, mask, OP.arith_shift_right, OP.bitwise_and)
-    p15, second, first, p31, h8, q8 = [T.pf[:, i:i + 1] for i in range(6)]
-    m64, aq, u64, p15n, sb, sb2, p62, p16 = [T.cs[:, i:i + 1] for i in range(8)]
-    vop([], "set", T.spf[:], 0.0)
-    bits([t_pi], 0, 1, T.pidx[:, 0:1], 0, 15)
-    t = bits([], 1, 3, T.pidx[:, 0:2], 4, 1)
-    bits([], 3, 4, T.pidx[:, 0:1], 0, 31)
-    t_2 = vop([t], "copy", T.pf[:, 0:3], T.pm[:, 0:3])
-    bits([], 4, 5, T.pidx[:, 0:1], 3, 8)
-    t_dup = vop([t_2, t_id], "ts", T.dup[:], T.i_dup[:], p15, None, OP.add)
-    t = bits([], 5, 6, T.pidx[:, 0:1], 2, 24)
-    if nl:
-        bits([], 6, 7, T.pidx[:, 0:1], 0, 1)
-        t = bits([], 7, 8, T.pidx[:, 0:1], 1, 15)
-    n = 8 if nl else 6
-    need("v", [t])
-    t_as = lin([t_2], T.asel[:, 0:1], second, 32.0, p15)
-    t_sf = lin([t_sp], T.spf[0:32, :], T.spi[0:32, :], T.pf[0:32, 1:2])
+    p15, p1, ph, h8, second, q8 = [T.pf[:, i:i + 1] for i in range(6)]
+    m64, aq, u64, p15n, sb, sb2, p62, p16, p31, sr = [T.cs[:, i:i + 1] for i in range(10)]
+
+    def bits(i, shift, mask):
+        return vop([t_pi], "ts", T.pm[:, i:i + 1], T.pidx[:], shift, mask, OP.arith_shift_right, OP.bitwise_and)
+    vop([], "set", T.lki[64:128, :], 0)
+    vop([], "set", T.spx[0:32, :], 0.0)
+    for i, (shift, mask) in enumerate(((0, 15), (0, 1), (1, 7), (3, 8))):
+        t = bits(i, shift, mask)
+    bits(4, 4, 1)
+    t_pf = vop([t], "copy", T.pf[:, 0:4], T.pm[:, 0:4])
+    t_b = bits(5, 2, 24)
+    t_dup = vop([t_pf, t_id], "ts", T.dup[:], T.i_dup[:], p15, None, OP.add)
 
     t_ks = None
     if low:
-        for b in range(3):
-            t = vop([t_lk], "copy", T.klu[quad(b), :], T.lki[0:32, 8 * b:8 * b + 8])
-        need("g", [t, sop([t_lk], T.klu[quad(3), :], T.lki[0:32, 24:32], AF.Copy)])
-        t_ks = send(low, "kin%d" % r, lambda d: T.klu[:], lambda d: T.kb[:, 8 * (r - d - 1):8 * (r - d)], short, "ksent")
+        need("g", [vop([t_kl], "copy", T.klu[:], T.kl[:])])
+        ids = [DstId(rid=topo.addr(T.cores[d])[0], pnc=topo.addr(T.cores[d])[1]) for d in low]
+        g.remote_dma_fused([RemoteDMATransfer(dst_ids=ids, dma_engine_mask=sum(1 << e for e in fe), remote_sem=T.sem["kin%d" % r], srcs=[T.klu[:]],
+                                              dsts=[T.kb[:, 8 * (r - d - 1):8 * (r - d)] for d in low])], local_sem=T.sem.ksent)
+        total["ksent"] = len(fe)
+        t_ks = ("ksent", len(fe))
+    t_o = lin([t_pf], sr, p1, 32.0, ph)
+    t_q8 = sop([t_b], T.pf[:, 4:6], T.pm[:, 4:6], AF.Copy)
+    t_o = lin([t_o], T.osel[:, 0:1], sr, 1.0, h8)
+    t_as = lin([t_q8], T.asel[:, 0:1], second, 32.0, p15)
     t_w = dma("y", [t_ks, t_lk], T.wt[:], T.w[:], "dw")
     dma("y", [], T.kcs[:].bitcast(dt.uint8), T.kc[:], "dk")
     t_k = dma("y", [], T.kss[:], T.ks[:], "dk")
-    t_l4 = vop([t_lk, t_l2], "copy", T.lki[64:128, :], T.lki[0:64, :])
-    t_pf = vop([], "copy", T.pf[:, 3:n], T.pm[:, 3:n])
-    if nl:
-        t_one = vop([], "set", T.ones[:], 1.0)
-        vop([t_pf], "ts", T.osel[:, 0:1], T.pf[:, 6:7], 32.0, T.pf[:, 7:8], OP.mult, OP.add)
-    t_rot = vop([t_pf], "ts", T.rot1[:], T.i_dup[:, 0:4:2], p15, q8, OP.add, OP.add)
 
-    if r == 0:
-        t_zt = fill(T.zt[:, 128:C])
+    t_z1 = t_zt = fill(T.zt[:, 0:128 if r else C])
     t_i16 = iota(T.i_16[:], [[16, 16]], NS + 1)
     fill(T.zq[:, 16:64])
     t_zs = fill(T.st[:, 0:1])
@@ -187,64 +178,76 @@ def rank_program(g, core, T, topo):
     fill(T.yw[:, 0:8])
     if r:
         t_zt = fill(T.zt[:, 128:C])
-    t_wo = fill(T.wo[:, 0:2 * S:2], -1)
+    if r == 0:
+        t_wo = fill(T.wo[:, 0:2 * S:2], -1)
 
-    t = lin([t_sf, t_l4, t_dup], T.xd[:], T.lki[:].indirect(T.dup[:]), first, T.spf[:])
-    t_yd = vop([t], "tr", T.yd[:, 0:64], T.xd[:])
+    t = vop([t_lk, t_dup], "copy", T.xd[:], T.lki[:].indirect(T.dup[:]))
     if nl:
-        t_ol = vop([t_yd], "copy", T.ol[:], T.yd[:, 0:64].indirect(T.osel[:, 0:1]))
+        t_one = vop([], "set", T.ones[:], 1.0)
+    need("v", [t])
+    for b in range(2):
+        t_yd = vop([], "tr", T.yd[64 * b:64 * b + 64, 0:64], T.xd[0:64, :])
+    t = sop([t_sp], T.spf[0:16, :], T.spi[0:16, :], AF.Copy)
+    t_sx = lin([t, t_yc], T.spx[0:16, :], T.i_yc[0:16, 0:32], 0.0, T.spf[0:16, :])
+    if nl:
+        t_ol = vop([t_yd, t_o], "copy", T.ol[:], T.yd[:, 0:64].indirect(T.osel[:, 0:1]))
         t_tab = vop([t_ol, t_one], "copy", T.tab[:].indirect(T.ol[:]), T.ones[:])
+    t_sb = vop([t_sx], "tr", T.spb[0:32, :], T.spx[0:32, :])
     tk = {}
 
     def zeros():
         vop([t_zt], "q", T.fw[:, 0:128], T.fsc[:, 0:128], T.zt[:])
     if r == 0:
         zeros()
-    t = lin([t_yd, t_as], T.at[:], T.yd[:, 0:64].indirect(T.asel[:, 0:1]), 1.0, 0.5)
-    need("s", [t, t_r4])
-    for j in range(N - 1):
-        t = sop([], T.sg[0:32, 16 * j:16 * j + 16], T.at[0:32, :], AF.Sign, bias=T.yd[0:32, 16 + j:17 + j], scale=-1.0)
-    t_m = sop([], m64, p15, AF.Relu, bias=64.0, scale=-64.0)
-    lin([t_pf], aq, h8, 1.0, second)
+    lin([t_yd, t_as], T.at[:], T.yd[:, 0:64].indirect(T.asel[:, 0:1]), 1.0, 0.5)
+    sop([], m64, p15, AF.Relu, bias=64.0, scale=-64.0)
+    lin([], aq, h8, 1.0, second)
     t2 = lin([], p15n, p15, -16.0)
+    t_u = lin([t2], u64, m64, 1.0, aq)
+    t_yn = lin([], T.yd[:, 64:128], T.i_yc[:], 1.0, p15n)
+    need("s", [t_r4, t_sb])
+    for j in range(N - 1):
+        t = sop([], T.sg[0:32, 16 * j:16 * j + 16], T.at[0:32, :], AF.Sign, bias=T.spb[0:32, j:j + 1], scale=-1.0)
+    t2 = lin([t_u, t_xe], T.xe[:], T.i_xe[:], 1.0, u64)
     need("s", [t])
     for j in range(N - 1):
         t_r = lin([], T.r4[0:32, j:64:4], T.sg[0:32, 16 * j:16 * j + 16], -SL * (j + 1) / 2.0, SL * (j + 1) / 2.0)
     rr = T.rr[0:64, 1:32:2]
-    t = lin([t2], u64, m64, 1.0, aq)
-    t2 = lin([t_z1], T.yd[:, 64:128], T.i_yc[:], 1.0, p15n)
-    t = lin([t], T.xe[:], T.i_xe[:], 1.0, u64)
-    t_16 = lin([], p16, second, 16.0)
-    t_xa = sop([t, t2], T.xa[:], T.yd[:].indirect(T.xe[:]), AF.Copy)
+
+    def values():
+        return sop([t2, t_yn], T.xa[:], T.yd[:].indirect(T.xe[:]), AF.Copy)
+    if r == 0:
+        t_xa = values()
 
     fl = T.fl[0:64, :]
 
-    def ranges():
-        for b in range(2):
-            vop([t_r], "scan", T.rr[quad(b), :], T.r4[0:32, 0:64:2], T.r4[0:32, 1:64:2], 0.0, OP.max, OP.max)
+    def ranges(b):
+        vop([t_r], "scan", T.rr[quad(b), :], T.r4[0:32, 0:64:2], T.r4[0:32, 1:64:2], 0.0, OP.max, OP.max)
     if nl == 0:
-        t_rot = vop([t_rot], "ts", T.rot2[:], T.rot1[:], 31, None, OP.bitwise_and)
-        ranges()
+        ranges(0)
+        ranges(1)
         t_f = vop([], "set", fl, 1.0)
     else:
         t = t_tab
-        t_rot = vop([t_rot], "ts", T.rot2[:], T.rot1[:], 31, None, OP.bitwise_and)
         for a in range(nl):
             kin = "kin%d" % (r + 1 + a)
-            total[kin] = KE
-            t = vop([t, (kin, KE), t_z1], "copy", T.tab[:].indirect(T.kb[:, 8 * a:8 * a + 8]), T.zt[:, 0:128])
-        t2 = sop([t], T.hit[:, GV:C // 2], T.tab[:].indirect(T.ol[:, GV // 16:16]), AF.Copy)
+            total[kin] = len(fe)
+            t = vop([t, (kin, len(fe)), t_z1], "copy", T.tab[:].indirect(T.kb[:, 8 * a:8 * a + 8]), T.zt[:, 0:128])
+        t3 = sop([t], T.hit[:, GV:C // 2], T.tab[:].indirect(T.ol[:, GV // 16:16]), AF.Copy)
         t = vop([t], "copy", T.hit[:, 0:GV], T.tab[:].indirect(T.ol[:, 0:GV // 16]))
-        ranges()
-        t = vop([t, t2], "tr", T.hitt[:], T.hit[:])
+        ranges(0)
+        t = vop([t, t3], "tr", T.hitt[:], T.hit[:])
+        ranges(1)
         need("v", [t])
         for h in range(2):
-            t = vop([], "tt", T.h4[0:64, 8 * h:8 * h + 8], T.hitt[0:64, 16 * h:C // 2:32], T.hitt[64:128, 16 * h:C // 2:32], OP.min)
+            t = vop([], "tt", T.h4[0:32, 16 * h:16 * h + 16], T.hitt[quad(2 * h), 0:C // 2:16], T.hitt[quad(2 * h + 1), 0:C // 2:16], OP.min)
         need("v", [t])
         for b in range(2):
-            t_f = vop([], "tt", T.fl[quad(b), :], T.h4[0:32, :], T.h4[32:64, :], OP.min)
+            t_f = vop([], "tt", T.fl[quad(b), :], T.h4[0:32, 0:32:2], T.h4[0:32, 1:32:2], OP.min)
 
-    t_dm = lin([t_i16], T.dmp[:], T.i_16[:], 1.0, p15)
+    if r:
+        t_xa = values()
+    lin([t_i16], T.dmp[:], T.i_16[:], 1.0, p15)
     t_e = sop([t_f], T.e1[0:64, :], fl, AF.Copy, scale=float(2 * NS))
     vop([t_f, t_zs], "scan", T.zq[0:64, 0:16], rr, fl, 0.0, OP.max, OP.add)
     t = vop([], "scan", T.zq[0:64, 32:48], T.zq[0:64, 16:32], fl, 0.0, OP.add, OP.add)
@@ -257,10 +260,18 @@ def rank_program(g, core, T, topo):
     need("v", [t, t2])
     for b in range(2):
         t = vop([], "tt", T.off[64 * b:64 * b + 64, :], T.qq[0:64, 8 * b:8 * b + 8], T.e2[0:64, 8 * b:8 * b + 8], OP.max)
-    t_sb = lin([t_16], sb, m64, -8192.0, p16)
-    t2 = lin([], p62, p31, 2.0)
+    t3 = lin([t_as], sr, p15, 1.0, q8)
+    t_sb = lin([], p16, second, 16.0)
+    t2 = lin([], p31, second, 16.0, p15)
+    t3 = lin([t3], T.rot1[:], T.i_dup[:, 0:4:2], 1.0, sr)
+    t_sb = lin([t_sb], sb, m64, -8192.0, p16)
+    t3 = sop([t3], T.rot2[:], T.rot1[:], AF.Sign, bias=-31.5)
+    t2 = lin([t2], p62, p31, 2.0)
+    t3 = lin([t3], T.rot2[:], T.rot2[:], -16.0, -16.0)
     lin([], T.sc3[:, 0:1], p15, 0.0, R0)
-    sop([t_rot], T.rot[:], T.rot2[:], AF.Copy)
+    need("s", [t3])
+    for c in range(2):
+        lin([], T.rot[:, c:c + 1], T.rot2[:, c:c + 1], 1.0, T.rot1[:, c:c + 1])
     t_sb = lin([t_sb], sb2, q8, 32.0, sb)
     lin([t2, t_oc], T.oc6[:], T.i_oc[:], 1.0, p62)
     lin([t_iv], T.exp3[:], T.i_exp[:], 1.0, q8)
@@ -281,11 +292,17 @@ def rank_program(g, core, T, topo):
     NZ = N * NB
     t = vop([t, t_vk, t_wk], "copy", T.wk[:].indirect(T.off[:]), T.vk[:])
     t = vop([t], "tr", T.tk[:], T.wk[:, 1:NS + 1])
-    pairs(t, T.tk, NZ, (0, 1), T.z2, OP.min)
-    for b in range(2):
-        t_zz = vop([], "tt", T.zz[64 * b:64 * b + 64, 0:2 * NZ], T.z2[0:64, :], T.z2[64:128, :], OP.min)
-    need("g", [t_zz])
-    send(others, "slk", lambda d: T.zz[:, NZ + NB * d:NZ + NB * d + 8], lambda d: T.ap[:, 8 * r:8 * r + 8], short)
+    need("v", [t])
+    two = [vop([], "tt", T.z2[:, NZ * row:NZ * (row + 1)], T.tk[:, row:NS:32], T.tk[:, 16 + row:NS:32], OP.min) for row in (1, 0)]
+    for row, t in zip((1, 0), two):
+        for b in range(2):
+            t_zz = vop([t], "tt", T.zz[64 * b:64 * b + 64, NZ * row:NZ * (row + 1)], T.z2[0:64, NZ * row:NZ * (row + 1)],
+                       T.z2[64:128, NZ * row:NZ * (row + 1)], OP.min)
+        if row:
+            need("g", [t_zz])
+    send(far + near, "slk", lambda d: T.zz[:, NZ + NB * d:NZ + NB * d + 8], lambda d: T.ap[:, 8 * r:8 * r + 8], short)
+    if r:
+        t_wo = fill(T.wo[:, 0:2 * S:2], -1)
     t_own = sop([t_zz, t_wk], T.ap[:, 8 * r:8 * r + 8], T.zz[:, NZ + NB * r:NZ + NB * r + 8], AF.Copy)
     t = vop([t_zz], "tr", T.sw1[:], T.zz[:, 0:32])
     t_lj = lists(t, T.sw1, T.sw2, T.lj, -1.0, 0.0)
@@ -304,43 +321,40 @@ def rank_program(g, core, T, topo):
 
     def own():
         tk["v"], tk["s"] = pick(r, T.fw[:, w0:w0 + CAPP], T.fsc[:, w0:w0 + CAPP])
-        if r:
-            zeros()
+
+    def pack():
         tk["w"] = vop([t_w], "q", T.wq[:], T.wsc[:], T.wt[:])
     if r:
         own()
+        zeros()
+        pack()
 
     total["slk"] = KE * (N - 1)
     total["colc"] = total["cols"] = sum(len(eng[d]) for d in others)
     t_in = [("slk", total["slk"]), t_own, t_c]
-    H = SL // 2 if r else SL
-    t2 = sop(t_in, T.x3[:, H:SL], T.ap[:].indirect(T.exp3[:, H // 16:SL // 16]), AF.Copy) if r else None
+    H = SL // 2
+    t2 = sop(t_in, T.x3[:, H:SL], T.ap[:].indirect(T.exp3[:, H // 16:SL // 16]), AF.Copy)
     t_ax = lin(t_in, T.apx[:], T.ap[:].indirect(T.rot[:]), 1.0, -0.5)
     t = vop(t_in, "copy", T.x3[:, 0:H], T.ap[:].indirect(T.exp3[:, 0:H // 16]))
     t_b3 = vop([t, t2], "tr", T.b3[:], T.x3[:])
-    t_em = sop([t_ax], T.em[:], T.apx[:, 0:NB], AF.Relu, bias=2 * S - EMPTY + 0.5)
+    t_em = sop([], T.em[:], T.ap[:].indirect(T.rot[:, 0:1]), AF.Relu, bias=float(2 * S - EMPTY))
 
     def scal(c):
         a = 8 * (1 + c // NB) + c % NB
         return T.apx[:, a:a + 1]
-    t_bf = sop([t_b3], T.b3f[:], T.b3[:], AF.Copy)
+    t_bf = sop([t_b3, t_ax], T.b3f[:], T.b3[:], AF.Copy)
     for c in range(A3):
         t_s = sop([], T.j3[:, CAPP * c:CAPP * (c + 1)], T.b3[:, 0:CAPP], AF.Sign, bias=scal(c), scale=-1.0, accum_out=T.rc[:, NB + c:NB + c + 1])
     need("v", [t_b3, t_ax])
     for x in range(M3):
         t = vop([], "ts", T.cmp3[:, CAPP * x:CAPP * (x + 1)], T.b3[:, 0:CAPP], scal(A3 + x), 2.0, OP.is_lt, OP.mult)
     H = CAPP // 2
-    vop([t_em, t_wo], "tt", T.rc[:, 0:NB], T.em[:], T.oc6[:], OP.add)
+    vop([t_em, t_wo], "tt", T.rc[:, 0:NB], T.em[:, 0:NB], T.oc6[:], OP.add)
     t = vop([t], "scan", T.sc3[:, 1:M3 * H + 1], T.cmp3[:, 0:M3 * CAPP:2], T.cmp3[:, 1:M3 * CAPP:2], R0, OP.add, OP.add)
     t_v3 = vop([t_bf], "tt", T.v3[:], T.b3f[:].indirect(T.sel[:]), T.v3c[:], OP.max)
     t = vop([t], "tt", T.rc[:, NB + A3:4 * NB], T.sc3[:, H:M3 * H + 1:H], T.sc3[:, 0:(M3 - 1) * H + 1:H], OP.subtract)
     if r == 0:
         own()
-    for s in [r] + others:
-        a = LW * (s + 1)
-        need("t", [tk["w"]] + ([tk["v"], tk["s"]] if s == r else [("colc", total["colc"]), ("cols", total["cols"])]))
-        t_t = done(g.tensor.matmul_mx(T.pz[:, 512 * s:512 * s + CAPP], T.wq[:], T.wsc[:], T.fw[:, a:a + CAPP], T.fsc[:, a:a + CAPP], True, True), "t")
-        t_y = sop([t_t], T.yw[:, a:a + CAPP], T.pz[:, 512 * s:512 * s + CAPP], AF.Copy)
     W = 2 * NB
     vop([t, t_s], "tt", T.u3[0:64, 0:W], T.rc[0:64, 0:W], T.rc[64:128, W:2 * W], OP.add)
     t = vop([], "tt", T.u3[0:64, W:2 * W], T.rc[0:64, W:2 * W], T.rc[64:128, 0:W], OP.add)
@@ -349,6 +363,13 @@ def rank_program(g, core, T, topo):
         k = (s - 1) % N
         t = vop([], "tt", T.off3[quad(s), :], T.u3[0:32, NB * s:NB * (s + 1)], T.u3[32:64, NB * k:NB * (k + 1)], OP.add)
     t = vop([t, t_v3], "copy", T.wo[:].indirect(T.off3[:]), T.v3[:])
+    if r == 0:
+        pack()
+    for s in [r] + others:
+        a = LW * (s + 1)
+        need("t", [tk["w"]] + ([tk["v"], tk["s"]] if s == r else [("colc", total["colc"]), ("cols", total["cols"])]))
+        t_t = done(g.tensor.matmul_mx(T.pz[:, 512 * s:512 * s + CAPP], T.wq[:], T.wsc[:], T.fw[:, a:a + CAPP], T.fsc[:, a:a + CAPP], True, True), "t")
+        t_y = sop([t_t], T.yw[:, a:a + CAPP], T.pz[:, 512 * s:512 * s + CAPP], AF.Copy)
     t = vop([t], "tr", T.to[:], T.wo[:, 0:2 * S:2])
     NO = S // 32
     pairs(t, T.to, NO, (1, 0), T.y2, OP.max)

@@ -6,11 +6,11 @@ KEYS = 65536
 SL = 192
 NB = SL // 32
 NS = N * SL
-LW = 256
+LW = NS
 EMPTY = 2 * KEYS
 GAP = 576
 GV = 128
-SIGNS = (9, 8, 8, 8)
+SIGNS = (11, 10, 10, 10)
 TAIL = [("c", 0, 96), ("y", 0, 96), ("c", 96, 352), ("y", 96, 352), ("c", 352, 640), ("y", 352, 640), ("s",)]
 SV = 320
 
@@ -22,7 +22,7 @@ def _s(n, d="float32"):
 X4, U8, U16, BF, I32, F16 = "float8_e4m3fn_x4", "uint8", "uint16", "bfloat16", "int32", "float16"
 SCRATCH = {
     "lki": _s(32, I32), "spi": _s(1, I32), "kl": _s(8, I32), "klu": _s(8, U16), "wt": _s(512, BF), "wq": _s(128, X4), "wsc": _s(128, U8), "kcs": _s(C, X4), "kss": _s(C, U8),
-    "pidx": _s(1, I32), "pm": _s(6, I32), "pf": _s(6), "cs": _s(10), "spx": _s(32), "spb": _s(32),
+    "pidx": _s(1, I32), "pm": _s(6, I32), "pf": _s(6), "cs": _s(11), "spx": _s(32), "spb": _s(32),
     "i_dup": _s(4), "dup": _s(4, U16), "osel": _s(2, U16), "asel": _s(2, U16), "i_xe": _s(8), "xe": _s(8, U16), "i_yc": _s(64),
     "i_sel": _s(NB), "sel": _s(NB, U16), "i_exp": _s(2 * NB), "exp3": _s(2 * NB, U16),
     "i_16": _s(16), "rot1": _s(2), "rot2": _s(2), "rot": _s(2, U16), "dmp": _s(16),
@@ -30,16 +30,15 @@ SCRATCH = {
     "spf": _s(1), "xd": _s(64), "yd": _s(128), "ol": _s(16, U16), "at": _s(16), "sg": _s(48), "r4": _s(64), "rr": _s(32), "xa": _s(128), "vk": _s(128),
     "kb": _s(24, U16), "tab": _s(KEYS, BF), "hit": _s(C // 2, BF), "hitt": _s(C // 2, BF), "h4": _s(32), "fl": _s(16),
     "zq": _s(64), "zqt": _s(64), "st": _s(64), "bt": _s(32), "qq": _s(16), "e1": _s(16), "e2": _s(16), "off": _s(8, U16),
-    "wk": _s(NS + 264), "tk": _s(NS), "z2": _s(48), "zz": _s(56),
-    "sw1": _s(32), "sw2": _s(64, U16), "lj": _s(64, U16),
-    "pc0": _s(CAPP, X4), "pc1": _s(CAPP, X4), "pc2": _s(CAPP, X4), "pc3": _s(CAPP, X4),
-    "ps0": _s(CAPP, U8), "ps1": _s(CAPP, U8), "ps2": _s(CAPP, U8), "ps3": _s(CAPP, U8),
-    "ap": _s(32), "apx": _s(32), "x3": _s(SL, U16), "b3": _s(SL, U16), "b3f": _s(SL), "cmp3": _s((3 * NB - min(SIGNS)) * CAPP, F16),
-    "sc3": _s((3 * NB - min(SIGNS)) * CAPP // 2 + 1, F16), "j3": _s(max(SIGNS) * CAPP, BF), "em": _s(16), "rc": _s(4 * NB), "u3": _s(4 * NB), "p3": _s(NB), "off3": _s(NB, U16), "v3": _s(96),
-    "wo": _s(2 * (S + NB * (GAP + 64))), "to": _s(S), "y2": _s(40), "y4": _s(40), "zo": _s(64), "so1": _s(64), "so2": _s(64, U16), "lf": _s(64, U16),
+    "wk": _s(NS + 264), "tk": ("sbuf", [128, NS // 32, 32], "float32"), "z2": ("sbuf", [128, NS // 32, 2], "float32"), "zz": _s(32), "zc": _s(32, U16),
+    "sw2": ("sbuf", [128, 4, 16], U16), "lj": _s(64, U16),
+    "ap": _s(32), "apx": _s(32), "x3": _s(SL, U16), "b3": _s(SL, U16), "b3f": _s(SL), "v3": _s(96), "cmp3": _s((3 * NB - min(SIGNS)) * CAPP, F16),
+    "sc3": _s((3 * NB - min(SIGNS)) * CAPP // 2 + 1, F16), "j3": _s(max(SIGNS) * CAPP, BF), "em": _s(16), "rc": ("sbuf", [128, 2, 2 * NB], "float32"), "u3": _s(4 * NB), "off3": _s(NB, U16),
+    "wo": _s(2 * (S + NB * (GAP + 64))), "to": ("sbuf", [128, S // 32, 32], "float32"), "y2": ("sbuf", [128, S // 32, 2], "float32"), "y4": _s(40), "zo": _s(32, U16), "zk": _s(32), "sok": _s(32),
+    "so2": ("sbuf", [128, 4, 16], U16), "lf": _s(64, U16),
     "rki": _s(32, U16), "rkf": _s(32),
-    "fw": _s(LW * (N + 1), X4), "fsc": _s(LW * (N + 1), U8), "oq": _s(S, X4), "os_": _s(S, U8),
-    "yw": _s(LW * (N + 1)), "ys": _s(S), "pz": ("psum", [128, 512 * N], "float32"),
+    "fw": _s(LW * N + CAPP, X4), "fsc": _s(LW * N + CAPP, U8), "oq": _s(S, X4), "os_": _s(S, U8),
+    "yw": _s(LW * N + CAPP), "ys": _s(S), "pz": ("psum", [128, 512 * N], "float32"),
 }
 SEMAPHORES = ["v", "s", "t", "gi", "dkl", "dlk", "dsp", "dw", "dk", "kin1", "kin2", "kin3", "slk", "colc", "cols", "ksent", "lsent", "st1"]
 
@@ -131,20 +130,25 @@ def rank_program(g, core, T, topo):
     t_yc = iota(T.i_yc[:], [[-256, 2], [-1, 32]], 0)
     t_xe = iota(T.i_xe[:], [[2, 4], [32, 2]], 0)
     t_r4 = fill(T.r4[:, 3:64:4])
+    fill(T.zq[:, 16:64])
+    t_zs = fill(T.st[:, 0:1])
 
     p15, p1, ph, h8, second, q8 = [T.pf[:, i:i + 1] for i in range(6)]
-    m64, aq, u64, p15n, sb, sb2, p62, p16, p31, sr = [T.cs[:, i:i + 1] for i in range(10)]
+    m64, aq, u64, p15n, sb, sb2, p62, p16, p31, sr, far1 = [T.cs[:, i:i + 1] for i in range(11)]
 
     def bits(i, shift, mask):
         return vop([t_pi], "ts", T.pm[:, i:i + 1], T.pidx[:], shift, mask, OP.arith_shift_right, OP.bitwise_and)
     vop([], "set", T.lki[64:128, :], 0)
-    vop([], "set", T.spx[0:32, :], 0.0)
+    vop([], "set", T.spx[0:64, :], 0.0)
     for i, (shift, mask) in enumerate(((0, 15), (0, 1), (1, 7), (3, 8))):
         t = bits(i, shift, mask)
     bits(4, 4, 1)
     t_pf = vop([t], "copy", T.pf[:, 0:4], T.pm[:, 0:4])
     t_b = bits(5, 2, 24)
     t_dup = vop([t_pf, t_id], "ts", T.dup[:], T.i_dup[:], p15, None, OP.add)
+    if nl:
+        vop([], "set", T.ones[:], 1.0)
+    vop([], "set", T.zt[:, 0:128], 0.0)
 
     t_ks = None
     if low:
@@ -162,91 +166,81 @@ def rank_program(g, core, T, topo):
     dma("y", [], T.kcs[:].bitcast(dt.uint8), T.kc[:], "dk")
     t_k = dma("y", [], T.kss[:], T.ks[:], "dk")
 
-    t_z1 = t_zt = fill(T.zt[:, 0:128 if r else C])
     t_i16 = iota(T.i_16[:], [[16, 16]], NS + 1)
-    fill(T.zq[:, 16:64])
-    t_zs = fill(T.st[:, 0:1])
-    fill(T.zz[:, 48:56])
-    t_wk = iota(T.wk[:, 1:NS + 1], [[0, N], [2 * GAP, NB], [0, 32]], EMPTY)
+    fill(T.zz[:, 24:32])
+    if r == 0:
+        t_zt = fill(T.zt[:, 128:C])
+    t_wk = iota(T.wk[:, 1:NS + 1], [[0, N], [-2 * GAP, NB], [0, 32]], -EMPTY)
     iota(T.i_exp[:], [[1, NB], [0, 2]], 0)
     iota(T.i_sel[:], [[32, NB]], 0)
-    t_iv = iota(T.i_v3[:], [[32, NB], [1, 16]], KEYS + LW)
+    t_iv = iota(T.i_v3[:], [[32, NB], [1, 16]], LW)
     for a, b, n in ((0, A3 % NB, A3 // NB + 1), (A3 % NB, NB, A3 // NB)):
         if a < b:
             t_oc = iota(T.i_oc[:, a:b], [[64, b - a]], n * CAPP + 64 * a)
-    fill(T.zo[:, 40:64])
+    fill(T.zk[:, 20:32])
     fill(T.yw[:, 0:8])
     if r:
         t_zt = fill(T.zt[:, 128:C])
     if r == 0:
         t_wo = fill(T.wo[:, 0:2 * S:2], -1)
 
-    t = vop([t_lk, t_dup], "copy", T.xd[:], T.lki[:].indirect(T.dup[:]))
-    if nl:
-        t_one = vop([], "set", T.ones[:], 1.0)
-    need("v", [t])
+    need("v", [vop([t_lk, t_dup], "copy", T.xd[:], T.lki[:].indirect(T.dup[:]))])
     for b in range(2):
         t_yd = vop([], "tr", T.yd[64 * b:64 * b + 64, 0:64], T.xd[0:64, :])
+    sop([], m64, p15, AF.Relu, bias=64.0, scale=-64.0)
+    lin([], aq, h8, 1.0, second)
+    t2 = lin([], p15n, p15, -16.0)
     t = sop([t_sp], T.spf[0:16, :], T.spi[0:16, :], AF.Copy)
-    t_sx = lin([t, t_yc], T.spx[0:16, :], T.i_yc[0:16, 0:32], 0.0, T.spf[0:16, :])
+    t_u = lin([t2], u64, m64, 1.0, aq)
+    for b in range(2):
+        t_sx = lin([t, t_yc], T.spx[32 * b:32 * b + 16, :], T.i_yc[0:16, 0:32], 0.0, T.spf[0:16, :])
+    t_yn = lin([], T.yd[:, 64:128], T.i_yc[:], 1.0, p15n)
+    t2 = lin([t_u, t_xe], T.xe[:], T.i_xe[:], 1.0, u64)
     if nl:
         t_ol = vop([t_yd, t_o], "copy", T.ol[:], T.yd[:, 0:64].indirect(T.osel[:, 0:1]))
-        t_tab = vop([t_ol, t_one], "copy", T.tab[:].indirect(T.ol[:]), T.ones[:])
-    t_sb = vop([t_sx], "tr", T.spb[0:32, :], T.spx[0:32, :])
+    t_sb = vop([t_sx], "tr", T.spb[0:64, :], T.spx[0:64, :])
+    if nl:
+        t_tab = vop([t_ol], "copy", T.tab[:].indirect(T.ol[:]), T.ones[:])
     tk = {}
+    t = lin([t_yd, t_as], T.at[:], T.yd[:, 0:64].indirect(T.asel[:, 0:1]), 1.0, 0.5)
+    t_xa = sop([t2, t_yn], T.xa[:], T.yd[:].indirect(T.xe[:]), AF.Copy, scale=-1.0)
+    need("s", [t, t_r4, t_sb])
+    for j in range(N - 1):
+        t = sop([], T.sg[0:64, 16 * j:16 * j + 16], T.at[0:64, :], AF.Sign, bias=T.spb[0:64, j:j + 1], scale=-1.0)
+    need("s", [t])
+    for j in range(N - 1):
+        t_r = lin([], T.r4[0:64, j:64:4], T.sg[0:64, 16 * j:16 * j + 16], -SL * (j + 1) / 2.0, SL * (j + 1) / 2.0)
+    t_vk = vop([t_xa], "tr", T.vk[:], T.xa[:])
 
     def zeros():
         vop([t_zt], "q", T.fw[:, 0:128], T.fsc[:, 0:128], T.zt[:])
     if r == 0:
         zeros()
-    lin([t_yd, t_as], T.at[:], T.yd[:, 0:64].indirect(T.asel[:, 0:1]), 1.0, 0.5)
-    sop([], m64, p15, AF.Relu, bias=64.0, scale=-64.0)
-    lin([], aq, h8, 1.0, second)
-    t2 = lin([], p15n, p15, -16.0)
-    t_u = lin([t2], u64, m64, 1.0, aq)
-    t_yn = lin([], T.yd[:, 64:128], T.i_yc[:], 1.0, p15n)
-    need("s", [t_r4, t_sb])
-    for j in range(N - 1):
-        t = sop([], T.sg[0:32, 16 * j:16 * j + 16], T.at[0:32, :], AF.Sign, bias=T.spb[0:32, j:j + 1], scale=-1.0)
-    t2 = lin([t_u, t_xe], T.xe[:], T.i_xe[:], 1.0, u64)
-    need("s", [t])
-    for j in range(N - 1):
-        t_r = lin([], T.r4[0:32, j:64:4], T.sg[0:32, 16 * j:16 * j + 16], -SL * (j + 1) / 2.0, SL * (j + 1) / 2.0)
     rr = T.rr[0:64, 1:32:2]
 
-    def values():
-        return sop([t2, t_yn], T.xa[:], T.yd[:].indirect(T.xe[:]), AF.Copy)
-    if r == 0:
-        t_xa = values()
+    def ranges():
+        vop([t_r], "scan", T.rr[0:64, :], T.r4[0:64, 0:64:2], T.r4[0:64, 1:64:2], 0.0, OP.max, OP.max)
 
     fl = T.fl[0:64, :]
-
-    def ranges(b):
-        vop([t_r], "scan", T.rr[quad(b), :], T.r4[0:32, 0:64:2], T.r4[0:32, 1:64:2], 0.0, OP.max, OP.max)
     if nl == 0:
-        ranges(0)
-        ranges(1)
+        ranges()
         t_f = vop([], "set", fl, 1.0)
     else:
         t = t_tab
         for a in range(nl):
             kin = "kin%d" % (r + 1 + a)
             total[kin] = len(fe)
-            t = vop([t, (kin, len(fe)), t_z1], "copy", T.tab[:].indirect(T.kb[:, 8 * a:8 * a + 8]), T.zt[:, 0:128])
+            t = vop([t, (kin, len(fe))], "copy", T.tab[:].indirect(T.kb[:, 8 * a:8 * a + 8]), T.zt[:, 0:128])
         t3 = sop([t], T.hit[:, GV:C // 2], T.tab[:].indirect(T.ol[:, GV // 16:16]), AF.Copy)
         t = vop([t], "copy", T.hit[:, 0:GV], T.tab[:].indirect(T.ol[:, 0:GV // 16]))
-        ranges(0)
-        t = vop([t, t3], "tr", T.hitt[:], T.hit[:])
-        ranges(1)
-        need("v", [t])
+        ranges()
+        need("v", [vop([t, t3], "tr", T.hitt[:], T.hit[:])])
         for h in range(2):
             t = vop([], "tt", T.h4[0:32, 16 * h:16 * h + 16], T.hitt[quad(2 * h), 0:C // 2:16], T.hitt[quad(2 * h + 1), 0:C // 2:16], OP.min)
         need("v", [t])
         for b in range(2):
             t_f = vop([], "tt", T.fl[quad(b), :], T.h4[0:32, 0:32:2], T.h4[0:32, 1:32:2], OP.min)
 
-    if r:
-        t_xa = values()
     lin([t_i16], T.dmp[:], T.i_16[:], 1.0, p15)
     t_e = sop([t_f], T.e1[0:64, :], fl, AF.Copy, scale=float(2 * NS))
     vop([t_f, t_zs], "scan", T.zq[0:64, 0:16], rr, fl, 0.0, OP.max, OP.add)
@@ -255,7 +249,6 @@ def rank_program(g, core, T, topo):
     t = vop([t], "scan", T.st[0:64, 1:33], T.zqt[0:64, 32:64], T.zqt[0:64, 0:32], 0.0, OP.add, OP.max)
     t2 = vop([t_e], "tt", T.e2[0:64, :], T.dmp[0:64, :], T.e1[0:64, :], OP.subtract)
     t = vop([t], "tr", T.bt[0:64, :], T.st[0:64, 0:32])
-    t_vk = vop([t_xa], "tr", T.vk[:], T.xa[:])
     t = vop([t], "scan", T.qq[0:64, :], rr, fl, T.bt[0:64, 15:16], OP.max, OP.add)
     need("v", [t, t2])
     for b in range(2):
@@ -264,7 +257,10 @@ def rank_program(g, core, T, topo):
     t_sb = lin([], p16, second, 16.0)
     t2 = lin([], p31, second, 16.0, p15)
     t3 = lin([t3], T.rot1[:], T.i_dup[:, 0:4:2], 1.0, sr)
-    t_sb = lin([t_sb], sb, m64, -8192.0, p16)
+    t_sb = lin([t_sb], sb, m64, 8192.0, p16)
+    lin([], far1, m64, -8192.0, 64 * 8192.0)
+    lin([], T.zc[:, 24:32], T.i_16[:, 0:8], 0.0)
+    lin([], T.zo[:, 20:32], T.i_16[:, 0:12], 0.0)
     t3 = sop([t3], T.rot2[:], T.rot1[:], AF.Sign, bias=-31.5)
     t2 = lin([t2], p62, p31, 2.0)
     t3 = lin([t3], T.rot2[:], T.rot2[:], -16.0, -16.0)
@@ -272,93 +268,83 @@ def rank_program(g, core, T, topo):
     need("s", [t3])
     for c in range(2):
         lin([], T.rot[:, c:c + 1], T.rot2[:, c:c + 1], 1.0, T.rot1[:, c:c + 1])
-    t_sb = lin([t_sb], sb2, q8, 32.0, sb)
+    t_sb = lin([t_sb], sb2, q8, LW / 8.0, sb)
     lin([t2, t_oc], T.oc6[:], T.i_oc[:], 1.0, p62)
     lin([t_iv], T.exp3[:], T.i_exp[:], 1.0, q8)
     lin([], T.sel[:], T.i_sel[:], 1.0, p31)
     t_c = lin([t_sb], T.v3c[:], T.i_v3[:], 1.0, sb2)
 
-    def pairs(tok, turned, n, rows, two, op):
+    def lists(tok, z, twice, out, between=None):
         need("v", [tok])
-        for i, row in enumerate(rows):
-            t = vop([], "tt", two[:, n * i:n * (i + 1)], turned[:, row:32 * n:32], turned[:, 16 + row:32 * n:32], op)
-        need("v", [t])
-
-    def lists(tok, s1, s2, out, scale, shift):
-        t = vop([tok], "ts", s2[:], s1[:, 0:32].indirect(T.dup[:]), scale, shift, OP.mult, OP.add)
-        vop([t], "tr", out[:, 0:64:2], s2[:, 0:32])
-        return [vop([], "tr", out[:, 1:64:2], s2[:, 32:64])]
+        t1 = [vop([], "tr", twice[:, a:4:2, :], z[:]) for a in range(2)][1]
+        if between:
+            between()
+        need("v", [t1])
+        return t1, [[vop([], "tr", out[:, a:64:2], twice[:, 2 * a:2 * a + 2, :]) for a in range(2)][1]]
 
     NZ = N * NB
     t = vop([t, t_vk, t_wk], "copy", T.wk[:].indirect(T.off[:]), T.vk[:])
     t = vop([t], "tr", T.tk[:], T.wk[:, 1:NS + 1])
-    need("v", [t])
-    two = [vop([], "tt", T.z2[:, NZ * row:NZ * (row + 1)], T.tk[:, row:NS:32], T.tk[:, 16 + row:NS:32], OP.min) for row in (1, 0)]
-    for row, t in zip((1, 0), two):
-        for b in range(2):
-            t_zz = vop([t], "tt", T.zz[64 * b:64 * b + 64, NZ * row:NZ * (row + 1)], T.z2[0:64, NZ * row:NZ * (row + 1)],
-                       T.z2[64:128, NZ * row:NZ * (row + 1)], OP.min)
-        if row:
-            need("g", [t_zz])
-    send(far + near, "slk", lambda d: T.zz[:, NZ + NB * d:NZ + NB * d + 8], lambda d: T.ap[:, 8 * r:8 * r + 8], short)
+    t, t2 = [vop([t], "tt", T.z2[:, :, row], T.tk[:, :, row], T.tk[:, :, 16 + row], OP.max) for row in (1, 0)]
+    for b in range(2):
+        t_zz = vop([t], "tt", T.zz[64 * b:64 * b + 64, 0:NZ], T.z2[0:64, :, 1], T.z2[64:128, :, 1], OP.max)
+    need("g", [t_zz])
+    send(far + near, "slk", lambda d: T.zz[:, NB * d:NB * d + 8], lambda d: T.ap[:, 8 * r:8 * r + 8], short)
     if r:
         t_wo = fill(T.wo[:, 0:2 * S:2], -1)
-    t_own = sop([t_zz, t_wk], T.ap[:, 8 * r:8 * r + 8], T.zz[:, NZ + NB * r:NZ + NB * r + 8], AF.Copy)
-    t = vop([t_zz], "tr", T.sw1[:], T.zz[:, 0:32])
-    t_lj = lists(t, T.sw1, T.sw2, T.lj, -1.0, 0.0)
+    t_own = sop([t_zz, t_wk], T.ap[:, 8 * r:8 * r + 8], T.zz[:, NB * r:NB * r + 8], AF.Copy)
+    for b in range(2):
+        t = vop([t2, t_c], "tt", T.zc[64 * b:64 * b + 64, 0:NZ], T.z2[0:64, :, 0], T.z2[64:128, :, 0], OP.max)
+    t_lj = lists(t, T.zc, T.sw2, T.lj)[1]
 
-    def pick(d, oc, osc):
-        L = T.lj[:, 2 * NB * d:2 * NB * d + CAPP // 16]
-        return (vop(t_lj + [t_k], "copy", oc.bitcast(dt.uint32), T.kcs[:].bitcast(dt.uint32).indirect(L)),
-                sop(t_lj + [t_k], osc, T.kss[:].indirect(L), AF.Copy))
-    for d in far + near:
-        t_pv, t_ps = pick(d, T["pc%d" % d][:], T["ps%d" % d][:])
-    w0 = LW * (r + 1)
-    need("g", [t_pv])
-    send(far + near, "colc", lambda d: T["pc%d" % d][:].bitcast(dt.uint8), lambda d: T.fw[:, w0:w0 + CAPP].bitcast(dt.uint8), eng.get)
-    need("g", [t_ps])
-    send(far + near, "cols", lambda d: T["ps%d" % d][:], lambda d: T.fsc[:, w0:w0 + CAPP], eng.get)
+    w0, NP = LW * (r + 1), NS - SL + CAPP
+    p0 = w0 - SL * r
 
-    def own():
-        tk["v"], tk["s"] = pick(r, T.fw[:, w0:w0 + CAPP], T.fsc[:, w0:w0 + CAPP])
+    def pick(a, b):
+        L = T.lj[:, a // 16:b // 16]
+        tk["v"] = vop(t_lj + [t_k], "copy", T.fw[:, p0 + a:p0 + b].bitcast(dt.uint32), T.kcs[:].bitcast(dt.uint32).indirect(L))
+        tk["s"] = sop(t_lj + [t_k], T.fsc[:, p0 + a:p0 + b], T.kss[:].indirect(L), AF.Copy)
+    pick(0 if r else SL, NP)
+    need("g", [tk["v"]])
+    send(far + near, "colc", lambda d: T.fw[:, p0 + SL * d:p0 + SL * d + CAPP].bitcast(dt.uint8), lambda d: T.fw[:, w0:w0 + CAPP].bitcast(dt.uint8), eng.get)
+    need("g", [tk["s"]])
+    send(far + near, "cols", lambda d: T.fsc[:, p0 + SL * d:p0 + SL * d + CAPP], lambda d: T.fsc[:, w0:w0 + CAPP], eng.get)
 
     def pack():
+        if r:
+            zeros()
         tk["w"] = vop([t_w], "q", T.wq[:], T.wsc[:], T.wt[:])
     if r:
-        own()
-        zeros()
         pack()
 
     total["slk"] = KE * (N - 1)
     total["colc"] = total["cols"] = sum(len(eng[d]) for d in others)
     t_in = [("slk", total["slk"]), t_own, t_c]
     H = SL // 2
-    t2 = sop(t_in, T.x3[:, H:SL], T.ap[:].indirect(T.exp3[:, H // 16:SL // 16]), AF.Copy)
-    t_ax = lin(t_in, T.apx[:], T.ap[:].indirect(T.rot[:]), 1.0, -0.5)
-    t = vop(t_in, "copy", T.x3[:, 0:H], T.ap[:].indirect(T.exp3[:, 0:H // 16]))
+    t2 = sop(t_in, T.x3[:, H:SL], T.ap[:].indirect(T.exp3[:, H // 16:SL // 16]), AF.Copy, scale=-1.0)
+    t_ax = lin(t_in, T.apx[:], T.ap[:].indirect(T.rot[:]), -1.0, -0.5)
+    t = vop(t_in, "ts", T.x3[:, 0:H], T.ap[:].indirect(T.exp3[:, 0:H // 16]), -1.0, None, OP.mult)
     t_b3 = vop([t, t2], "tr", T.b3[:], T.x3[:])
-    t_em = sop([], T.em[:], T.ap[:].indirect(T.rot[:, 0:1]), AF.Relu, bias=float(2 * S - EMPTY))
+    t_em = sop([], T.em[:], T.ap[:].indirect(T.rot[:, 0:1]), AF.Relu, bias=float(2 * S - EMPTY), scale=-1.0)
 
     def scal(c):
         a = 8 * (1 + c // NB) + c % NB
         return T.apx[:, a:a + 1]
-    t_bf = sop([t_b3, t_ax], T.b3f[:], T.b3[:], AF.Copy)
+    W = 2 * NB
+    t_bf = lin([t_b3, t_ax], T.b3f[:], T.b3[:], 1.0, far1)
     for c in range(A3):
-        t_s = sop([], T.j3[:, CAPP * c:CAPP * (c + 1)], T.b3[:, 0:CAPP], AF.Sign, bias=scal(c), scale=-1.0, accum_out=T.rc[:, NB + c:NB + c + 1])
+        t_s = sop([], T.j3[:, CAPP * c:CAPP * (c + 1)], T.b3[:, 0:CAPP], AF.Sign, bias=scal(c), scale=-1.0, accum_out=T.rc[:, (NB + c) // W, (NB + c) % W:(NB + c) % W + 1])
     need("v", [t_b3, t_ax])
     for x in range(M3):
         t = vop([], "ts", T.cmp3[:, CAPP * x:CAPP * (x + 1)], T.b3[:, 0:CAPP], scal(A3 + x), 2.0, OP.is_lt, OP.mult)
     H = CAPP // 2
-    vop([t_em, t_wo], "tt", T.rc[:, 0:NB], T.em[:, 0:NB], T.oc6[:], OP.add)
+    vop([t_em, t_wo], "tt", T.rc[:, 0, 0:NB], T.em[:, 0:NB], T.oc6[:], OP.add)
     t = vop([t], "scan", T.sc3[:, 1:M3 * H + 1], T.cmp3[:, 0:M3 * CAPP:2], T.cmp3[:, 1:M3 * CAPP:2], R0, OP.add, OP.add)
-    t_v3 = vop([t_bf], "tt", T.v3[:], T.b3f[:].indirect(T.sel[:]), T.v3c[:], OP.max)
-    t = vop([t], "tt", T.rc[:, NB + A3:4 * NB], T.sc3[:, H:M3 * H + 1:H], T.sc3[:, 0:(M3 - 1) * H + 1:H], OP.subtract)
+    t_v3 = vop([t_bf], "tt", T.v3[:], T.b3f[:].indirect(T.sel[:]), T.v3c[:], OP.min)
+    t = vop([t], "tt", T.rc[:, 1, A3 - NB:W], T.sc3[:, H:M3 * H + 1:H], T.sc3[:, 0:(M3 - 1) * H + 1:H], OP.subtract)
     if r == 0:
-        own()
-    W = 2 * NB
-    vop([t, t_s], "tt", T.u3[0:64, 0:W], T.rc[0:64, 0:W], T.rc[64:128, W:2 * W], OP.add)
-    t = vop([], "tt", T.u3[0:64, W:2 * W], T.rc[0:64, W:2 * W], T.rc[64:128, 0:W], OP.add)
-    need("v", [t])
+        pick(0, CAPP)
+    need("v", [vop([t, t_s], "tt", T.u3[0:64, :], T.rc[0:64], T.rc[64:128, ::-1, :], OP.add)])
     for s in range(N):
         k = (s - 1) % N
         t = vop([], "tt", T.off3[quad(s), :], T.u3[0:32, NB * s:NB * (s + 1)], T.u3[32:64, NB * k:NB * (k + 1)], OP.add)
@@ -370,19 +356,19 @@ def rank_program(g, core, T, topo):
         need("t", [tk["w"]] + ([tk["v"], tk["s"]] if s == r else [("colc", total["colc"]), ("cols", total["cols"])]))
         t_t = done(g.tensor.matmul_mx(T.pz[:, 512 * s:512 * s + CAPP], T.wq[:], T.wsc[:], T.fw[:, a:a + CAPP], T.fsc[:, a:a + CAPP], True, True), "t")
         t_y = sop([t_t], T.yw[:, a:a + CAPP], T.pz[:, 512 * s:512 * s + CAPP], AF.Copy)
-    t = vop([t], "tr", T.to[:], T.wo[:, 0:2 * S:2])
     NO = S // 32
-    pairs(t, T.to, NO, (1, 0), T.y2, OP.max)
-    need("v", [vop([], "tt", T.y4[0:64, :], T.y2[0:64, :], T.y2[64:128, :], OP.max)])
+    t = vop([t], "tr", T.to[:], T.wo[:, 0:2 * S:2])
+    t = vop([t], "tt", T.y2[:], T.to[:, :, 0:2], T.to[:, :, 16:18], OP.max)
+    need("v", [vop([t], "tt", T.y4[0:64, :], T.y2[0:64], T.y2[64:128], OP.max)])
     for b in range(4):
-        t = vop([], "tt", T.zo[quad(b), 0:2 * NO], T.y4[0:32, :], T.y4[32:64, :], OP.max)
-    t_so = vop([t], "tr", T.so1[:], T.zo[:])
-    t = lin([t_so], T.rki[0:32, :], T.so1[0:32, 0:32], 1.0 / LW, -(KEYS / LW + 0.35))
+        t = vop([], "tt", T.zo[quad(b), 0:NO], T.y4[0:32, 1:2 * NO:2], T.y4[32:64, 1:2 * NO:2], OP.max)
+    t2 = vop([], "tt", T.zk[0:32, 0:NO], T.y4[0:32, 0:2 * NO:2], T.y4[32:64, 0:2 * NO:2], OP.max)
+
+    def keys():
+        dma("y", [vop([t2], "tr", T.sok[0:32, :], T.zk[0:32, :])], T.ok[0:1, :], T.sok[0:NO, :], "st1")
+    t_so, t_lf = lists(t, T.zo, T.so2, T.lf, keys)
+    t = lin([t_so], T.rki[0:32, :], T.so2[0:32, 0:4:2, :], 1.0 / LW, -0.35)
     t_rk = lin([t], T.rkf[0:32, :], T.rki[0:32, :], 1.0, -1.0)
-    t_lf = lists(t_so, T.so1, T.so2, T.lf, 1.0, -float(KEYS))
-    n1 = 32 - NO
-    dma("y", [t_so], T.ok[0:1, 0:32 * n1], T.so1[NO:32, 0:32], "st1")
-    dma("y", [], T.ok[0:1, 32 * n1:S], T.so1[0:NO - n1, 32:64], "st1")
     dma("y", [t_rk], T.ok[1:2, :], T.rkf[0:NO, :], "st1")
 
     def at(lo, hi):

from concourse.bass import DstId, RemoteDMATransfer
from concourse.mybir import dt, AluOpType as OP, ActivationFunctionType as AF

N, C, S, CAPP = 4, 512, 640, 176
KEYS = 65536
SL = 192
NB = SL // 32
NS = N * SL
LW = NS
EMPTY = 2 * KEYS
GAP = 576
GV = 128
SIGNS = (11, 10, 10, 10)
TAIL = [("c", 0, 96), ("y", 0, 96), ("c", 96, 352), ("y", 96, 352), ("c", 352, 640), ("y", 352, 640), ("s",)]
SV = 320


def _s(n, d="float32"):
    return ("sbuf", [128, n], d)


X4, U8, U16, BF, I32, F16 = "float8_e4m3fn_x4", "uint8", "uint16", "bfloat16", "int32", "float16"
SCRATCH = {
    "lki": _s(32, I32), "spi": _s(1, I32), "kl": _s(8, I32), "klu": _s(8, U16), "wt": _s(512, BF), "wq": _s(128, X4), "wsc": _s(128, U8), "kcs": _s(C, X4), "kss": _s(C, U8),
    "pidx": _s(1, I32), "pm": _s(6, I32), "pf": _s(6), "cs": _s(11), "spx": _s(32), "spb": _s(32),
    "i_dup": _s(4), "dup": _s(4, U16), "osel": _s(2, U16), "asel": _s(2, U16), "i_xe": _s(8), "xe": _s(8, U16), "i_yc": _s(64),
    "i_sel": _s(NB), "sel": _s(NB, U16), "i_exp": _s(2 * NB), "exp3": _s(2 * NB, U16),
    "i_16": _s(16), "rot1": _s(2), "rot2": _s(2), "rot": _s(2, U16), "dmp": _s(16),
    "i_v3": _s(96), "v3c": _s(96), "i_oc": _s(NB), "oc6": _s(NB), "ones": _s(C // 2, BF), "zt": _s(C, BF),
    "spf": _s(1), "xd": _s(64), "yd": _s(128), "ol": _s(16, U16), "at": _s(16), "sg": _s(48), "r4": _s(64), "rr": _s(32), "xa": _s(128), "vk": _s(128),
    "kb": _s(24, U16), "tab": _s(KEYS, BF), "hit": _s(C // 2, BF), "hitt": _s(C // 2, BF), "h4": _s(32), "fl": _s(16),
    "zq": _s(64), "zqt": _s(64), "st": _s(64), "bt": _s(32), "qq": _s(16), "e1": _s(16), "e2": _s(16), "off": _s(8, U16),
    "wk": _s(NS + 264), "tk": ("sbuf", [128, NS // 32, 32], "float32"), "z2": ("sbuf", [128, NS // 32, 2], "float32"), "zz": _s(32), "zc": _s(32, U16),
    "sw2": ("sbuf", [128, 4, 16], U16), "lj": _s(64, U16),
    "ap": _s(32), "apx": _s(32), "x3": _s(SL, U16), "b3": _s(SL, U16), "b3f": _s(SL), "v3": _s(96), "cmp3": _s((3 * NB - min(SIGNS)) * CAPP, F16),
    "sc3": _s((3 * NB - min(SIGNS)) * CAPP // 2 + 1, F16), "j3": _s(max(SIGNS) * CAPP, BF), "em": _s(16), "rc": ("sbuf", [128, 2, 2 * NB], "float32"), "u3": _s(4 * NB), "off3": _s(NB, U16),
    "wo": _s(2 * (S + NB * (GAP + 64))), "to": ("sbuf", [128, S // 32, 32], "float32"), "y2": ("sbuf", [128, S // 32, 2], "float32"), "y4": _s(40), "zo": _s(32, U16), "zk": _s(32), "sok": _s(32),
    "so2": ("sbuf", [128, 4, 16], U16), "lf": _s(64, U16),
    "rki": _s(32, U16), "rkf": _s(32),
    "fw": _s(LW * N + CAPP, X4), "fsc": _s(LW * N + CAPP, U8), "oq": _s(S, X4), "os_": _s(S, U8),
    "yw": _s(LW * N + CAPP), "ys": _s(S), "pz": ("psum", [128, 512 * N], "float32"),
}
SEMAPHORES = ["v", "s", "t", "gi", "dkl", "dlk", "dsp", "dw", "dk", "kin1", "kin2", "kin3", "slk", "colc", "cols", "ksent", "lsent", "st1"]


def rank_program(g, core, T, topo):
    r = T.rank_of(core)
    if r is None:
        return
    Q = {"v": g.vector, "s": g.scalar, "t": g.tensor, "g": g, "y": g.sync}
    seen, total = {}, {}

    def need(q, toks):
        for tok in toks:
            if tok is not None and seen.get((q, tok[0]), 0) < tok[1]:
                Q[q].wait_ge(T.sem[tok[0]], tok[1])
                seen[(q, tok[0])] = tok[1]

    def done(inst, sem, n=1):
        inst.then_inc(T.sem[sem], n)
        total[sem] = total.get(sem, 0) + n
        return (sem, total[sem])

    vec, act = g.vector, g.scalar

    def vop(deps, name, *a):
        need("v", deps)
        f = {"copy": vec.tensor_copy, "tt": vec.tensor_tensor, "ts": vec.tensor_scalar, "tr": vec.transpose, "scan": vec.tensor_tensor_scan,
             "set": vec.memset, "q": vec.quantize_mx}[name]
        return done(f(*a), "v")

    def sop(deps, *a, **k):
        need("s", deps)
        return done(act.activation(*a, **k), "s")

    def lin(deps, out, in_, scale=1.0, bias=0.0):
        return sop(deps, out, in_, AF.Identity, bias=bias, scale=scale)

    def dma(q, deps, out, in_, sem):
        need(q, deps)
        return done(Q[q].dma_start(out, in_), sem, 16)

    def iota(out, pat, base, cm=0, i32=False):
        if i32:
            return done(g.iota(out, pat, base, cm), "gi")
        return done(g.iota(out, pat, base, cm, allow_small_or_imprecise_dtypes=True), "gi")

    def fill(out, value=0):
        return iota(out, [[0, out.shape[1]]], value)

    def quad(b):
        return slice(32 * b, 32 * b + 32)

    others = [d for d in range(N) if d != r]
    far = [d for d in others if topo.chip(T.cores[d]) != topo.chip(core)]
    near = [d for d in others if d not in far]
    fe = topo.engines(core, T.cores[far[0]])
    KE = len(fe) // len(far)
    eng = {d: fe[i * KE:(i + 1) * KE] for i, d in enumerate(far)}
    for d in near:
        eng[d] = [e for e in topo.engines(core, T.cores[d]) if e not in fe]

    def short(d):
        return eng[d][:KE]

    def send(dests, sem, src, dst, engines, local="lsent"):
        tr = []
        for d in dests:
            rid, pid, _ = topo.addr(T.cores[d])
            tr.append(RemoteDMATransfer(dst_ids=[DstId(rid=rid, pnc=pid)], dma_engine_mask=sum(1 << e for e in engines(d)), remote_sem=T.sem[sem],
                                        src=src(d), dst=dst(d)))
            total[local] = total.get(local, 0) + len(engines(d))
        g.remote_dma_fused(tr, local_sem=T.sem[local])
        return (local, total[local])

    low = [d for d in others if d < r]
    nl = N - 1 - r
    A3 = SIGNS[r]
    M3 = 3 * NB - A3
    R0 = -float(M3 * CAPP)

    for a in range(2 if low else 0):
        t_kl = dma("ys"[a], [], T.kl[64 * a:64 * a + 64, :], T.ky[:], "dkl")
    for a in range(4):
        t_lk = dma("ys"[a % 2], [], T.lki[16 * a:16 * a + 16, :], T.ky[:], "dlk")
    t_sp = dma("s", [], T.spi[0:16, :], T.sp[:], "dsp")

    t_pi = iota(T.pidx[:], [[0, 1]], 0, 1, True)
    t_id = iota(T.i_dup[:], [[16, 2], [0, 2]], 0)
    t_yc = iota(T.i_yc[:], [[-256, 2], [-1, 32]], 0)
    t_xe = iota(T.i_xe[:], [[2, 4], [32, 2]], 0)
    t_r4 = fill(T.r4[:, 3:64:4])
    fill(T.zq[:, 16:64])
    t_zs = fill(T.st[:, 0:1])

    p15, p1, ph, h8, second, q8 = [T.pf[:, i:i + 1] for i in range(6)]
    m64, aq, u64, p15n, sb, sb2, p62, p16, p31, sr, far1 = [T.cs[:, i:i + 1] for i in range(11)]

    def bits(i, shift, mask):
        return vop([t_pi], "ts", T.pm[:, i:i + 1], T.pidx[:], shift, mask, OP.arith_shift_right, OP.bitwise_and)
    vop([], "set", T.lki[64:128, :], 0)
    vop([], "set", T.spx[0:64, :], 0.0)
    for i, (shift, mask) in enumerate(((0, 15), (0, 1), (1, 7), (3, 8))):
        t = bits(i, shift, mask)
    bits(4, 4, 1)
    t_pf = vop([t], "copy", T.pf[:, 0:4], T.pm[:, 0:4])
    t_b = bits(5, 2, 24)
    t_dup = vop([t_pf, t_id], "ts", T.dup[:], T.i_dup[:], p15, None, OP.add)
    if nl:
        vop([], "set", T.ones[:], 1.0)
    vop([], "set", T.zt[:, 0:128], 0.0)

    t_ks = None
    if low:
        need("g", [vop([t_kl], "copy", T.klu[:], T.kl[:])])
        ids = [DstId(rid=topo.addr(T.cores[d])[0], pnc=topo.addr(T.cores[d])[1]) for d in low]
        g.remote_dma_fused([RemoteDMATransfer(dst_ids=ids, dma_engine_mask=sum(1 << e for e in fe), remote_sem=T.sem["kin%d" % r], srcs=[T.klu[:]],
                                              dsts=[T.kb[:, 8 * (r - d - 1):8 * (r - d)] for d in low])], local_sem=T.sem.ksent)
        total["ksent"] = len(fe)
        t_ks = ("ksent", len(fe))
    t_o = lin([t_pf], sr, p1, 32.0, ph)
    t_q8 = sop([t_b], T.pf[:, 4:6], T.pm[:, 4:6], AF.Copy)
    t_o = lin([t_o], T.osel[:, 0:1], sr, 1.0, h8)
    t_as = lin([t_q8], T.asel[:, 0:1], second, 32.0, p15)
    t_w = dma("y", [t_ks, t_lk], T.wt[:], T.w[:], "dw")
    dma("y", [], T.kcs[:].bitcast(dt.uint8), T.kc[:], "dk")
    t_k = dma("y", [], T.kss[:], T.ks[:], "dk")

    t_i16 = iota(T.i_16[:], [[16, 16]], NS + 1)
    fill(T.zz[:, 24:32])
    if r == 0:
        t_zt = fill(T.zt[:, 128:C])
    t_wk = iota(T.wk[:, 1:NS + 1], [[0, N], [-2 * GAP, NB], [0, 32]], -EMPTY)
    iota(T.i_exp[:], [[1, NB], [0, 2]], 0)
    iota(T.i_sel[:], [[32, NB]], 0)
    t_iv = iota(T.i_v3[:], [[32, NB], [1, 16]], LW)
    for a, b, n in ((0, A3 % NB, A3 // NB + 1), (A3 % NB, NB, A3 // NB)):
        if a < b:
            t_oc = iota(T.i_oc[:, a:b], [[64, b - a]], n * CAPP + 64 * a)
    fill(T.zk[:, 20:32])
    fill(T.yw[:, 0:8])
    if r:
        t_zt = fill(T.zt[:, 128:C])
    if r == 0:
        t_wo = fill(T.wo[:, 0:2 * S:2], -1)

    need("v", [vop([t_lk, t_dup], "copy", T.xd[:], T.lki[:].indirect(T.dup[:]))])
    for b in range(2):
        t_yd = vop([], "tr", T.yd[64 * b:64 * b + 64, 0:64], T.xd[0:64, :])
    sop([], m64, p15, AF.Relu, bias=64.0, scale=-64.0)
    lin([], aq, h8, 1.0, second)
    t2 = lin([], p15n, p15, -16.0)
    t = sop([t_sp], T.spf[0:16, :], T.spi[0:16, :], AF.Copy)
    t_u = lin([t2], u64, m64, 1.0, aq)
    for b in range(2):
        t_sx = lin([t, t_yc], T.spx[32 * b:32 * b + 16, :], T.i_yc[0:16, 0:32], 0.0, T.spf[0:16, :])
    t_yn = lin([], T.yd[:, 64:128], T.i_yc[:], 1.0, p15n)
    t2 = lin([t_u, t_xe], T.xe[:], T.i_xe[:], 1.0, u64)
    if nl:
        t_ol = vop([t_yd, t_o], "copy", T.ol[:], T.yd[:, 0:64].indirect(T.osel[:, 0:1]))
    t_sb = vop([t_sx], "tr", T.spb[0:64, :], T.spx[0:64, :])
    if nl:
        t_tab = vop([t_ol], "copy", T.tab[:].indirect(T.ol[:]), T.ones[:])
    tk = {}
    t = lin([t_yd, t_as], T.at[:], T.yd[:, 0:64].indirect(T.asel[:, 0:1]), 1.0, 0.5)
    t_xa = sop([t2, t_yn], T.xa[:], T.yd[:].indirect(T.xe[:]), AF.Copy, scale=-1.0)
    need("s", [t, t_r4, t_sb])
    for j in range(N - 1):
        t = sop([], T.sg[0:64, 16 * j:16 * j + 16], T.at[0:64, :], AF.Sign, bias=T.spb[0:64, j:j + 1], scale=-1.0)
    need("s", [t])
    for j in range(N - 1):
        t_r = lin([], T.r4[0:64, j:64:4], T.sg[0:64, 16 * j:16 * j + 16], -SL * (j + 1) / 2.0, SL * (j + 1) / 2.0)
    t_vk = vop([t_xa], "tr", T.vk[:], T.xa[:])

    def zeros():
        vop([t_zt], "q", T.fw[:, 0:128], T.fsc[:, 0:128], T.zt[:])
    if r == 0:
        zeros()
    rr = T.rr[0:64, 1:32:2]

    def ranges():
        vop([t_r], "scan", T.rr[0:64, :], T.r4[0:64, 0:64:2], T.r4[0:64, 1:64:2], 0.0, OP.max, OP.max)

    fl = T.fl[0:64, :]
    if nl == 0:
        ranges()
        t_f = vop([], "set", fl, 1.0)
    else:
        t = t_tab
        for a in range(nl):
            kin = "kin%d" % (r + 1 + a)
            total[kin] = len(fe)
            t = vop([t, (kin, len(fe))], "copy", T.tab[:].indirect(T.kb[:, 8 * a:8 * a + 8]), T.zt[:, 0:128])
        t3 = sop([t], T.hit[:, GV:C // 2], T.tab[:].indirect(T.ol[:, GV // 16:16]), AF.Copy)
        t = vop([t], "copy", T.hit[:, 0:GV], T.tab[:].indirect(T.ol[:, 0:GV // 16]))
        ranges()
        need("v", [vop([t, t3], "tr", T.hitt[:], T.hit[:])])
        for h in range(2):
            t = vop([], "tt", T.h4[0:32, 16 * h:16 * h + 16], T.hitt[quad(2 * h), 0:C // 2:16], T.hitt[quad(2 * h + 1), 0:C // 2:16], OP.min)
        need("v", [t])
        for b in range(2):
            t_f = vop([], "tt", T.fl[quad(b), :], T.h4[0:32, 0:32:2], T.h4[0:32, 1:32:2], OP.min)

    lin([t_i16], T.dmp[:], T.i_16[:], 1.0, p15)
    t_e = sop([t_f], T.e1[0:64, :], fl, AF.Copy, scale=float(2 * NS))
    vop([t_f, t_zs], "scan", T.zq[0:64, 0:16], rr, fl, 0.0, OP.max, OP.add)
    t = vop([], "scan", T.zq[0:64, 32:48], T.zq[0:64, 16:32], fl, 0.0, OP.add, OP.add)
    t = vop([t], "tr", T.zqt[0:64, :], T.zq[0:64, :])
    t = vop([t], "scan", T.st[0:64, 1:33], T.zqt[0:64, 32:64], T.zqt[0:64, 0:32], 0.0, OP.add, OP.max)
    t2 = vop([t_e], "tt", T.e2[0:64, :], T.dmp[0:64, :], T.e1[0:64, :], OP.subtract)
    t = vop([t], "tr", T.bt[0:64, :], T.st[0:64, 0:32])
    t = vop([t], "scan", T.qq[0:64, :], rr, fl, T.bt[0:64, 15:16], OP.max, OP.add)
    need("v", [t, t2])
    for b in range(2):
        t = vop([], "tt", T.off[64 * b:64 * b + 64, :], T.qq[0:64, 8 * b:8 * b + 8], T.e2[0:64, 8 * b:8 * b + 8], OP.max)
    t3 = lin([t_as], sr, p15, 1.0, q8)
    t_sb = lin([], p16, second, 16.0)
    t2 = lin([], p31, second, 16.0, p15)
    t3 = lin([t3], T.rot1[:], T.i_dup[:, 0:4:2], 1.0, sr)
    t_sb = lin([t_sb], sb, m64, 8192.0, p16)
    lin([], far1, m64, -8192.0, 64 * 8192.0)
    lin([], T.zc[:, 24:32], T.i_16[:, 0:8], 0.0)
    lin([], T.zo[:, 20:32], T.i_16[:, 0:12], 0.0)
    t3 = sop([t3], T.rot2[:], T.rot1[:], AF.Sign, bias=-31.5)
    t2 = lin([t2], p62, p31, 2.0)
    t3 = lin([t3], T.rot2[:], T.rot2[:], -16.0, -16.0)
    lin([], T.sc3[:, 0:1], p15, 0.0, R0)
    need("s", [t3])
    for c in range(2):
        lin([], T.rot[:, c:c + 1], T.rot2[:, c:c + 1], 1.0, T.rot1[:, c:c + 1])
    t_sb = lin([t_sb], sb2, q8, LW / 8.0, sb)
    lin([t2, t_oc], T.oc6[:], T.i_oc[:], 1.0, p62)
    lin([t_iv], T.exp3[:], T.i_exp[:], 1.0, q8)
    lin([], T.sel[:], T.i_sel[:], 1.0, p31)
    t_c = lin([t_sb], T.v3c[:], T.i_v3[:], 1.0, sb2)

    def lists(tok, z, twice, out, between=None):
        need("v", [tok])
        t1 = [vop([], "tr", twice[:, a:4:2, :], z[:]) for a in range(2)][1]
        if between:
            between()
        need("v", [t1])
        return t1, [[vop([], "tr", out[:, a:64:2], twice[:, 2 * a:2 * a + 2, :]) for a in range(2)][1]]

    NZ = N * NB
    t = vop([t, t_vk, t_wk], "copy", T.wk[:].indirect(T.off[:]), T.vk[:])
    t = vop([t], "tr", T.tk[:], T.wk[:, 1:NS + 1])
    t, t2 = [vop([t], "tt", T.z2[:, :, row], T.tk[:, :, row], T.tk[:, :, 16 + row], OP.max) for row in (1, 0)]
    for b in range(2):
        t_zz = vop([t], "tt", T.zz[64 * b:64 * b + 64, 0:NZ], T.z2[0:64, :, 1], T.z2[64:128, :, 1], OP.max)
    need("g", [t_zz])
    send(far + near, "slk", lambda d: T.zz[:, NB * d:NB * d + 8], lambda d: T.ap[:, 8 * r:8 * r + 8], short)
    if r:
        t_wo = fill(T.wo[:, 0:2 * S:2], -1)
    t_own = sop([t_zz, t_wk], T.ap[:, 8 * r:8 * r + 8], T.zz[:, NB * r:NB * r + 8], AF.Copy)
    for b in range(2):
        t = vop([t2, t_c], "tt", T.zc[64 * b:64 * b + 64, 0:NZ], T.z2[0:64, :, 0], T.z2[64:128, :, 0], OP.max)
    t_lj = lists(t, T.zc, T.sw2, T.lj)[1]

    w0, NP = LW * (r + 1), NS - SL + CAPP
    p0 = w0 - SL * r

    def pick(a, b):
        L = T.lj[:, a // 16:b // 16]
        tk["v"] = vop(t_lj + [t_k], "copy", T.fw[:, p0 + a:p0 + b].bitcast(dt.uint32), T.kcs[:].bitcast(dt.uint32).indirect(L))
        tk["s"] = sop(t_lj + [t_k], T.fsc[:, p0 + a:p0 + b], T.kss[:].indirect(L), AF.Copy)
    pick(0 if r else SL, NP)
    need("g", [tk["v"]])
    send(far + near, "colc", lambda d: T.fw[:, p0 + SL * d:p0 + SL * d + CAPP].bitcast(dt.uint8), lambda d: T.fw[:, w0:w0 + CAPP].bitcast(dt.uint8), eng.get)
    need("g", [tk["s"]])
    send(far + near, "cols", lambda d: T.fsc[:, p0 + SL * d:p0 + SL * d + CAPP], lambda d: T.fsc[:, w0:w0 + CAPP], eng.get)

    def pack():
        if r:
            zeros()
        tk["w"] = vop([t_w], "q", T.wq[:], T.wsc[:], T.wt[:])
    if r:
        pack()

    total["slk"] = KE * (N - 1)
    total["colc"] = total["cols"] = sum(len(eng[d]) for d in others)
    t_in = [("slk", total["slk"]), t_own, t_c]
    H = SL // 2
    t2 = sop(t_in, T.x3[:, H:SL], T.ap[:].indirect(T.exp3[:, H // 16:SL // 16]), AF.Copy, scale=-1.0)
    t_ax = lin(t_in, T.apx[:], T.ap[:].indirect(T.rot[:]), -1.0, -0.5)
    t = vop(t_in, "ts", T.x3[:, 0:H], T.ap[:].indirect(T.exp3[:, 0:H // 16]), -1.0, None, OP.mult)
    t_b3 = vop([t, t2], "tr", T.b3[:], T.x3[:])
    t_em = sop([], T.em[:], T.ap[:].indirect(T.rot[:, 0:1]), AF.Relu, bias=float(2 * S - EMPTY), scale=-1.0)

    def scal(c):
        a = 8 * (1 + c // NB) + c % NB
        return T.apx[:, a:a + 1]
    W = 2 * NB
    t_bf = lin([t_b3, t_ax], T.b3f[:], T.b3[:], 1.0, far1)
    for c in range(A3):
        t_s = sop([], T.j3[:, CAPP * c:CAPP * (c + 1)], T.b3[:, 0:CAPP], AF.Sign, bias=scal(c), scale=-1.0, accum_out=T.rc[:, (NB + c) // W, (NB + c) % W:(NB + c) % W + 1])
    need("v", [t_b3, t_ax])
    for x in range(M3):
        t = vop([], "ts", T.cmp3[:, CAPP * x:CAPP * (x + 1)], T.b3[:, 0:CAPP], scal(A3 + x), 2.0, OP.is_lt, OP.mult)
    H = CAPP // 2
    vop([t_em, t_wo], "tt", T.rc[:, 0, 0:NB], T.em[:, 0:NB], T.oc6[:], OP.add)
    t = vop([t], "scan", T.sc3[:, 1:M3 * H + 1], T.cmp3[:, 0:M3 * CAPP:2], T.cmp3[:, 1:M3 * CAPP:2], R0, OP.add, OP.add)
    t_v3 = vop([t_bf], "tt", T.v3[:], T.b3f[:].indirect(T.sel[:]), T.v3c[:], OP.min)
    t = vop([t], "tt", T.rc[:, 1, A3 - NB:W], T.sc3[:, H:M3 * H + 1:H], T.sc3[:, 0:(M3 - 1) * H + 1:H], OP.subtract)
    if r == 0:
        pick(0, CAPP)
    need("v", [vop([t, t_s], "tt", T.u3[0:64, :], T.rc[0:64], T.rc[64:128, ::-1, :], OP.add)])
    for s in range(N):
        k = (s - 1) % N
        t = vop([], "tt", T.off3[quad(s), :], T.u3[0:32, NB * s:NB * (s + 1)], T.u3[32:64, NB * k:NB * (k + 1)], OP.add)
    t = vop([t, t_v3], "copy", T.wo[:].indirect(T.off3[:]), T.v3[:])
    if r == 0:
        pack()
    for s in [r] + others:
        a = LW * (s + 1)
        need("t", [tk["w"]] + ([tk["v"], tk["s"]] if s == r else [("colc", total["colc"]), ("cols", total["cols"])]))
        t_t = done(g.tensor.matmul_mx(T.pz[:, 512 * s:512 * s + CAPP], T.wq[:], T.wsc[:], T.fw[:, a:a + CAPP], T.fsc[:, a:a + CAPP], True, True), "t")
        t_y = sop([t_t], T.yw[:, a:a + CAPP], T.pz[:, 512 * s:512 * s + CAPP], AF.Copy)
    NO = S // 32
    t = vop([t], "tr", T.to[:], T.wo[:, 0:2 * S:2])
    t = vop([t], "tt", T.y2[:], T.to[:, :, 0:2], T.to[:, :, 16:18], OP.max)
    need("v", [vop([t], "tt", T.y4[0:64, :], T.y2[0:64], T.y2[64:128], OP.max)])
    for b in range(4):
        t = vop([], "tt", T.zo[quad(b), 0:NO], T.y4[0:32, 1:2 * NO:2], T.y4[32:64, 1:2 * NO:2], OP.max)
    t2 = vop([], "tt", T.zk[0:32, 0:NO], T.y4[0:32, 0:2 * NO:2], T.y4[32:64, 0:2 * NO:2], OP.max)

    def keys():
        dma("y", [vop([t2], "tr", T.sok[0:32, :], T.zk[0:32, :])], T.ok[0:1, :], T.sok[0:NO, :], "st1")
    t_so, t_lf = lists(t, T.zo, T.so2, T.lf, keys)
    t = lin([t_so], T.rki[0:32, :], T.so2[0:32, 0:4:2, :], 1.0 / LW, -0.35)
    t_rk = lin([t], T.rkf[0:32, :], T.rki[0:32, :], 1.0, -1.0)
    dma("y", [t_rk], T.ok[1:2, :], T.rkf[0:NO, :], "st1")

    def at(lo, hi):
        return T.lf[:, lo // 16:hi // 16]

    def codes(lo, hi):
        t = vop(t_lf + [("colc", total["colc"]), tk["v"], tk["w"]], "copy", T.oq[:, lo:hi].bitcast(dt.uint32), T.fw[:].bitcast(dt.uint32).indirect(at(lo, hi)))
        dma("y", [t], T.oc[:, 4 * lo:4 * hi], T.oq[:, lo:hi].bitcast(dt.uint8), "st1")

    def products(lo, hi):
        t = sop(t_lf + [t_y], T.ys[:, lo:hi], T.yw[:].indirect(at(lo, hi)), AF.Copy)
        dma("y", [t], T.y[:, lo:hi], T.ys[:, lo:hi], "st1")

    def scales():
        t2 = sop([("cols", total["cols"]), tk["s"], tk["w"]], T.os_[:, SV:S], T.fsc[:].indirect(at(SV, S)), AF.Copy)
        t = vop([("cols", total["cols"]), tk["s"]], "copy", T.os_[:, 0:SV], T.fsc[:].indirect(at(0, SV)))
        for i in range(4):
            dma("ys"[i % 2], [t, t2], T.osc[4 * i:4 * i + 4, :], T.os_[32 * i:32 * i + 4, :], "st1")
    for step in TAIL:
        if step[0] == "s":
            scales()
        else:
            (codes if step[0] == "c" else products)(step[1], step[2])
    need("g", list(total.items()))
